import numpy as np, ml_dtypes
CORES = [10,34,74,98]
N = 4
BF = ml_dtypes.bfloat16
def gentries(a):
    return np.ascontiguousarray(a.reshape(8, 16, -1).transpose(0, 2, 1)).reshape(8, -1)
def gtable(e):
    e = np.asarray(e); return np.ascontiguousarray(e.reshape(8, -1, 16).transpose(0, 2, 1)).reshape(128, -1).astype(np.int32)
W, F, C, K, TV, R = 4096, 2048, 256, 4, 3, 16
def num(l, b, t):
    return ((l * b >> 5) + l + 37 * b + 77 * t) & (F - 1)
def parts(rng):
    x = rng.integers(0, 16, (N, 8, 16, W)); fa = rng.integers(0, W, (N, 8, 16, F))
    l = rng.integers(0, W, (N, 8, K, C)); u = np.stack([rng.integers(-1, k, (N, 8, C)) for k in range(K)], axis=2)
    return x, fa, l, u, rng.integers(0, W, (N, 8, C)), rng.integers(36, 76, (N, 8, K)), rng.integers(0, 16, (N, 8, 16))
def pack(x, fa, l, u, e, th, w):
    return {"xs": np.ascontiguousarray(x.reshape(N, 128, W)).astype(np.float32).astype(BF), "fa": np.ascontiguousarray(fa.reshape(N, 128, F)).astype(np.int32),
            "lc": np.stack([gtable(a.reshape(8, -1)) for a in l]), "up": np.stack([gtable(a.reshape(8, -1)) for a in u]), "ex": np.stack([gtable(a) for a in e]),
            "th": np.ascontiguousarray(th).astype(np.int32), "wt": np.ascontiguousarray(w.reshape(N, 128, 1)).astype(np.int32)}
def setup_inputs(rng):
    return pack(*parts(rng))
def setup_inputs_spread(rng):
    x, fa, l, u, e, th, w = parts(rng)
    x = np.minimum((np.exp2(4 * rng.random((N, 8, 1, W))) * rng.random((N, 8, 16, W))).astype(np.int64), 15)
    a = rng.choice(np.array([1, 2, 4]), (N, 8, 1, 1))
    fa = np.minimum((W * rng.random(fa.shape) ** a).astype(np.int64), W - 1); l = np.minimum((W * rng.random(l.shape) ** a).astype(np.int64), W - 1)
    e = np.minimum((W * rng.random(e.shape) ** a[..., 0]).astype(np.int64), W - 1)
    th = np.minimum(np.exp2(8 * rng.random(th.shape)).astype(np.int64) - 1, 255); w = np.minimum(np.exp2(4 * rng.random(w.shape)).astype(np.int64) - 1, 15)
    return pack(x, fa, l, u, e, th, w)
def setup_inputs_ends(rng):
    x, fa, l, u, e, th, w = parts(rng)
    kind = rng.integers(0, 4, (N, 8, 1, W)); x = np.where(kind == 0, 0, np.where(kind == 1, 15, 15 * rng.integers(0, 2, x.shape)))
    x[..., 0] = 0; x[..., W - 1] = 15
    kind = rng.integers(0, 4, (N, 8, 1, F)); end = (W - 1) * rng.integers(0, 2, fa.shape)
    fa = np.where(kind == 0, 0, np.where(kind == 1, W - 1, np.where((kind == 2) | (rng.random(fa.shape) < 0.5), end, fa)))
    l = np.where(rng.random(l.shape) < 0.85, (W - 1) * rng.integers(0, 2, l.shape), l)
    e = np.where(rng.random(e.shape) < 0.85, (W - 1) * rng.integers(0, 2, e.shape), e)
    u = np.where(rng.random(u.shape) < 0.6, -1, np.arange(K)[:, None] - 1)
    th = 255 * rng.integers(0, 2, th.shape); th[:, 0, 0] = 0; th[:, 7] = 255
    w = 15 * rng.integers(0, 2, w.shape); w[:, 0] = 0; w[:, 7] = 15
    e[:, :, C - 1] = W - 1; l[:, :, 0, C - 1] = W - 1; l[:, :, 1, C - 1] = 0; u[:, :, 1, C - 1] = -1; u[:, :, K - 1, 0] = K - 2
    n0, n1 = num(W - 1, W - 1, 0), num(0, W - 1, 0)
    for g in (3, 7):
        x[:, g, :, 1:4] = 0; fa[:, g, :, n0] = rng.integers(0, 4, (N, 16)); fa[:, g, 0, n0] = 3; fa[:, g, 1, n0] = 0; fa[:, g, :, n1] = W - 1
    return pack(x, fa, l, u, e, th, w)
def setup_inputs_corners(rng):
    x, fa, l, u, e, th, w = parts(rng); k = np.arange(K)[:, None]
    for s in range(N):
        for g in range(8):
            m = (g + s) % 8
            if m == 0: u[s, g] = k - 1; th[s, g] = 255; th[s, g, 0] = 0
            if m == 1: u[s, g] = k - 1; th[s, g] = 255
            if m == 2: u[s, g] = -1; th[s, g] = rng.choice(np.array([0, 255]), K); w[s, g] = 0
            if m == 3: u[s, g] = k - 1; th[s, g] = 255; th[s, g, K - 1] = 0; w[s, g] = 15
            if m == 4: u[s, g] = np.minimum(k - 1, 0)
            if m == 5: x[s, g] = rng.integers(0, 16, W); th[s, g] = rng.choice(np.array([0, 1, 16, 17, 32]), K)
            if m == 6: x[s, g] = x[s, g][:, rng.integers(0, 8, W)]
            if m == 7:
                fa[s, g] = fa[s, g, :1].copy(); fa[s, g, :, ::4] = rng.choice(np.array([0, W - 1, W // 2, W // 2 + 1]), (16, F // 4))
                e[s, g] = rng.choice(np.array([0, W - 1, W // 2, 1]), C); l[s, g, ::2] = e[s, g]; th[s, g] = rng.integers(60, 110, K)
    return pack(x, fa, l, u, e, th, w)
def setup_inputs_crowd(rng):
    x, fa, l, u, e, th, w = parts(rng)
    for s in (0, 2):
        for g in range(8):
            x[s, g, :, :8] = 0; o = np.argsort(np.sum(x[s, g], axis=0)); e[s, g] = rng.choice(o[W // 2:], C); one = s == 2 and g == 7
            if one: l[s, g, K - 1, C - 1] = e[s, g, C - 1]; u[s, g, K - 1, C - 1] = -1; th[s, g] = 1
            n = num(l[s, g], e[s, g], 0)
            fa[s, g][:, n.reshape(-1)] = rng.integers(0, 8, (16, K * C))
            if one: fa[s, g, int(rng.integers(0, 16)), n[K - 1, C - 1]] = e[s, g, C - 1]
    for s in range(1, N, 2):
        for g in (0, 4):
            e[s, g] = int(e[s, g, 0]); l[s, g] = l[s, g, :, :1].copy(); u[s, g] = u[s, g, :, :1].copy()
        l[s, 4, :, C - 1] = rng.integers(0, W, K)
    if N > 5: th[5] = 255
    return pack(x, fa, l, u, e, th, w)
def setup_inputs_brink(rng):
    x, fa, l, u, e, th, w = parts(rng); al = np.arange(W); odd = np.arange(1, C, 2)
    pq = np.array([[3, 21], [21, 3], [5, 19], [19, 5], [7, 9], [9, 7]])
    for s in range(N):
        for g in range(8):
            m = (g + s) % 8
            if m < 3: u[s, g] = np.arange(K)[:, None] - 1; th[s, g] = 255
            if m == 0:
                used = np.zeros(F, bool)
                for i in range(C):
                    n = num(al, int(e[s, g, i]), 0); room = np.flatnonzero(~used[n])
                    if len(room) == 0: e[s, g, i] = 0; n = num(al, 0, 0); room = np.flatnonzero(~used[n])
                    v = int(room[int(rng.integers(0, len(room)))]); l[s, g, 0, i] = v; used[n[v]] = True
            if m == 1:
                lo = 512 * int(rng.integers(0, W // 512)); d = int(rng.integers(0, 512)); v = lo + d
                fa[s, g] = lo + rng.integers(0, 512, (16, F)); x[s, g, :, v] = 15
                e[s, g, C - 1] = v; l[s, g, 0, C - 1] = v; n = num(v, v, 0)
                fa[s, g, :15, n] = lo + ((d + rng.integers(1, 512, 15)) & 511); fa[s, g, 15, n] = v
            if m == 2:
                j = pq[rng.integers(0, 6, len(odd))]; l[s, g, 0, odd] = W - j[:, 0]; e[s, g, odd] = W - j[:, 1]
            if m == 3 or m == 4:
                o = rng.permutation(W)[:192]; x[s, g][:, o[:128]] = 0; x[s, g][rng.integers(0, 16, 64), o[64:128]] = 1; x[s, g][:, o[128:]] = 15
                e[s, g, odd] = rng.choice(o[128:], len(odd)); u[s, g][:, odd] = -1
                n = num(l[s, g][:, odd], e[s, g, odd], 0).reshape(-1); c = rng.choice(o[:64], (16, F))
                if m == 4:
                    hit = rng.random((16, F)) < 0.25; hit[0] = False; hit[15] = True
                    c = np.where(hit, rng.choice(o[64:128], (16, F)), c)
                fa[s, g][:, n] = c[:, n]
                th[s, g] = np.resize(np.array([240, 241, 239]) if m == 3 else np.array([240, 239, 241]), K)
    return pack(x, fa, l, u, e, th, w)
def check_inputs(d):
    bad = []
    for k, lo, hi in (("xs", 0, 15), ("fa", 0, W - 1), ("lc", 0, W - 1), ("up", -1, K - 2), ("ex", 0, W - 1), ("th", 0, 255), ("wt", 0, 15)):
        v = np.asarray(d[k]).astype(np.float32)
        if not (np.min(v) >= lo and np.max(v) <= hi): bad.append("range of " + k)
        if k == "xs" and np.any(v != np.floor(v)): bad.append("whole numbers in xs")
    u = np.stack([gentries(a) for a in np.asarray(d["up"])]).reshape(N, 8, K, C)
    if np.any(u > np.arange(K)[:, None] - 1): bad.append("inputs in up that are not rows before")
    return bad
def reference(xs, fa, lc, up, ex, th, wt):
    X = xs.astype(np.float32).astype(np.int32).reshape(N, 8, 16, W); FC = fa.astype(np.int64).reshape(N, 8, 16, F)
    L = np.stack([gentries(a) for a in lc]).astype(np.int64).reshape(N, 8, K, C); U = np.stack([gentries(a) for a in up]).astype(np.int64).reshape(N, 8, K, C)
    E = np.stack([gentries(a) for a in ex]).astype(np.int64); H = th.astype(np.int64); V = wt.astype(np.int64).reshape(N, 8, 16, 1)
    A = np.zeros(N, np.int64)
    for t in range(TV):
        deaths = np.zeros(N, np.int64)
        for s in range(N):
            r = (s - t) % N; l, u, x = L[r], U[r], X[s]
            beta = np.zeros((8, K + 1, C), np.int64); beta[:, 0] = E[s]
            live = np.ones((8, K + 1, C), bool); y = np.zeros((8, 16, C), np.int32)
            for k in range(K):
                j = u[:, k:k + 1] + 1
                b = np.take_along_axis(beta, j, 1)[:, 0]; ok = np.take_along_axis(live, j, 1)[:, 0]
                c = np.take_along_axis(FC[s], num(l[:, k], b, t)[:, None, :], 2)
                q = np.maximum(np.take_along_axis(x, l[:, k:k + 1], 2), np.take_along_axis(x, b[:, None, :], 2))
                v = np.take_along_axis(x, np.ascontiguousarray(c.transpose(0, 2, 1)).reshape(8, 1, 16 * C), 2).reshape(8, 16, C, 16)
                dist = np.add.reduce(np.abs(v - q[..., None]), axis=1)
                m = np.argmin(dist, axis=2)
                ok = ok & (np.min(dist, axis=2) < H[s][:, k:k + 1] + A[s])
                beta[:, k + 1] = np.take_along_axis(c, m[:, None, :], 1)[:, 0]; live[:, k + 1] = ok
                y = np.maximum(y, np.where(ok[:, None, :], np.take_along_axis(x, beta[:, k + 1:k + 2], 2), 0))
            place = R * np.arange(C) + (np.add.reduce(V[s] * y, axis=1) & (R - 1))
            np.put_along_axis(x, np.repeat(place[:, None, :], 16, axis=1), y, 2)
            last = np.zeros((8, C), np.int64)
            for k in range(K):
                p = np.take_along_axis(beta, last[:, None, :], 1)[:, 0]; dead = ~live[:, k + 1]
                l[:, k] = np.where(dead, ((l[:, k] * p >> 5) + 37 * p + k) & (W - 1), l[:, k])
                u[:, k] = np.where(dead, last - 1, u[:, k])
                last = np.where(dead, last, k + 1)
            deaths[s] = np.count_nonzero(~live)
        A = deaths & 31
    return {"yl": np.stack([gtable(a.reshape(8, -1)) for a in L]).astype(np.float32), "yi": np.stack([gtable(a.reshape(8, -1)) for a in U]).astype(np.float32),
            "yx": X.reshape(N, 128, W).astype(np.float32).astype(BF)}

@@ -1,0 +1,589 @@
+import numpy as np
+from concourse.mybir import AluOpType, AxisListType, ActivationFunctionType
+
+ALU, ACT = AluOpType, ActivationFunctionType
+W, F, K, TV, NR = 4096, 2048, 4, 3, 4
+NCH, CW = 2, 8
+CL = 16 * CW
+PC, NP, NB = 64, 2, 5
+QFIRST = True
+KW = 17 * CW
+NENG = 8
+XL_ENG = "s"
+Y0_ENG = "v"
+SPLIT = (True, True)
+XFIRST = True
+ABS = [(0, 1, 0), (0, 2, 0), (0, 3, 0), (1, 3, 1)]
+CYC = 0.83 * np.array([1.25, 1.1, 1.4, 1.25, 1.25])
+CG = np.array([1.56, 1.2, 1.9, 1.56, 1.56])
+CS = np.array([3.8, 2.5, 5.0, 3.8, 3.8])
+PE = 0.5 * CYC * np.array([1.0, 1.0, 1.0, 1.0, 1.3])
+FIX = np.array([0.0, 0.0, 0.0, 30.0, 0.0])
+LAT = np.array([60.0, 60.0, 60.0, 100.0, 40.0])
+REM = np.array([3000.0, 2500.0, 3500.0, 4000.0, 3000.0])
+WGT = np.array([2.0, 1.0, 1.0, 1.0, 1.0])
+CFG = {"rounds": 300, "jit": 100.0, "seed": 1, "free": 9999, "win": 1e9}
+ORDER = {}
+
+SCRATCH = {
+    "X": ("sbuf", [128, W + 16], "bfloat16"),
+    "XO": ("sbuf", [128, W // 2], "bfloat16"),
+    "FA": ("sbuf", [128, F], "int32"),
+    "lci": ("sbuf", [128, 4, 16], "int32"), "upi": ("sbuf", [128, 4, 16], "int32"), "exi": ("sbuf", [128, 16], "int32"),
+    "thi": ("sbuf", [128, 4], "int32"), "wti": ("sbuf", [128, 4], "int32"),
+    "thb": ("sbuf", [128, 4], "bfloat16"), "thf": ("sbuf", [128, 4], "float32"), "tha": ("sbuf", [128, 12], "float32"),
+    "IO": ("sbuf", [128, 160], "float32"), "pci": ("sbuf", [128, 4], "int32"), "col": ("sbuf", [128, 12], "float32"),
+    "E8": ("sbuf", [128, 128], "bfloat16"), "E8i": ("sbuf", [128, 128], "float32"),
+    "ID": ("sbuf", [128, 128], "bfloat16"), "NI": ("sbuf", [128, 128], "bfloat16"), "ON": ("sbuf", [128, 128], "bfloat16"),
+    "NQ": ("sbuf", [128, 128], "bfloat16"), "I2": ("sbuf", [128, 128], "bfloat16"),
+    "ZV": ("sbuf", [128, 144], "bfloat16"), "ZM": ("sbuf", [128, 144], "bfloat16"), "ZW": ("sbuf", [128, 144], "bfloat16"),
+    "G0": ("sbuf", [128, 160], "float32"), "G1": ("sbuf", [128, 160], "float32"),
+    "RS": ("sbuf", [128, KW], "float32"), "IX": ("sbuf", [128, 6 * CW], "float32"), "KC": ("sbuf", [128, 4 * CW], "float32"),
+    "BASE": ("sbuf", [128, CW], "float32"), "E16": ("sbuf", [128, 16], "uint16"),
+    "OUT": ("sbuf", [128, 2, 4, 16], "float32"), "FIN": ("sbuf", [128, 2, 4, 16], "float32"),
+    "cnt": ("sbuf", [128, 4], "float32"), "cni": ("sbuf", [128, 4], "int32"),
+}
+for _c in range(NCH):
+    for _n, _s, _d in (
+        ("V", [16 * CL], "bfloat16"), ("M", [CL, 18], "bfloat16"), ("Ma", [CL, 18], "bfloat16"), ("XL", [4 * CL], "bfloat16"),
+        ("ya", [CL], "bfloat16"), ("yb", [CL], "bfloat16"),
+        ("c16", [CL], "uint16"), ("cf", [4, 2, 16], "float32"), ("ct", [4, 2, 17], "float32"), ("SK", [KW], "float32"),
+        ("BE", [6 * CW], "float32"), ("MK", [24 * CW], "float32"), ("D0", [24 * CW], "float32"),
+        ("D1", [6 * CW], "float32"), ("SN", [6 * CW], "float32"),
+        ("si", [6 * CW], "int32"), ("so", [3 * CW], "uint16"), ("y16", [4 * CW], "uint16"), ("w0", [4 * CW], "float32"),
+        ("L16", [4 * CW], "uint16"), ("Fb", [CW], "bfloat16"), ("u0", [CW], "float32"),
+        ("LB", [6 * CW], "float32"), ("DD", [4 * CW], "bfloat16"), ("PP", [6 * CW], "float32"), ("JJ", [6 * CW], "float32"),
+        ("K3", [4 * CW], "float32"), ("w1", [4 * CW], "float32"), ("w2", [4 * CW], "float32"), ("w3", [4 * CW], "int32"),
+        ("w4", [4 * CW], "int32"), ("w5", [4 * CW], "float32"), ("w6", [4 * CW], "float32"), ("w7", [4 * CW], "float32"),
+        ("s3", [CW], "float32"),
+        ("snd0", [2, 4, CW], "float32"), ("snd1", [2, 4, CW], "float32"),
+        ("lnd0", [2, 4, CW], "float32"), ("lnd1", [2, 4, CW], "float32"),
+    ):
+        SCRATCH["%s_%d" % (_n, _c)] = ("sbuf", [128] + _s, _d)
+    SCRATCH["KT_%d" % _c] = ("psum", [128, 512], "float32")
+for _p in range(NB):
+    SCRATCH["PB_%d" % _p] = ("psum", [128, 32, 8, 2], "float32")
+SCRATCH["MS"] = ("psum", [128, 512], "float32")
+SI = {"r": 0, "c": 1, "u": 2, "n": 3, "s1": 4, "s2": 5}
+SO = {"n16": 0, "b16": 1, "p16": 2}
+
+SEMAPHORES = ["sv", "ss", "sp", "sg", "sent"] + ["d%d" % _i for _i in range(24)]
+ESEM = {"v": "sv", "s": "ss", "p": "sp", "g": "sg"}
+
+
+def build_ops(g, core, T, topo):
+    rank = T.rank_of(core)
+    ops = []
+    V, S = g.vector, g.scalar
+
+    def op(eng, fn, r=(), w=(), x=(), cost=0.0, dma=None, grp=None, inc=16, big=False):
+        ops.append({"big": big, "e": eng, "fn": fn, "r": list(r), "w": list(w), "x": list(x), "c": cost + 0 * CG, "dma": dma is not None,
+                    "l": (0.0 if dma is None else dma) + 0 * CG, "grp": grp, "inc": inc})
+
+    def vc(n):
+        return (max(64, n) + FIX) * CYC
+
+    def ts(out, in0, s1, s2, o0, o1, r, w, n=8, x=()):
+        if o1 is None:
+            op("v", lambda: V.tensor_scalar(out, in0, s1, None, o0), r, w, x, vc(n))
+        else:
+            op("v", lambda: V.tensor_scalar(out, in0, s1, s2, o0, o1), r, w, x, vc(n))
+
+    def tt(out, a, b, o, r, w, n=16, x=()):
+        op("v", lambda: V.tensor_tensor(out, a, b, o), r, w, x, vc(n))
+
+    def cp(out, in_, r, w, n=8, x=()):
+        op("v", lambda: V.tensor_copy(out, in_), r, w, x, vc(n))
+
+    def ms(ap, val, w, n=8):
+        op("v", lambda: V.memset(ap, val), (), w, (), vc(n))
+
+    def scan(out, d0, d1, o0, o1, r, w, n, x=()):
+        op("v", lambda: V.tensor_tensor_scan(out, d0, d1, 0.0, o0, o1), r, w, x, vc(n))
+
+    def gc_(n, c=None):
+        return 55 + n * (CG if c is None else c) * CYC
+
+    def gather(eng, out, src, r, w, n, big=False):
+        if eng == "v":
+            op("v", lambda: V.tensor_copy(out, src), r, w, (), gc_(n))
+        else:
+            op("s", lambda: S.activation(out, src, ACT.Copy), r, w, (), gc_(n) + 10, big=big)
+
+    def mm(lst, r, w, x, grp, f32=False):
+        n = sum(max(64, a[3]) for a in lst) * (4 if f32 else 1)
+        op("p", lst, r, w, x, 10 + n * PE, grp=grp)
+
+    def dma(eng, out, in_, r, w, nbytes, after=0.0):
+        q = {"y": g.sync, "s": g.scalar}[eng]
+        op(eng, lambda: q.dma_start(out, in_), r, w, (), 60.0, dma=1800.0 + nbytes / 180.0 + after)
+
+    def iota(out, pat, base, w, cost):
+        op("g", lambda: g.iota(out, pat, base, 0, allow_small_or_imprecise_dtypes=True), (), w, (), cost)
+
+    def send(dst, out, in_, r, w):
+        rid, pid = topo.addr(dst)[0], topo.addr(dst)[1]
+        m = 0
+        for e in topo.engines(core, dst)[:NENG]:
+            m += 1 << e
+        op("g", lambda sem: g.remote_dma(out, in_, sem, T.sem.sent, pid, rid, m), r, w, (), 100.0, dma=REM + (2000.0 if not [1 for o in ops if o["dma"] and o["e"] == "g"] else 0.0), inc=NENG)
+
+    def B(n, c):
+        return T["%s_%d" % (n, c)]
+
+    def A(n, c):
+        if n in SI:
+            return B("si", c)[:, CW * SI[n]:CW * SI[n] + CW]
+        return B("so", c)[:, CW * SO[n]:CW * SO[n] + CW]
+
+    MS = T.MS
+    X, XW = T.X, T.X[:, 0:W + 16]
+    dma("y", T.lci[:], T.lc[:], (), ["lci"], 32768)
+    dma("s", T.exi[:], T.ex[:], (), ["exi"], 8192)
+    dma("y", T.upi[:], T.up[:], (), ["upi"], 32768)
+    dma("s", T.thi[0:8, :], T.th[:], (), ["thi"], 128)
+    if XFIRST:
+        dma("y", X[:, 0:W], T.xs[:], (), ["X0", "X1"], 1 << 20)
+        dma("s", T.wti[:, 0:1], T.wt[:], (), ["wti"], 512)
+        dma("s", T.FA[:], T.fa[:], (), ["FA"], 2 << 20)
+    else:
+        dma("y", T.FA[:], T.fa[:], (), ["FA"], 1 << 20)
+        dma("s", T.wti[:, 0:1], T.wt[:], (), ["wti"], 512)
+        dma("s", X[:, 0:W], T.xs[:], (), ["X0", "X1"], 2 << 20)
+    nload = len(ops)
+    op("g", lambda: g.iota(T.pci[:, 0:1], [[1, 1]], 0, 1), (), ["pc0"], (), 150)
+    iota(T.IO[:], [[1, 160]], -16, ["IO"], 450)
+    iota(T.E8i[0:8, :], [[1, 8], [0, 16]], 0, ["E8i"], 400)
+    iota(T.KC[:], [[32, 4], [0, CW]], 65536 - 4194304, ["KC"], 200)
+    iota(T.IX[:], [[0, CW], [1, 6]], -2, ["IX"], 250)
+    iota(T.BASE[:], [[256, CW]], 0, ["BASE"], 150)
+    col = T.col
+    cP, cG, cH1, cH0, cM, c16_, cW = (col[:, j:j + 1] for j in range(7))
+    cp(cP, T.pci[:, 0:1], ["pc0"], ["cP"])
+    ts(T.pci[:, 1:2], T.pci[:, 0:1], 4, None, ALU.arith_shift_right, None, ["pc0"], ["pc1"])
+    ts(T.pci[:, 2:3], T.pci[:, 0:1], 4, 1, ALU.arith_shift_right, ALU.bitwise_and, ["pc0"], ["pc2"])
+    ts(T.pci[:, 3:4], T.pci[:, 0:1], 15, None, ALU.bitwise_and, None, ["pc0"], ["pc3"])
+    cp(cG, T.pci[:, 1:2], ["pc1"], ["cG"])
+    cp(cH1, T.pci[:, 2:3], ["pc2"], ["cH1"])
+    ts(cH0, T.pci[:, 2:3], -1.0, 1.0, ALU.mult, ALU.add, ["pc2"], ["cH0"])
+    ts(c16_, T.pci[:, 3:4], 16.0, None, ALU.mult, None, ["pc3"], ["c16_"])
+    cp(cW, T.wti[:, 0:1], ["wti"], ["cW"])
+    ts(T.ID[:], T.IO[:, 16:144], cP, None, ALU.is_equal, None, ["IO", "cP"], ["ID"], 128)
+    ts(cM, T.pci[:, 3:4], 4096.0, 4096.0, ALU.mult, ALU.add, ["pc3"], ["cM"])
+    ts(T.NI[:], T.IO[:, 16:144], cP, 65536.0, ALU.is_equal, ALU.mult, ["IO", "cP"], ["NI"], 128)
+    ts(T.NQ[:], T.IO[:, 16:144], cP, -1.0, ALU.is_equal, ALU.mult, ["IO", "cP"], ["NQ"], 128)
+    ts(T.I2[:], T.IO[:, 16:144], cP, 2.0, ALU.is_equal, ALU.mult, ["IO", "cP"], ["I2"], 128)
+    ms(T.ON[:], 1.0, ["ON"])
+    for nm, sc in (("ZV", 65536.0), ("ZM", -65536.0), ("ZW", cW)):
+        ms(T[nm][:], 0.0, [nm], 72)
+        ts(T[nm][:, 15:128:16], T.IO[:, 16:24], cG, sc, ALU.is_equal, ALU.mult, ["IO", "cG", nm] + (["cW"] if nm == "ZW" else []), [nm])
+    ts(T.G0[:], T.IO[:], cP, cH0, ALU.is_equal, ALU.mult, ["IO", "cP", "cH0"], ["G0"], 160)
+    ts(T.G1[:], T.IO[:], cP, cH1, ALU.is_equal, ALU.mult, ["IO", "cP", "cH1"], ["G1"], 160)
+    ms(T.RS[:], 0.0, ["RS"], KW)
+    ms(T.RS[:, 1:KW:17], 67108864.0, ["RS"])
+    ms(X[:, W:W + 16], 0.0, ["XZ"])
+    ts(T.E8[0:8, :], T.E8i[0:8, :], col[0:8, 0:1], None, ALU.is_equal, None, ["E8i", "cP"], ["E8"], 128)
+    cp(T.thb[0:8, :], T.thi[0:8, :], ["thi"], ["thb"])
+    mm([(MS[:, 0:4], T.E8[0:8, :], T.thb[0:8, :], 4)], ["E8", "thb"], ["MS"], ["MS"], None)
+    ts(T.tha[:, 0:4], MS[:, 0:4], 241.0, None, ALU.min, None, ["MS"], ["tha0"], x=["MS"])
+    cp(T.thf[:], MS[:, 0:4], ["MS"], ["thf"], x=["MS"])
+    cp(T.E16[:], T.exi[:], ["exi"], ["E16"])
+    for c in range(NCH):
+        ms(B("BE", c)[:], 1.0, ["BE%d_%d" % (c, s) for s in range(6)])
+        cp(B("BE", c)[:, 1::6], T.exi[:, CW * c:CW * c + CW], ["exi"], ["BE%d_1" % c])
+        ms(B("MK", c)[:, 0::6], -2048.0, ["MK%d_0" % c])
+        ts(B("w0", c)[:, 0:CW], T.exi[:, CW * c:CW * c + CW], -2048.0, None, ALU.add, None, ["exi"], ["w0%d_0" % c])
+        ms(B("w5", c)[:, 0:CW], 0.0, ["w5%d_0" % c])
+        ms(B("D0", c)[:], 1.0, ["D0%d_0" % c, "D0%d_6" % c], 224)
+        ms(B("D0", c)[:, 0::6], 0.0, ["D0%d_0" % c])
+        ms(B("Ma", c)[:, :, 1], 0.0, ["Mz%d" % c])
+        ms(B("ct", c)[:, :, :, 0], 0.0, ["cz%d" % c])
+
+    XK = ["X0", "X1", "XZ"]
+    nbank = [0]
+
+    def state(t, c, k=None):
+        kk = slice(0, K) if k is None else k
+        if t == 0:
+            return T.lci[:, kk, CW * c:CW * c + CW], T.upi[:, kk, CW * c:CW * c + CW], ["lci"], ["upi"]
+        a = B("lnd%d" % (t - 1), c)
+        key = ["lnd%d_%d" % (t - 1, c)]
+        return a[:, 0, kk, :], a[:, 1, kk, :], key, key
+
+    def prep(t, c):
+        L, J, kl, kj = state(t, c)
+        MK, D0 = B("MK", c), B("D0", c)
+        ts(D0[:, 5::6], L, 1184.0, None, ALU.add, None, kl, ["D0%d_6" % c], 32)
+        ts(MK[:, 5::6], L, 2080.0, float(2464 * t - 4194304), ALU.mult, ALU.add, kl, ["MK%d_5" % c], 32)
+        for s in range(4):
+            ts(MK[:, s + 1::6], J, float(s - 1), None, ALU.is_equal, None, kj, ["MK%d_%d" % (c, s + 1)], 32)
+        cp(B("L16", c)[:], L, kl, ["L16%d" % c], 32)
+        ts(B("w7", c)[:], L, 2048.0, None, ALU.mult, None, kl, ["w7%d" % c], 32)
+        tt(B("K3", c)[:], B("w7", c)[:], T.KC[:], ALU.add, ["w7%d" % c, "KC"], ["K3%d" % c], 64)
+        gather("v", B("XL", c)[:, 0:CL], XW.indirect(B("L16", c)[:, 0:CW]), XK + ["L16%d" % c], ["XL%d_0" % c], CL)
+        gather(XL_ENG, B("XL", c)[:, CL:4 * CL], XW.indirect(B("L16", c)[:, CW:4 * CW]), XK + ["L16%d" % c], ["XL%d_1" % c], 3 * CL)
+
+    def chain(t, c, k):
+        BE, SN, n6 = B("BE", c), B("SN", c), 6 * CW
+        th = T.tha[:, 4 * t + k:4 * t + k + 1]
+        if k == 0:
+            E, ek = B("w0", c)[:, 0:CW], "w0%d_0" % c
+            tt(B("u0", c)[:], B("D0", c)[:, 5:n6:6], E, ALU.mult, ["D0%d_6" % c, ek], ["u0%d" % c])
+            tt(A("u", c), B("u0", c)[:], B("MK", c)[:, 5:n6:6], ALU.add, ["u0%d" % c, "MK%d_5" % c], ["u%d" % c])
+            ts(B("Fb", c)[:], E, 2048.0, th, ALU.is_lt, ALU.mult, [ek, "tha%d" % t], ["Fb%d" % c])
+        else:
+            tt(B("D1", c)[:], BE[:], B("MK", c)[:, n6 * k:n6 * k + n6], ALU.mult,
+               ["BE%d_%d" % (c, s) for s in range(6)] + ["MK%d_%d" % (c, s) for s in range(6)], ["D1%d" % c], 96)
+            scan(SN[:], B("D0", c)[:, n6 * k:n6 * k + n6], B("D1", c)[:], ALU.mult, ALU.add, ["D0%d_0" % c, "D0%d_6" % c, "D1%d" % c], ["SN%d" % c], 48)
+            ts(A("u", c), SN[:, 5::6], 16777216.0, -16777216.0, ALU.min, ALU.max, ["SN%d" % c], ["u%d" % c])
+            ts(A("b16", c), SN[:, 4::6], 2048.0, 4096.0, ALU.add, ALU.min, ["SN%d" % c], ["b16%d" % c])
+            ts(B("Fb", c)[:], SN[:, 4::6], 2048.0, th, ALU.is_lt, ALU.mult, ["SN%d" % c, "tha%d" % t], ["Fb%d" % c])
+        ts(A("n", c), A("u", c), 5, F - 1, ALU.arith_shift_right, ALU.bitwise_and, ["u%d" % c], ["n%d" % c])
+        cp(A("n16", c), A("n", c), ["n%d" % c], ["n16%d" % c])
+        gather("v", B("c16", c)[:], T.FA[:].indirect(A("n16", c)), ["FA", "n16%d" % c], ["c16%d" % c], CL)
+        for h in range(2):
+            ts(B("cf", c)[:, :, h, :], B("c16", c)[:, PC * h:PC * h + PC], cM, None, ALU.add, None, ["c16%d" % c, "cM"], ["cf%d_%d" % (c, h)], PC)
+        op("v", lambda: V.transpose(B("ct", c)[:, :, :, 1:17], B("cf", c)[:]), ["cf%d_0" % c, "cf%d_1" % c], ["ct%d" % c], (), vc(CL))
+
+    def row(t, c, k):
+        KT, kt, grp = B("KT", c), "KT%d" % c, "k%d_%d_%d" % (t, c, k)
+        Vt, Mt, Ma = B("V", c), B("M", c), B("Ma", c)
+        off, ok = (T.E16[:, CW * c:CW * c + CW], "E16") if k == 0 else (A("b16", c), "b16%d" % c)
+        op("v", lambda: V.tensor_tensor(Mt[:, :, 0], XW.indirect(off), B("XL", c)[:, CL * k:CL * k + CL], ALU.max),
+           XK + [ok, "XL%d_%d" % (c, min(k, 1))], ["q%d" % c], (), gc_(CL))
+        cp(Mt[:, :, 1], Mt[:, :, 0], ["q%d" % c], ["qq%d" % c], 64)
+        qk = ["q%d" % c, "qq%d" % c]
+        thr = KT[:, 0:KW:17]
+        keys = []
+        mm([(KT[:, 68 * h:68 * h + 68], T["G%d" % h][:, 16 - 16 * (gp - h):144 - 16 * (gp - h)], B("ct", c)[:, :, gp, :], 68) for h in range(2) for gp in range(2)],
+           ["G0", "G1", "ct%d" % c, "cz%d" % c], [kt + "c"], [kt], grp, f32=True)
+        for p in range(NP):
+            vk, mk = "V%d_%d" % (c, p), "M%d_%d" % (c, p)
+            lo, hi = PC * p, PC * p + PC
+            vks = [vk + "a", vk + "b"]
+            if SPLIT[p]:
+                for j in range(2):
+                    gather("s", Vt[:, 1024 * p + 512 * j:1024 * p + 512 * j + 512], XW.indirect(B("c16", c)[:, lo + 32 * j:lo + 32 * j + 32]),
+                           XK + ["c16%d" % c], [vks[j]], 8 * PC, True)
+            else:
+                gather("s", Vt[:, 1024 * p:1024 * p + 1024], XW.indirect(B("c16", c)[:, lo:hi]), XK + ["c16%d" % c], vks, 16 * PC, True)
+            ab = (c, k, p) in ABS
+            mks = [mk + "_%d%d" % (j, ab) for j in range(2)]
+            for j in range(2):
+                bn = "PB_%d" % (nbank[0] % NB)
+                nbank[0] += 1
+                bank, g2, a0, vo = T[bn], grp + "b%d%d" % (p, j), lo + 32 * j, 1024 * p + 512 * j
+                mq = ([(bank[:, :, a, :], (T.NQ if ab else T.I2)[:], Mt[:, a0:a0 + 32, 0:2], PC) for a in range(8)], ["NQ", "I2"] + qk)
+                mv = ([(bank[:], (T.ID if ab else T.NQ)[:], Vt[:, vo:vo + 512], 512)], ["ID", "NQ", vks[j]])
+                for lst, rd in ((mq, mv) if QFIRST else (mv, mq)):
+                    mm(lst, rd, [bn], [bn], g2)
+                if ab:
+                    op("s", lambda a0=a0, bank=bank: S.activation(Ma[:, a0:a0 + 32, 2:18], bank[:], ACT.Abs), [bn], [mks[j]], [bn], vc(512))
+                else:
+                    tt(Mt[:, a0:a0 + 32, 2:18], Vt[:, vo:vo + 512], bank[:], ALU.min, [vks[j], bn], [mks[j]], 512, x=[bn])
+            Z, Ms = (T.ZV, Ma) if ab else (T.ZM, Mt)
+            mm([(KT[:, 68 * p:68 * p + 68], Z[:, 15 - i:143 - i], Ms[:, lo + i:hi:16, 1:18], 68) for i in range(16)],
+               ["ZV", "ZM", "Mz%d" % c, kt + "c"] + mks + qk, [kt + "m%d" % p], [kt], grp)
+            keys.append(kt + "m%d" % p)
+        mm([(thr, T.NI[:], B("Fb", c)[:], CW)], ["NI", "Fb%d" % c, kt + "c"], [kt + "f"], [kt], grp)
+        scan(B("SK", c)[:], T.RS[:], KT[:, 0:KW], ALU.add, ALU.min, ["RS", kt + "c", kt + "f"] + keys, ["SK%d" % c], KW, x=[kt])
+        tt(A("r", c), B("SK", c)[:, 16::17], thr, ALU.subtract, ["SK%d" % c, kt + "f"], ["r%d" % c], x=[kt])
+        ts(A("c", c), A("r", c), W - 1, None, ALU.bitwise_and, None, ["r%d" % c], ["c%d" % c])
+        bk, Bk = ("BE%d_%d" % (c, k + 2), B("BE", c)[:, k + 2::6]) if k < K - 1 else ("u0%d" % c, B("u0", c)[:])
+        tt(Bk, A("c", c), A("r", c), ALU.max, ["c%d" % c, "r%d" % c], [bk])
+        yl_, yk = B("y16", c)[:, CW * k:CW * k + CW], "y16%d_%d" % (c, k)
+        ts(yl_, Bk, 4096.0, None, ALU.min, None, [bk], [yk])
+        ysrc = XW.indirect(yl_)
+        yo, yi_ = ("yb", "ya") if k % 2 == 0 else ("ya", "yb")
+        if k == 0:
+            gather(Y0_ENG, B(yo, c)[:], ysrc, XK + [yk], [yo + str(c)], CL)
+        else:
+            op("v", lambda: V.tensor_tensor(B(yo, c)[:], ysrc, B(yi_, c)[:], ALU.max), XK + [yk, yi_ + str(c)], [yo + str(c)], (), gc_(CL))
+
+    def place(t, c):
+        KT, kt = B("KT", c), "KT%d" % c
+        so = KT[:, 256:256 + CW]
+        y = B("ya", c)
+        allk = [kt + a for a in ("s", "c", "f", "m0", "m1")]
+        mm([(so, T.ZW[:, 15 - i:143 - i], y[:, i:CL:16], CW) for i in range(16)], ["ZW", "ya%d" % c], allk, [kt], "s%d_%d" % (t, c))
+        cp(A("s1", c), so, [kt + "s"], ["s1%d" % c], x=[kt])
+        ts(A("s2", c), A("s1", c), 15, None, ALU.bitwise_and, None, ["s1%d" % c], ["s2%d" % c])
+        tt(B("s3", c)[:], A("s2", c), T.BASE[:], ALU.add, ["s2%d" % c, "BASE"], ["s3%d" % c])
+        ts(A("p16", c), B("s3", c)[:], c16_, None, ALU.add, None, ["s3%d" % c, "c16_"], ["p16%d" % c])
+
+    def scatter(t, c):
+        if t == TV - 1 and c == 0:
+            buf, o, key = T.XO, 0, "XO"
+        else:
+            buf, o, key = X, 2048 * c, "X%d" % c
+        op("v", lambda: V.tensor_copy(buf[:, o:o + 2048].indirect(A("p16", c)), B("ya", c)[:]), ["p16%d" % c, "ya%d" % c, key], [key], (), gc_(CL, CS))
+        if t == TV - 1:
+            dma("y", T.yx[:, 2048 * c:2048 * c + 2048], buf[:, o:o + 2048], [key], (), 1 << 19, 0.0 if c else 3500.0)
+
+    def rewire_pre(t, c):
+        L, J, kl, kj = state(t, c)
+        BE = B("BE", c)
+        be = ["BE%d_%d" % (c, s) for s in range(6)]
+        n = lambda a: a + str(c)
+        w0k, w5k = ["w0%d_%d" % (c, k) for k in range(K)], ["w5%d_%d" % (c, k) for k in range(K)]
+        ts(B("LB", c)[:], BE[:], 4096.0, 8192.0, ALU.is_lt, ALU.mult, be, [n("LB")], 48)
+        scan(B("PP", c)[:], B("LB", c)[:], BE[:], ALU.add, ALU.min, be + [n("LB")], [n("PP")], 48)
+        scan(B("JJ", c)[:], B("LB", c)[:], T.IX[:], ALU.add, ALU.min, ["IX", n("LB")], [n("JJ")], 48)
+        for k in range(1, K):
+            ts(B("w0", c)[:, CW * k:CW * k + CW], B("PP", c)[:, k + 1::6], -2048.0, None, ALU.add, None, [n("PP")], [w0k[k]])
+            tt(B("w5", c)[:, CW * k:CW * k + CW], B("JJ", c)[:, k + 1::6], state(t, c, k)[1], ALU.subtract, [n("JJ")] + kj, [w5k[k]])
+        tt(B("w2", c)[:], B("w0", c)[:], B("D0", c)[:, 5::6], ALU.mult, w0k + ["D0%d_6" % c], [n("w2")], 64)
+        tt(B("w3", c)[:], B("w2", c)[:], B("K3", c)[:], ALU.add, [n("w2"), n("K3")], [n("w3")], 64)
+        ts(B("w4", c)[:], B("w3", c)[:], 5, W - 1, ALU.arith_shift_right, ALU.bitwise_and, [n("w3")], [n("w4")], 32)
+        tt(B("w1", c)[:], B("w4", c)[:], L, ALU.subtract, [n("w4")] + kl, [n("w1")], 64)
+
+    def rewire(t, c):
+        L, J, kl, kj = state(t, c)
+        n = lambda a: a + str(c)
+        w1k, w5k = [n("w1")], ["w5%d_%d" % (c, k) for k in range(K)]
+        D, dk = B("DD", c)[:], [n("DD")]
+        ts(D, B("y16", c)[:], 4096.0, None, ALU.is_ge, None, ["y16%d_%d" % (c, k) for k in range(K)], dk, 32)
+        tt(B("w2", c)[:], B("w1", c)[:], D, ALU.mult, w1k + dk, [n("w2")], 64)
+        tt(B("w6", c)[:], B("w5", c)[:], D, ALU.mult, w5k + dk, [n("w6")], 64)
+        if t < TV - 1:
+            sb, sk = B("snd%d" % t, c), "snd%d_%d" % (t, c)
+            tt(sb[:, 0], B("w2", c)[:], L, ALU.add, [n("w2")] + kl, [sk + "a"], 64)
+            tt(sb[:, 1], B("w6", c)[:], J, ALU.add, [n("w6")] + kj, [sk + "b"], 64)
+            send(T.cores[(rank + 1) % NR], B("lnd%d" % t, c)[:], sb[:], [sk + "a", sk + "b"], ["lnd%d_%d" % (t, c)])
+        else:
+            tt(T.OUT[:, 0, :, CW * c:CW * c + CW], B("w2", c)[:], L, ALU.add, [n("w2")] + kl, ["OUT%d" % c], 64)
+            tt(T.OUT[:, 1, :, CW * c:CW * c + CW], B("w6", c)[:], J, ALU.add, [n("w6")] + kj, ["OUJ%d" % c], 64)
+
+    for t in range(TV):
+        for c in range(NCH):
+            prep(t, c)
+        if t == TV - 1:
+            dma("y", T.XO[:], X[:, 0:W // 2], ["X0"], ["XO"], 1 << 19)
+        for k in range(K):
+            for c in range(NCH):
+                chain(t, c, k)
+                if k == K - 1:
+                    rewire_pre(t, c)
+                row(t, c, k)
+        for c in range(NCH):
+            place(t, c)
+            rewire(t, c)
+        for c in range(NCH):
+            scatter(t, c)
+        if t < TV - 1:
+            mm([(MS[:, 0:32], T.ON[:], B("DD", c)[:], 32) for c in range(NCH)],
+               ["ON", "DD0", "DD1"], ["MS"], ["MS"], "d%d" % t)
+            op("v", lambda: V.tensor_reduce(T.cnt[:, 0:1], MS[:, 0:32], AxisListType.X, ALU.add), ["MS"], ["cn0"], ["MS"], vc(32))
+            cp(T.cni[:, 0:1], T.cnt[:, 0:1], ["cn0"], ["cn1"])
+            ts(T.cni[:, 1:2], T.cni[:, 0:1], 31, None, ALU.bitwise_and, None, ["cn1"], ["cn2"])
+            cp(T.cnt[:, 1:2], T.cni[:, 1:2], ["cn2"], ["cn3"])
+            ts(T.tha[:, 4 * t + 4:4 * t + 8], T.thf[:], T.cnt[:, 1:2], 241.0, ALU.add, ALU.min, ["thf", "cn3"], ["tha%d" % (t + 1)])
+    send(T.cores[(rank - (TV - 1)) % NR], T.FIN[:], T.OUT[:], ["OUT0", "OUT1", "OUJ0", "OUJ1"], ["FIN"])
+    dma("y", T.yl[:], T.FIN[:, 0], ["FIN"], (), 32768)
+    dma("s", T.yi[:], T.FIN[:, 1], ["FIN"], (), 32768)
+    return ops, nload
+
+
+def depend(ops):
+    lastw, readers, epoch = {}, {}, {}
+    for i, o in enumerate(ops):
+        d = set()
+        for k in o["r"]:
+            if k in lastw:
+                d.add(lastw[k])
+        for k in o["w"]:
+            if k in lastw:
+                d.add(lastw[k])
+            d.update(readers.get(k, ()))
+        for k in o["x"]:
+            e = epoch.setdefault("#" + k, [o["e"], [], []])
+            if e[0] != o["e"]:
+                e[0], e[2], e[1] = o["e"], e[1], []
+            d.update(e[2])
+            e[1].append(i)
+        for k in o["r"]:
+            readers.setdefault(k, []).append(i)
+        for k in o["w"]:
+            lastw[k] = i
+            readers[k] = []
+        d.discard(i)
+        o["d"] = sorted(d)
+
+
+def schedule(ops, nload):
+    n = len(ops)
+    eng = [o["e"] for o in ops]
+    pred = [[(j, 0 if eng[j] == o["e"] == "p" else 1) for j in o["d"]] for o in ops]
+    lastq = {}
+    for i in range(nload):
+        if eng[i] in lastq:
+            pred[i].append((lastq[eng[i]], 2))
+        lastq[eng[i]] = i
+    succ = [[] for _ in ops]
+    for i in range(n):
+        for j, kind in pred[i]:
+            succ[j].append((i, kind))
+    rs = [CFG["seed"]]
+
+    def rnd():
+        rs[0] = (rs[0] * 1103515245 + 12345) % 2147483648
+        return rs[0] / 2147483648.0
+
+    def pack(seq, back, m):
+        dur = [float(o["c"][m]) for o in ops]
+        lag = [float(o["l"][m]) for o in ops]
+        lat = float(LAT[m])
+        st = [0.0] * n
+        busy = {}
+        for i in seq:
+            t = lag[i] if back else 0.0
+            for j, kind in (succ[i] if back else pred[i]):
+                gap = 0.0 if kind != 1 else lat + lag[i if back else j]
+                if st[j] + dur[j] + gap > t:
+                    t = st[j] + dur[j] + gap
+            b = busy.setdefault(eng[i], [])
+            lo, hi = 0, len(b)
+            while lo < hi:
+                mid = (lo + hi) // 2
+                if b[mid][1] <= t:
+                    lo = mid + 1
+                else:
+                    hi = mid
+            while lo < len(b) and b[lo][0] < t + dur[i]:
+                t = max(t, b[lo][1])
+                lo += 1
+            b.insert(lo, (t, t + dur[i]))
+            st[i] = t
+        return st, dur
+
+    def topo_order(key, back):
+        nb, left = (pred if back else succ), [len(succ[i] if back else pred[i]) for i in range(n)]
+        rank_ = sorted(range(n), key=lambda i: key[i])
+        placed, seq = [False] * n, []
+        waiting = {}
+        for i in rank_:
+            stack = [i] if left[i] == 0 else []
+            if left[i]:
+                waiting[i] = True
+            while stack:
+                a = stack.pop()
+                seq.append(a)
+                new = []
+                for j, _ in nb[a]:
+                    left[j] -= 1
+                    if left[j] == 0 and j in waiting:
+                        new.append(j)
+                stack.extend(sorted(new, key=lambda j: -key[j]))
+        return seq
+
+    def length(seq):
+        fin, free = [None] * n, {}
+        for i in seq:
+            t = free.get(eng[i], 0 * CG)
+            for j, kind in pred[i]:
+                if kind == 1:
+                    t = np.maximum(t, fin[j] + LAT)
+            free[eng[i]] = t + ops[i]["c"]
+            fin[i] = free[eng[i]] + ops[i]["l"]
+        return np.max(np.array(fin), axis=0)
+
+    pr, nxt = [0.0] * n, 0.0
+    for i in range(n - 1, -1, -1):
+        pr[i] = float(ops[i]["c"][0] + ops[i]["l"][0]) + max([60.0 + pr[j] for j, _ in succ[i]] + [0.0])
+        if ops[i]["big"]:
+            pr[i] = nxt = max(pr[i], float(ops[i]["c"][0]) * 1.3 + nxt)
+    key = [-a for a in pr]
+    best, base = None, None
+    for r in range(CFG["rounds"]):
+        m = 0 if r % 2 == 0 else int(rnd() * len(CG))
+        st, dur = pack(topo_order(key, False), False, m)
+        seq = sorted(range(n), key=lambda i: (st[i], i))
+        ln = length(seq)
+        if base is None:
+            base = ln
+        val = float(np.sum(WGT * ln / base))
+        if best is None or val < best[0]:
+            best = (val, seq, st, dur, ln)
+        elif r % 2 == 1 or r > CFG["free"]:
+            st, dur = best[2], best[3]
+        lo = rnd() * max(st)
+        hi = lo + CFG["win"]
+        jit = [CFG["jit"] * rnd() * (1.0 if lo <= st[i] <= hi else 0.02) for i in range(n)]
+        if r > CFG["free"] and r % 3:
+            key = [st[i] + jit[i] for i in range(n)]
+            continue
+        bs, dur = pack(topo_order([-(st[i] + dur[i]) + jit[i] for i in range(n)], True), True, m)
+        key = [-(bs[i] + dur[i]) for i in range(n)]
+    ORDER["len"] = best[4]
+    return best[1]
+
+
+def rank_program(g, core, T, topo):
+    if T.rank_of(core) is None:
+        return
+    ops, nload = build_ops(g, core, T, topo)
+    depend(ops)
+    if "seq" not in ORDER:
+        ORDER["seq"] = schedule(ops, nload)
+    order = ORDER["seq"]
+    Q = {"v": g.vector, "s": g.scalar, "p": g.tensor, "g": g, "y": g.sync}
+    pos, nd = {}, 0
+    for i in order:
+        o = ops[i]
+        if o["dma"]:
+            o["sem"], o["at"] = "d%d" % nd, 1
+            nd += 1
+        else:
+            pos[o["e"]] = pos.get(o["e"], 0) + 1
+            o["sem"], o["at"] = ESEM[o["e"]], pos[o["e"]]
+    know = {e: {} for e in Q}
+    need = set()
+    for i in order:
+        o = ops[i]
+        kn = know[o["e"]]
+        want = {}
+        for j in sorted(o["d"], key=lambda j: -ops[j]["at"]):
+            a = ops[j]
+            if a["e"] == o["e"] == "p" or kn.get(a["sem"], 0) >= a["at"]:
+                continue
+            want[a["sem"]] = j
+            kn[a["sem"]] = a["at"]
+            if not (a["dma"] and a["e"] == "g"):
+                for s, v in a["kn"].items():
+                    kn[s] = max(kn.get(s, 0), v)
+        o["waits"] = sorted(want.values())
+        o["kn"] = dict(kn)
+        need.update(want.values())
+    first, last = {}, {}
+    for i in order:
+        gp = ops[i]["grp"]
+        if gp is not None:
+            first.setdefault(gp, i)
+            last[gp] = i
+    total, nsend = {}, 0
+    for i in order:
+        o = ops[i]
+        q = Q[o["e"]]
+        for j in o["waits"]:
+            q.wait_ge(T.sem[ops[j]["sem"]], ops[j]["val"])
+        if o["dma"]:
+            if o["e"] == "g":
+                o["fn"](T.sem[o["sem"]])
+                nsend += o["inc"]
+            else:
+                o["fn"]().then_inc(T.sem[o["sem"]], 16)
+            o["val"] = total[o["sem"]] = o["inc"]
+            continue
+        if o["e"] == "p":
+            gp, lst = o["grp"], o["fn"]
+            for a, m in enumerate(lst):
+                ins = q.matmul(m[0], m[1], m[2], gp is None or (first[gp] == i and a == 0), gp is None or ((last[gp] == i or "stop" in o) and a == len(lst) - 1))
+        else:
+            ins = o["fn"]()
+        if i in need:
+            total[o["sem"]] = total.get(o["sem"], 0) + 1
+            ins.then_inc(T.sem[o["sem"]], 1)
+        o["val"] = total.get(o["sem"], 0)
+    g.wait_ge(T.sem.sent, nsend)
+    for s in sorted(total):
+        g.wait_ge(T.sem[s], total[s])

@@ -5,41 +5,48 @@ ALU, ACT = AluOpType, ActivationFunctionType
 W, F, K, TV, NR = 4096, 2048, 4, 3, 4
 NCH, CW = 2, 8
 CL = 16 * CW
-PC, NP, NB = 64, 2, 5
-QFIRST = True
-KW = 17 * CW
+HC = CL // 2
 NENG = 8
-XL_ENG = "s"
-Y0_ENG = "v"
-SPLIT = (True, True)
-XFIRST = True
-ABS = [(0, 1, 0), (0, 2, 0), (0, 3, 0), (1, 3, 1)]
+KM = 69632.0
+BIG = 1073741824.0
+MAGIC = 25769803776.0
+KW = 17 * CW
+NB = 5
+PIECES = {None: (("s", 2), ("s", 1), ("s", 1)), (0, 0): (("s", 1), ("v", 1), ("s", 1), ("s", 1))}
+ABS = [(1, 3, 1)]
+EARLY = (0,)
+Q_ENG = "g"
+XL_ENG = ("vs", "ss")
+Y0_ENG = "s"
+PREP_ENG = "s"
 CYC = 0.83 * np.array([1.25, 1.1, 1.4, 1.25, 1.25])
 CG = np.array([1.56, 1.2, 1.9, 1.56, 1.56])
 CS = np.array([3.8, 2.5, 5.0, 3.8, 3.8])
-PE = 0.5 * CYC * np.array([1.0, 1.0, 1.0, 1.0, 1.3])
-FIX = np.array([0.0, 0.0, 0.0, 30.0, 0.0])
-LAT = np.array([60.0, 60.0, 60.0, 100.0, 40.0])
-REM = np.array([3000.0, 2500.0, 3500.0, 4000.0, 3000.0])
-WGT = np.array([2.0, 1.0, 1.0, 1.0, 1.0])
-CFG = {"rounds": 300, "jit": 100.0, "seed": 1, "free": 9999, "win": 1e9}
+PE = 0.5 * CYC * np.array([1.1, 1.0, 1.0, 1.0, 1.3])
+FIX = np.array([10.0, 0.0, 0.0, 30.0, 0.0])
+LAT = np.array([70.0, 60.0, 60.0, 100.0, 40.0])
+REM = np.array([3000.0, 1500.0, 3500.0, 3000.0, 2000.0])
+ISS = np.array([400.0, 100.0, 600.0, 300.0, 100.0])
+DFX = np.array([800.0, 800.0, 1800.0, 1000.0, 1200.0])
+DBW = np.array([400.0, 350.0, 180.0, 350.0, 250.0])
+WGT = np.array([2.0, 0.5, 2.0, 0.5, 0.5])
+CFG = {"rounds": 80, "jit": 30.0, "seed": 1, "swaps": 25000, "temp": 0.0005, "models": (0, 2), "eps": 0.1}
 ORDER = {}
 
 SCRATCH = {
-    "X": ("sbuf", [128, W + 16], "bfloat16"),
-    "XO": ("sbuf", [128, W // 2], "bfloat16"),
-    "FA": ("sbuf", [128, F], "int32"),
+    "XA": ("sbuf", [128, W + 16], "bfloat16"), "XB": ("sbuf", [128, W + 16], "bfloat16"),
+    "FA": ("sbuf", [128, F + 8], "int32"), "LJ": ("sbuf", [128, 2, 4, 16], "float32"),
     "lci": ("sbuf", [128, 4, 16], "int32"), "upi": ("sbuf", [128, 4, 16], "int32"), "exi": ("sbuf", [128, 16], "int32"),
     "thi": ("sbuf", [128, 4], "int32"), "wti": ("sbuf", [128, 4], "int32"),
-    "thb": ("sbuf", [128, 4], "bfloat16"), "thf": ("sbuf", [128, 4], "float32"), "tha": ("sbuf", [128, 12], "float32"),
+    "thb": ("sbuf", [128, 4], "bfloat16"), "thf": ("sbuf", [128, 4, CW], "float32"), "TH": ("sbuf", [128, TV, 4, CW], "bfloat16"),
     "IO": ("sbuf", [128, 160], "float32"), "pci": ("sbuf", [128, 4], "int32"), "col": ("sbuf", [128, 12], "float32"),
     "E8": ("sbuf", [128, 128], "bfloat16"), "E8i": ("sbuf", [128, 128], "float32"),
-    "ID": ("sbuf", [128, 128], "bfloat16"), "NI": ("sbuf", [128, 128], "bfloat16"), "ON": ("sbuf", [128, 128], "bfloat16"),
-    "NQ": ("sbuf", [128, 128], "bfloat16"), "I2": ("sbuf", [128, 128], "bfloat16"),
+    "NI": ("sbuf", [128, 128], "bfloat16"), "ON": ("sbuf", [128, 128], "bfloat16"),
+    "ID": ("sbuf", [128, 128], "bfloat16"), "NQ": ("sbuf", [128, 128], "bfloat16"), "I2": ("sbuf", [128, 128], "bfloat16"),
     "ZV": ("sbuf", [128, 144], "bfloat16"), "ZM": ("sbuf", [128, 144], "bfloat16"), "ZW": ("sbuf", [128, 144], "bfloat16"),
-    "G0": ("sbuf", [128, 160], "float32"), "G1": ("sbuf", [128, 160], "float32"),
-    "RS": ("sbuf", [128, KW], "float32"), "IX": ("sbuf", [128, 6 * CW], "float32"), "KC": ("sbuf", [128, 4 * CW], "float32"),
-    "BASE": ("sbuf", [128, CW], "float32"), "E16": ("sbuf", [128, 16], "uint16"),
+    "G0": ("sbuf", [128, 160], "float16"), "G1": ("sbuf", [128, 160], "float16"),
+    "RS": ("sbuf", [128, KW], "float32"), "IX": ("sbuf", [128, 4 * CW], "float32"), "KC": ("sbuf", [128, CW, 4], "float32"),
+    "BASE": ("sbuf", [128, CW], "float32"),
     "OUT": ("sbuf", [128, 2, 4, 16], "float32"), "FIN": ("sbuf", [128, 2, 4, 16], "float32"),
     "cnt": ("sbuf", [128, 4], "float32"), "cni": ("sbuf", [128, 4], "int32"),
 }
@@ -47,27 +54,27 @@ for _c in range(NCH):
     for _n, _s, _d in (
         ("V", [16 * CL], "bfloat16"), ("M", [CL, 18], "bfloat16"), ("Ma", [CL, 18], "bfloat16"), ("XL", [4 * CL], "bfloat16"),
         ("ya", [CL], "bfloat16"), ("yb", [CL], "bfloat16"),
-        ("c16", [CL], "uint16"), ("cf", [4, 2, 16], "float32"), ("ct", [4, 2, 17], "float32"), ("SK", [KW], "float32"),
-        ("BE", [6 * CW], "float32"), ("MK", [24 * CW], "float32"), ("D0", [24 * CW], "float32"),
-        ("D1", [6 * CW], "float32"), ("SN", [6 * CW], "float32"),
-        ("si", [6 * CW], "int32"), ("so", [3 * CW], "uint16"), ("y16", [4 * CW], "uint16"), ("w0", [4 * CW], "float32"),
-        ("L16", [4 * CW], "uint16"), ("Fb", [CW], "bfloat16"), ("u0", [CW], "float32"),
-        ("LB", [6 * CW], "float32"), ("DD", [4 * CW], "bfloat16"), ("PP", [6 * CW], "float32"), ("JJ", [6 * CW], "float32"),
-        ("K3", [4 * CW], "float32"), ("w1", [4 * CW], "float32"), ("w2", [4 * CW], "float32"), ("w3", [4 * CW], "int32"),
-        ("w4", [4 * CW], "int32"), ("w5", [4 * CW], "float32"), ("w6", [4 * CW], "float32"), ("w7", [4 * CW], "float32"),
-        ("s3", [CW], "float32"),
-        ("snd0", [2, 4, CW], "float32"), ("snd1", [2, 4, CW], "float32"),
-        ("lnd0", [2, 4, CW], "float32"), ("lnd1", [2, 4, CW], "float32"),
+        ("c16", [CL], "uint16"), ("cf", [4, 2, 16], "float16"), ("ct", [4, 2, 17], "float16"), ("SK", [KW], "float32"),
+        ("BE", [4 * CW + 4], "float32"), ("MK", [4 * CW, 4], "float32"), ("D0", [16 * CW, 4], "float32"), ("D1", [16 * CW, 4], "float32"),
+        ("se0", [CW], "float32"), ("se1", [CW], "float32"), ("le0", [CW], "float32"), ("le1", [CW], "float32"),
+        ("SN", [32 * CW], "float32"), ("si", [6 * CW], "int32"), ("so", [4 * CW], "uint16"), ("L16", [4 * CW], "uint16"),
+        ("sf", [3 * CW], "float32"),
+        ("LB", [4 * CW], "float32"), ("DD", [CW, 4], "bfloat16"), ("PP", [4 * CW], "float32"), ("JJ", [4 * CW], "float32"),
+        ("K3", [CW, 4], "float32"), ("w0", [CW, 4], "float32"), ("w1", [CW, 4], "float32"), ("w2", [CW, 4], "float32"),
+        ("w3", [CW, 4], "int32"), ("w4", [CW, 4], "int32"), ("w5", [CW, 4], "float32"), ("w7", [CW, 4], "float32"),
+        ("st0", [2, CW, 4], "float32"), ("st1", [2, CW, 4], "float32"), ("st2", [2, CW, 4], "float32"),
+        ("snd0", [2, CW, 4], "float32"), ("snd1", [2, CW, 4], "float32"), ("snd2", [2, CW, 4], "float32"),
     ):
         SCRATCH["%s_%d" % (_n, _c)] = ("sbuf", [128] + _s, _d)
     SCRATCH["KT_%d" % _c] = ("psum", [128, 512], "float32")
 for _p in range(NB):
     SCRATCH["PB_%d" % _p] = ("psum", [128, 32, 8, 2], "float32")
 SCRATCH["MS"] = ("psum", [128, 512], "float32")
-SI = {"r": 0, "c": 1, "u": 2, "n": 3, "s1": 4, "s2": 5}
-SO = {"n16": 0, "b16": 1, "p16": 2}
+SI = {"r": 0, "c": 1, "s1": 2, "s2": 3}
+SO = {"b16": 0, "n16": 1, "p16": 2, "y16": 3}
+SF = {"s3": 0, "ex": 1}
 
-SEMAPHORES = ["sv", "ss", "sp", "sg", "sent"] + ["d%d" % _i for _i in range(24)]
+SEMAPHORES = ["sv", "ss", "sp", "sg", "sent"] + ["d%d" % _i for _i in range(28)]
 ESEM = {"v": "sv", "s": "ss", "p": "sp", "g": "sg"}
 
 
@@ -89,6 +96,14 @@ def build_ops(g, core, T, topo):
         else:
             op("v", lambda: V.tensor_scalar(out, in0, s1, s2, o0, o1), r, w, x, vc(n))
 
+    def lin(eng, out, in0, a, b, r, w, n=64):
+        if eng == "v":
+            ts(out, in0, a, b, ALU.mult, ALU.add, r, w, n)
+        elif eng == "g":
+            op("g", lambda: g.affine_select(out, in0, [[0, CW]], ALU.is_ge, 0.0, 0, 0), r, w, (), 170 + 2 * CW * CYC)
+        else:
+            op("s", lambda: S.activation(out, in0, ACT.Identity, b, a), r, w, (), vc(n))
+
     def tt(out, a, b, o, r, w, n=16, x=()):
         op("v", lambda: V.tensor_tensor(out, a, b, o), r, w, x, vc(n))
 
@@ -104,61 +119,59 @@ def build_ops(g, core, T, topo):
     def gc_(n, c=None):
         return 55 + n * (CG if c is None else c) * CYC
 
-    def gather(eng, out, src, r, w, n, big=False):
-        if eng == "v":
-            op("v", lambda: V.tensor_copy(out, src), r, w, (), gc_(n))
+    def gather(eng, out, src, r, w, n, add=0.0, big=False):
+        if eng == "v" and add:
+            op("v", lambda: V.tensor_scalar(out, src, add, None, ALU.add), r, w, (), gc_(n), big=big)
+        elif eng == "v":
+            op("v", lambda: V.tensor_copy(out, src), r, w, (), gc_(n), big=big)
+        elif add:
+            op("s", lambda: S.activation(out, src, ACT.Identity, add), r, w, (), gc_(n) + 10, big=big)
         else:
             op("s", lambda: S.activation(out, src, ACT.Copy), r, w, (), gc_(n) + 10, big=big)
 
-    def mm(lst, r, w, x, grp, f32=False):
-        n = sum(max(64, a[3]) for a in lst) * (4 if f32 else 1)
-        op("p", lst, r, w, x, 10 + n * PE, grp=grp)
+    def mm(lst, r, w, x, grp):
+        op("p", lst, r, w, x, 10 + sum(max(64, a[3]) for a in lst) * PE, grp=grp)
 
     def dma(eng, out, in_, r, w, nbytes, after=0.0):
         q = {"y": g.sync, "s": g.scalar}[eng]
-        op(eng, lambda: q.dma_start(out, in_), r, w, (), 60.0, dma=1800.0 + nbytes / 180.0 + after)
+        op(eng, lambda: q.dma_start(out, in_), r, w, (), 60.0, dma=DFX + nbytes / DBW + after)
 
-    def iota(out, pat, base, w, cost):
-        op("g", lambda: g.iota(out, pat, base, 0, allow_small_or_imprecise_dtypes=True), (), w, (), cost)
+    def iota(out, pat, base, w, cost, r=()):
+        op("g", lambda: g.iota(out, pat, base, 0, allow_small_or_imprecise_dtypes=True), r, w, (), cost)
 
     def send(dst, out, in_, r, w):
         rid, pid = topo.addr(dst)[0], topo.addr(dst)[1]
         m = 0
         for e in topo.engines(core, dst)[:NENG]:
             m += 1 << e
-        op("g", lambda sem: g.remote_dma(out, in_, sem, T.sem.sent, pid, rid, m), r, w, (), 100.0, dma=REM + (2000.0 if not [1 for o in ops if o["dma"] and o["e"] == "g"] else 0.0), inc=NENG)
+        op("g", lambda sem: g.remote_dma(out, in_, sem, T.sem.sent, pid, rid, m), r, w, (), ISS, dma=REM + (2000.0 if not [1 for o in ops if o["dma"] and o["e"] == "g"] else 0.0), inc=NENG)
 
     def B(n, c):
         return T["%s_%d" % (n, c)]
 
-    def A(n, c):
-        if n in SI:
-            return B("si", c)[:, CW * SI[n]:CW * SI[n] + CW]
-        return B("so", c)[:, CW * SO[n]:CW * SO[n] + CW]
+    def A(n, c, lo=0, hi=CW):
+        buf, tab = ("si", SI) if n in SI else ("so", SO) if n in SO else ("sf", SF)
+        return B(buf, c)[:, CW * tab[n] + lo:CW * tab[n] + hi]
 
     MS = T.MS
-    X, XW = T.X, T.X[:, 0:W + 16]
+    XS = (T.XA, T.XB)
     dma("y", T.lci[:], T.lc[:], (), ["lci"], 32768)
     dma("s", T.exi[:], T.ex[:], (), ["exi"], 8192)
     dma("y", T.upi[:], T.up[:], (), ["upi"], 32768)
     dma("s", T.thi[0:8, :], T.th[:], (), ["thi"], 128)
-    if XFIRST:
-        dma("y", X[:, 0:W], T.xs[:], (), ["X0", "X1"], 1 << 20)
-        dma("s", T.wti[:, 0:1], T.wt[:], (), ["wti"], 512)
-        dma("s", T.FA[:], T.fa[:], (), ["FA"], 2 << 20)
-    else:
-        dma("y", T.FA[:], T.fa[:], (), ["FA"], 1 << 20)
-        dma("s", T.wti[:, 0:1], T.wt[:], (), ["wti"], 512)
-        dma("s", X[:, 0:W], T.xs[:], (), ["X0", "X1"], 2 << 20)
+    dma("y", T.XA[:, 0:W], T.xs[:], (), ["X0_0", "X0_1"], 1 << 20)
+    dma("s", T.wti[:, 0:1], T.wt[:], (), ["wti"], 512)
+    dma("s", T.FA[:, F:F + 8], T.fa[:, 0:8], (), ["FB"], 4096)
+    dma("s", T.FA[:, 0:F], T.fa[:], (), ["FA"], 2 << 20)
     nload = len(ops)
     op("g", lambda: g.iota(T.pci[:, 0:1], [[1, 1]], 0, 1), (), ["pc0"], (), 150)
     iota(T.IO[:], [[1, 160]], -16, ["IO"], 450)
     iota(T.E8i[0:8, :], [[1, 8], [0, 16]], 0, ["E8i"], 400)
-    iota(T.KC[:], [[32, 4], [0, CW]], 65536 - 4194304, ["KC"], 200)
-    iota(T.IX[:], [[0, CW], [1, 6]], -2, ["IX"], 250)
+    iota(T.KC[:], [[0, CW], [32, 4]], 65536 - 4194304, ["KC"], 200)
+    iota(T.IX[:], [[0, CW], [1, 4]], W - 1, ["IX"], 200)
     iota(T.BASE[:], [[256, CW]], 0, ["BASE"], 150)
     col = T.col
-    cP, cG, cH1, cH0, cM, c16_, cW = (col[:, j:j + 1] for j in range(7))
+    cP, cG, cH1, cH0, c16_, cW = (col[:, j:j + 1] for j in range(6))
     cp(cP, T.pci[:, 0:1], ["pc0"], ["cP"])
     ts(T.pci[:, 1:2], T.pci[:, 0:1], 4, None, ALU.arith_shift_right, None, ["pc0"], ["pc1"])
     ts(T.pci[:, 2:3], T.pci[:, 0:1], 4, 1, ALU.arith_shift_right, ALU.bitwise_and, ["pc0"], ["pc2"])
@@ -169,196 +182,203 @@ def build_ops(g, core, T, topo):
     ts(c16_, T.pci[:, 3:4], 16.0, None, ALU.mult, None, ["pc3"], ["c16_"])
     cp(cW, T.wti[:, 0:1], ["wti"], ["cW"])
     ts(T.ID[:], T.IO[:, 16:144], cP, None, ALU.is_equal, None, ["IO", "cP"], ["ID"], 128)
-    ts(cM, T.pci[:, 3:4], 4096.0, 4096.0, ALU.mult, ALU.add, ["pc3"], ["cM"])
-    ts(T.NI[:], T.IO[:, 16:144], cP, 65536.0, ALU.is_equal, ALU.mult, ["IO", "cP"], ["NI"], 128)
-    ts(T.NQ[:], T.IO[:, 16:144], cP, -1.0, ALU.is_equal, ALU.mult, ["IO", "cP"], ["NQ"], 128)
-    ts(T.I2[:], T.IO[:, 16:144], cP, 2.0, ALU.is_equal, ALU.mult, ["IO", "cP"], ["I2"], 128)
-    ms(T.ON[:], 1.0, ["ON"])
-    for nm, sc in (("ZV", 65536.0), ("ZM", -65536.0), ("ZW", cW)):
-        ms(T[nm][:], 0.0, [nm], 72)
-        ts(T[nm][:, 15:128:16], T.IO[:, 16:24], cG, sc, ALU.is_equal, ALU.mult, ["IO", "cG", nm] + (["cW"] if nm == "ZW" else []), [nm])
+    for nm, sc in (("NQ", -1.0), ("I2", 2.0), ("NI", KM)):
+        lin("s", T[nm][:], T.ID[:], sc, 0.0, ["ID"], [nm], 128)
+    lin("s", T.ON[:], T.ID[:], 0.0, 1.0, ["ID"], ["ON"], 128)
+    ms(T.ZW[:], 0.0, ["ZW"], 72)
+    ts(T.ZW[:, 15:128:16], T.IO[:, 16:24], cG, None, ALU.is_equal, None, ["IO", "cG", "ZW"], ["ZW"])
+    lin("s", T.ZM[:], T.ZW[:], -KM, 0.0, ["ZW"], ["ZM"], 144)
+    lin("s", T.ZV[:], T.ZW[:], KM, 0.0, ["ZW"], ["ZV"], 144)
+    lin("s", T.ZW[:], T.ZW[:], cW, 0.0, ["ZW", "cW"], ["ZW"], 144)
     ts(T.G0[:], T.IO[:], cP, cH0, ALU.is_equal, ALU.mult, ["IO", "cP", "cH0"], ["G0"], 160)
     ts(T.G1[:], T.IO[:], cP, cH1, ALU.is_equal, ALU.mult, ["IO", "cP", "cH1"], ["G1"], 160)
-    ms(T.RS[:], 0.0, ["RS"], KW)
-    ms(T.RS[:, 1:KW:17], 67108864.0, ["RS"])
-    ms(X[:, W:W + 16], 0.0, ["XZ"])
+    iota(T.RS[:], [[0, KW]], -W, ["RS"], 420)
+    for j in range(2):
+        ms(T.RS[:, j::17], BIG, ["RS"])
+    for X in XS:
+        ms(X[:, W:W + 16], 0.0, ["XZ"])
+        ms(X[:, W + 1:W + 2], 31.0, ["XZ"])
+    cp(T.LJ[:, 0], T.lci[:], ["lci"], ["LJ0"])
+    ts(T.LJ[:, 1], T.upi[:], float(W), None, ALU.add, None, ["upi"], ["LJ1"])
     ts(T.E8[0:8, :], T.E8i[0:8, :], col[0:8, 0:1], None, ALU.is_equal, None, ["E8i", "cP"], ["E8"], 128)
-    cp(T.thb[0:8, :], T.thi[0:8, :], ["thi"], ["thb"])
+    ts(T.thb[0:8, :], T.thi[0:8, :], -1.0, None, ALU.add, None, ["thi"], ["thb"])
     mm([(MS[:, 0:4], T.E8[0:8, :], T.thb[0:8, :], 4)], ["E8", "thb"], ["MS"], ["MS"], None)
-    ts(T.tha[:, 0:4], MS[:, 0:4], 241.0, None, ALU.min, None, ["MS"], ["tha0"], x=["MS"])
-    cp(T.thf[:], MS[:, 0:4], ["MS"], ["thf"], x=["MS"])
-    cp(T.E16[:], T.exi[:], ["exi"], ["E16"])
+    for k in range(K):
+        ts(T.thf[:, k, :], T.IO[:, 0:CW], 0.0, MS[:, k:k + 1], ALU.mult, ALU.add, ["MS", "IO"], ["thf%d" % k], x=["MS"])
+    thk = ["thf%d" % k for k in range(K)]
+    ts(T.TH[:, 0], T.thf[:], 240.0, None, ALU.min, None, thk, ["TH0"])
     for c in range(NCH):
-        ms(B("BE", c)[:], 1.0, ["BE%d_%d" % (c, s) for s in range(6)])
-        cp(B("BE", c)[:, 1::6], T.exi[:, CW * c:CW * c + CW], ["exi"], ["BE%d_1" % c])
-        ms(B("MK", c)[:, 0::6], -2048.0, ["MK%d_0" % c])
-        ts(B("w0", c)[:, 0:CW], T.exi[:, CW * c:CW * c + CW], -2048.0, None, ALU.add, None, ["exi"], ["w0%d_0" % c])
-        ms(B("w5", c)[:, 0:CW], 0.0, ["w5%d_0" % c])
-        ms(B("D0", c)[:], 1.0, ["D0%d_0" % c, "D0%d_6" % c], 224)
-        ms(B("D0", c)[:, 0::6], 0.0, ["D0%d_0" % c])
-        ms(B("Ma", c)[:, :, 1], 0.0, ["Mz%d" % c])
-        ms(B("ct", c)[:, :, :, 0], 0.0, ["cz%d" % c])
+        ex = T.exi[:, CW * c:CW * c + CW]
+        D0, D1 = B("D0", c), B("D1", c)
+        for k in range(K):
+            lin("sv"[k % 2], B("st0", c)[:, :, :, k], T.LJ[:, :, k, CW * c:CW * c + CW], 1.0, 0.0, ["LJ0", "LJ1"], ["st0_%d_%d" % (c, k)])
+        cp(A("ex", c), ex, ["exi"], ["ex%d" % c])
+        iota(B("BE", c)[:], [[0, 4 * CW + 4]], 0, ["BE%d_%d" % (c, s) for s in range(4)], 210)
+        k0 = ["D0%da" % c, "D0%db" % c, "D0c%d" % c]
+        k1 = ["D1c%d" % c, "D1k%da" % c, "D1k%db" % c] + ["D1%d_%d" % (c, k) for k in range(K)]
+        ms(D0[:], 1.0, k0, 512)
+        lin("s", D1[:], D0[:], 0.0, 0.0, k0, k1, 512)
+        ms(D0[:, 0::16, :], 0.0, ["D0c%d" % c])
+        ms(D1[:, 1::16, :], -1024.0, ["D1c%d" % c])
+        ms(D1[:, 14::16, :], MAGIC, ["D1c%d" % c])
+        ms(D1[:, 15::16, :], -MAGIC, ["D1c%d" % c])
+        cp(D1[:, 0::16, 0], ex, ["exi"], ["D1%d_0" % c])
+        iota(B("Ma", c)[:, :, 1], [[0, CL]], 0, ["Mz%d" % c], 400)
+        ts(B("ct", c)[:, :, :, 0], T.IO[:, 0:CW], 0.0, -2048.0, ALU.mult, ALU.add, ["IO"], ["cz%d" % c])
 
-    XK = ["X0", "X1", "XZ"]
     nbank = [0]
 
-    def state(t, c, k=None):
-        kk = slice(0, K) if k is None else k
+    def state(t, c):
+        a = B("st%d" % t, c)
         if t == 0:
-            return T.lci[:, kk, CW * c:CW * c + CW], T.upi[:, kk, CW * c:CW * c + CW], ["lci"], ["upi"]
-        a = B("lnd%d" % (t - 1), c)
-        key = ["lnd%d_%d" % (t - 1, c)]
-        return a[:, 0, kk, :], a[:, 1, kk, :], key, key
+            return a[:, 0], a[:, 1], ["st0_%d_%d" % (c, k) for k in range(K)], ["st0_%d_%d" % (c, k) for k in range(K)]
+        return a[:, 0], a[:, 1], ["st%d_%d" % (t, c)], ["st%d_%d" % (t, c)]
 
     def prep(t, c):
         L, J, kl, kj = state(t, c)
-        MK, D0 = B("MK", c), B("D0", c)
-        ts(D0[:, 5::6], L, 1184.0, None, ALU.add, None, kl, ["D0%d_6" % c], 32)
-        ts(MK[:, 5::6], L, 2080.0, float(2464 * t - 4194304), ALU.mult, ALU.add, kl, ["MK%d_5" % c], 32)
+        st = B("st%d" % t, c)
+        L0, k0 = (B("le%d" % (t - 1), c)[:], ["le%d_%d" % (t - 1, c)]) if t and c in EARLY else (st[:, 0, :, 0], kl)
+        if t and c in EARLY:
+            parts = ((slice(0, 1), L0, k0, ["a"]), (slice(1, K), st[:, 0, :, 1:K], kl, ["b"]))
+        else:
+            parts = ((slice(0, K), L, kl, ["a", "b"]),)
+        for rows, src, ks, ab in parts:
+            lin(PREP_ENG, B("D0", c)[:, 13::16, rows], src, 1.0 / 32, 37.0, ks, ["D0%d%s" % (c, a) for a in ab])
+            lin(PREP_ENG, B("D1", c)[:, 13::16, rows], src, 33.0, float(77 * t + 37 * 1024 - 80 * F - 1024), ks, ["D1k%d%s" % (c, a) for a in ab])
+        lin("g", B("BE", c)[:, 0:32:4], A("ex", c), 1.0, 0.0, ["ex%d" % c], ["BE%d_0" % c])
         for s in range(4):
-            ts(MK[:, s + 1::6], J, float(s - 1), None, ALU.is_equal, None, kj, ["MK%d_%d" % (c, s + 1)], 32)
-        cp(B("L16", c)[:], L, kl, ["L16%d" % c], 32)
-        ts(B("w7", c)[:], L, 2048.0, None, ALU.mult, None, kl, ["w7%d" % c], 32)
+            ts(B("MK", c)[:, s::4, :], J, float(W - 1 + s), None, ALU.is_equal, None, kj, ["MK%d_%d" % (c, s)])
+        for k in range(K):
+            cp(B("L16", c)[:, CW * k:CW * k + CW], st[:, 0, :, k] if k else L0, kl if k else k0, ["L16%d_%d" % (c, k)])
+        lin(PREP_ENG, B("w7", c)[:], L, 2048.0, 0.0, kl, ["w7%d" % c])
         tt(B("K3", c)[:], B("w7", c)[:], T.KC[:], ALU.add, ["w7%d" % c, "KC"], ["K3%d" % c], 64)
-        gather("v", B("XL", c)[:, 0:CL], XW.indirect(B("L16", c)[:, 0:CW]), XK + ["L16%d" % c], ["XL%d_0" % c], CL)
-        gather(XL_ENG, B("XL", c)[:, CL:4 * CL], XW.indirect(B("L16", c)[:, CW:4 * CW]), XK + ["L16%d" % c], ["XL%d_1" % c], 3 * CL)
+        gather(XL_ENG[c][0], B("XL", c)[:, 0:CL], XW.indirect(B("L16", c)[:, 0:CW]), XK + ["L16%d_0" % c], ["XL%d_0" % c], CL)
+        gather(XL_ENG[c][1], B("XL", c)[:, CL:4 * CL], XW.indirect(B("L16", c)[:, CW:4 * CW]), XK + ["L16%d_%d" % (c, k) for k in range(1, K)], ["XL%d_1" % c], 3 * CL)
 
     def chain(t, c, k):
-        BE, SN, n6 = B("BE", c), B("SN", c), 6 * CW
-        th = T.tha[:, 4 * t + k:4 * t + k + 1]
-        if k == 0:
-            E, ek = B("w0", c)[:, 0:CW], "w0%d_0" % c
-            tt(B("u0", c)[:], B("D0", c)[:, 5:n6:6], E, ALU.mult, ["D0%d_6" % c, ek], ["u0%d" % c])
-            tt(A("u", c), B("u0", c)[:], B("MK", c)[:, 5:n6:6], ALU.add, ["u0%d" % c, "MK%d_5" % c], ["u%d" % c])
-            ts(B("Fb", c)[:], E, 2048.0, th, ALU.is_lt, ALU.mult, [ek, "tha%d" % t], ["Fb%d" % c])
-        else:
-            tt(B("D1", c)[:], BE[:], B("MK", c)[:, n6 * k:n6 * k + n6], ALU.mult,
-               ["BE%d_%d" % (c, s) for s in range(6)] + ["MK%d_%d" % (c, s) for s in range(6)], ["D1%d" % c], 96)
-            scan(SN[:], B("D0", c)[:, n6 * k:n6 * k + n6], B("D1", c)[:], ALU.mult, ALU.add, ["D0%d_0" % c, "D0%d_6" % c, "D1%d" % c], ["SN%d" % c], 48)
-            ts(A("u", c), SN[:, 5::6], 16777216.0, -16777216.0, ALU.min, ALU.max, ["SN%d" % c], ["u%d" % c])
-            ts(A("b16", c), SN[:, 4::6], 2048.0, 4096.0, ALU.add, ALU.min, ["SN%d" % c], ["b16%d" % c])
-            ts(B("Fb", c)[:], SN[:, 4::6], 2048.0, th, ALU.is_lt, ALU.mult, ["SN%d" % c, "tha%d" % t], ["Fb%d" % c])
-        ts(A("n", c), A("u", c), 5, F - 1, ALU.arith_shift_right, ALU.bitwise_and, ["u%d" % c], ["n%d" % c])
-        cp(A("n16", c), A("n", c), ["n%d" % c], ["n16%d" % c])
-        gather("v", B("c16", c)[:], T.FA[:].indirect(A("n16", c)), ["FA", "n16%d" % c], ["c16%d" % c], CL)
+        SN, D1 = B("SN", c), B("D1", c)
+        if k:
+            tt(D1[:, 0::4, k], B("BE", c)[:, 0:32], B("MK", c)[:, :, k], ALU.mult,
+               ["BE%d_%d" % (c, s) for s in range(4)] + ["MK%d_%d" % (c, s) for s in range(4)], ["D1%d_%d" % (c, k)], 64)
+        scan(SN[:, 0:128], B("D0", c)[:, :, k], D1[:, :, k], ALU.mult, ALU.add,
+             ["D0%d%s" % (c, "ab"[k > 0]), "D0c%d" % c, "D1c%d" % c, "D1k%d%s" % (c, "ab"[k > 0]), "D1%d_%d" % (c, k)], ["SN%d" % c], 128)
+        tt(SN[:, 140::16], SN[:, 13:128:16], SN[:, 15:128:16], ALU.subtract, ["SN%d" % c], ["w%d" % c])
+        ts(B("so", c)[:, 0:2 * CW], SN[:, 12::16], 1024.0 - 31.0 / 64, float(W + 1), ALU.add, ALU.min, ["SN%d" % c, "w%d" % c], ["n16%d" % c, "b16%d" % c])
+        gather("v", B("c16", c)[:], T.FA[:].indirect(A("n16", c)), ["FA", "FB", "n16%d" % c], ["c16%d" % c], CL)
         for h in range(2):
-            ts(B("cf", c)[:, :, h, :], B("c16", c)[:, PC * h:PC * h + PC], cM, None, ALU.add, None, ["c16%d" % c, "cM"], ["cf%d_%d" % (c, h)], PC)
-        op("v", lambda: V.transpose(B("ct", c)[:, :, :, 1:17], B("cf", c)[:]), ["cf%d_0" % c, "cf%d_1" % c], ["ct%d" % c], (), vc(CL))
+            ts(B("cf", c)[:, :, h, :], B("c16", c)[:, HC * h:HC * h + HC], -2048.0, None, ALU.add, None, ["c16%d" % c], ["cf%d_%d" % (c, h)])
+        op("v", lambda: V.transpose(B("ct", c)[:, :, :, 1:17], B("cf", c)[:]), ["cf%d_0" % c, "cf%d_1" % c], ["ct%d" % c], (), vc(64))
 
     def row(t, c, k):
         KT, kt, grp = B("KT", c), "KT%d" % c, "k%d_%d_%d" % (t, c, k)
         Vt, Mt, Ma = B("V", c), B("M", c), B("Ma", c)
-        off, ok = (T.E16[:, CW * c:CW * c + CW], "E16") if k == 0 else (A("b16", c), "b16%d" % c)
-        op("v", lambda: V.tensor_tensor(Mt[:, :, 0], XW.indirect(off), B("XL", c)[:, CL * k:CL * k + CL], ALU.max),
+        ok = "b16%d" % c
+        qsrc = XW.indirect(A("b16", c))
+        op("v", lambda: V.tensor_tensor(Mt[:, :, 0], qsrc, B("XL", c)[:, CL * k:CL * k + CL], ALU.max),
            XK + [ok, "XL%d_%d" % (c, min(k, 1))], ["q%d" % c], (), gc_(CL))
-        cp(Mt[:, :, 1], Mt[:, :, 0], ["q%d" % c], ["qq%d" % c], 64)
+        if Q_ENG == "v":
+            cp(Mt[:, :, 1], Mt[:, :, 0], ["q%d" % c], ["qq%d" % c], 64)
+        elif Q_ENG == "s":
+            op("s", lambda: S.activation(Mt[:, :, 1], Mt[:, :, 0], ACT.Copy), ["q%d" % c], ["qq%d" % c], (), vc(CL))
+        else:
+            op("g", lambda: g.affine_select(Mt[:, :, 1], Mt[:, :, 0], [[0, CL]], ALU.is_ge, 0.0, 0, 0), ["q%d" % c], ["qq%d" % c], (), 170 + 2 * CL * CYC)
         qk = ["q%d" % c, "qq%d" % c]
-        thr = KT[:, 0:KW:17]
-        keys = []
+        vks = ["V%d_%d" % (c, j) for j in range(4)]
+        lo = 0
+        for eng, n in PIECES.get((c, k), PIECES[None]):
+            gather(eng, Vt[:, 512 * lo:512 * (lo + n)], XW.indirect(B("c16", c)[:, 32 * lo:32 * (lo + n)]), XK + ["c16%d" % c], vks[lo:lo + n], 512 * n, big=eng == "s")
+            lo += n
         mm([(KT[:, 68 * h:68 * h + 68], T["G%d" % h][:, 16 - 16 * (gp - h):144 - 16 * (gp - h)], B("ct", c)[:, :, gp, :], 68) for h in range(2) for gp in range(2)],
-           ["G0", "G1", "ct%d" % c, "cz%d" % c], [kt + "c"], [kt], grp, f32=True)
-        for p in range(NP):
-            vk, mk = "V%d_%d" % (c, p), "M%d_%d" % (c, p)
-            lo, hi = PC * p, PC * p + PC
-            vks = [vk + "a", vk + "b"]
-            if SPLIT[p]:
-                for j in range(2):
-                    gather("s", Vt[:, 1024 * p + 512 * j:1024 * p + 512 * j + 512], XW.indirect(B("c16", c)[:, lo + 32 * j:lo + 32 * j + 32]),
-                           XK + ["c16%d" % c], [vks[j]], 8 * PC, True)
-            else:
-                gather("s", Vt[:, 1024 * p:1024 * p + 1024], XW.indirect(B("c16", c)[:, lo:hi]), XK + ["c16%d" % c], vks, 16 * PC, True)
+           ["G0", "G1", "ct%d" % c, "cz%d" % c], [kt + "c"], [kt], grp)
+        mm([(KT[:, 0:KW:17], T.NI[:], T.TH[:, t, k, :], CW)], ["NI", "TH%d" % t, kt + "c"], [kt + "t"], [kt], grp)
+        for p in range(2):
             ab = (c, k, p) in ABS
-            mks = [mk + "_%d%d" % (j, ab) for j in range(2)]
+            mks = ["M%d_%d%d" % (c, 2 * p + j, ab) for j in range(2)]
             for j in range(2):
                 bn = "PB_%d" % (nbank[0] % NB)
                 nbank[0] += 1
-                bank, g2, a0, vo = T[bn], grp + "b%d%d" % (p, j), lo + 32 * j, 1024 * p + 512 * j
-                mq = ([(bank[:, :, a, :], (T.NQ if ab else T.I2)[:], Mt[:, a0:a0 + 32, 0:2], PC) for a in range(8)], ["NQ", "I2"] + qk)
-                mv = ([(bank[:], (T.ID if ab else T.NQ)[:], Vt[:, vo:vo + 512], 512)], ["ID", "NQ", vks[j]])
-                for lst, rd in ((mq, mv) if QFIRST else (mv, mq)):
-                    mm(lst, rd, [bn], [bn], g2)
+                bank, a0, vo, vk = T[bn], HC * p + 32 * j, 1024 * p + 512 * j, vks[2 * p + j]
+                mm([(bank[:, :, a, :], (T.NQ if ab else T.I2)[:], Mt[:, a0:a0 + 32, 0:2], 64) for a in range(8)], ["NQ", "I2"] + qk, [bn], [bn], grp + bn)
+                mm([(bank[:], (T.ID if ab else T.NQ)[:], Vt[:, vo:vo + 512], 512)], ["ID", "NQ", vk], [bn], [bn], grp + bn)
                 if ab:
                     op("s", lambda a0=a0, bank=bank: S.activation(Ma[:, a0:a0 + 32, 2:18], bank[:], ACT.Abs), [bn], [mks[j]], [bn], vc(512))
                 else:
-                    tt(Mt[:, a0:a0 + 32, 2:18], Vt[:, vo:vo + 512], bank[:], ALU.min, [vks[j], bn], [mks[j]], 512, x=[bn])
+                    tt(Mt[:, a0:a0 + 32, 2:18], Vt[:, vo:vo + 512], bank[:], ALU.min, [vk, bn], [mks[j]], 512, x=[bn])
             Z, Ms = (T.ZV, Ma) if ab else (T.ZM, Mt)
-            mm([(KT[:, 68 * p:68 * p + 68], Z[:, 15 - i:143 - i], Ms[:, lo + i:hi:16, 1:18], 68) for i in range(16)],
+            mm([(KT[:, 68 * p:68 * p + 68], Z[:, 15 - i:143 - i], Ms[:, HC * p + i:HC * p + HC:16, 1:18], 68) for i in range(16)],
                ["ZV", "ZM", "Mz%d" % c, kt + "c"] + mks + qk, [kt + "m%d" % p], [kt], grp)
-            keys.append(kt + "m%d" % p)
-        mm([(thr, T.NI[:], B("Fb", c)[:], CW)], ["NI", "Fb%d" % c, kt + "c"], [kt + "f"], [kt], grp)
-        scan(B("SK", c)[:], T.RS[:], KT[:, 0:KW], ALU.add, ALU.min, ["RS", kt + "c", kt + "f"] + keys, ["SK%d" % c], KW, x=[kt])
-        tt(A("r", c), B("SK", c)[:, 16::17], thr, ALU.subtract, ["SK%d" % c, kt + "f"], ["r%d" % c], x=[kt])
+        SK = B("SK", c)
+        scan(SK[:], T.RS[:], KT[:, 0:KW], ALU.add, ALU.min, ["RS"] + [kt + a for a in ("c", "t", "m0", "m1")], ["SK%d" % c], KW, x=[kt])
+        tt(A("r", c), SK[:, 16::17], SK[:, 0::17], ALU.subtract, ["SK%d" % c], ["r%d" % c])
         ts(A("c", c), A("r", c), W - 1, None, ALU.bitwise_and, None, ["r%d" % c], ["c%d" % c])
-        bk, Bk = ("BE%d_%d" % (c, k + 2), B("BE", c)[:, k + 2::6]) if k < K - 1 else ("u0%d" % c, B("u0", c)[:])
+        bk, Bk = "BE%d_%d" % (c, (k + 1) % 4), B("BE", c)[:, k + 1:k + 33:4]
         tt(Bk, A("c", c), A("r", c), ALU.max, ["c%d" % c, "r%d" % c], [bk])
-        yl_, yk = B("y16", c)[:, CW * k:CW * k + CW], "y16%d_%d" % (c, k)
-        ts(yl_, Bk, 4096.0, None, ALU.min, None, [bk], [yk])
-        ysrc = XW.indirect(yl_)
+        ts(A("y16", c), Bk, float(W), None, ALU.min, None, [bk], ["y16%d" % c])
+        ysrc = XW.indirect(A("y16", c))
         yo, yi_ = ("yb", "ya") if k % 2 == 0 else ("ya", "yb")
         if k == 0:
-            gather(Y0_ENG, B(yo, c)[:], ysrc, XK + [yk], [yo + str(c)], CL)
+            gather(Y0_ENG, B(yo, c)[:], ysrc, XK + ["y16%d" % c], [yo + str(c)], CL)
         else:
-            op("v", lambda: V.tensor_tensor(B(yo, c)[:], ysrc, B(yi_, c)[:], ALU.max), XK + [yk, yi_ + str(c)], [yo + str(c)], (), gc_(CL))
+            op("v", lambda: V.tensor_tensor(B(yo, c)[:], ysrc, B(yi_, c)[:], ALU.max), XK + ["y16%d" % c, yi_ + str(c)], [yo + str(c)], (), gc_(CL))
 
     def place(t, c):
-        KT, kt = B("KT", c), "KT%d" % c
-        so = KT[:, 256:256 + CW]
+        so, kt = B("KT", c)[:, 256:256 + CW], "KT%d" % c
         y = B("ya", c)
-        allk = [kt + a for a in ("s", "c", "f", "m0", "m1")]
-        mm([(so, T.ZW[:, 15 - i:143 - i], y[:, i:CL:16], CW) for i in range(16)], ["ZW", "ya%d" % c], allk, [kt], "s%d_%d" % (t, c))
-        cp(A("s1", c), so, [kt + "s"], ["s1%d" % c], x=[kt])
+        mm([(so, T.ZW[:, 15 - i:143 - i], y[:, i:CL:16], CW) for i in range(16)], ["ZW", "ya%d" % c],
+           [kt + a for a in ("s", "c", "t", "m0", "m1")], [kt], "s%d_%d" % (t, c))
+        cp(A("s1", c), so, [kt + "s"], ["s1%d" % c, kt + "c"], x=[kt])
         ts(A("s2", c), A("s1", c), 15, None, ALU.bitwise_and, None, ["s1%d" % c], ["s2%d" % c])
-        tt(B("s3", c)[:], A("s2", c), T.BASE[:], ALU.add, ["s2%d" % c, "BASE"], ["s3%d" % c])
-        ts(A("p16", c), B("s3", c)[:], c16_, None, ALU.add, None, ["s3%d" % c, "c16_"], ["p16%d" % c])
+        tt(A("s3", c), A("s2", c), T.BASE[:], ALU.add, ["s2%d" % c, "BASE"], ["s3%d" % c])
+        ts(A("p16", c), A("s3", c), c16_, None, ALU.add, None, ["s3%d" % c, "c16_"], ["p16%d" % c])
 
     def scatter(t, c):
-        if t == TV - 1 and c == 0:
-            buf, o, key = T.XO, 0, "XO"
-        else:
-            buf, o, key = X, 2048 * c, "X%d" % c
+        buf, o, key = XS[(t + 1) % 2], 2048 * c, "X%d_%d" % ((t + 1) % 2, c)
         op("v", lambda: V.tensor_copy(buf[:, o:o + 2048].indirect(A("p16", c)), B("ya", c)[:]), ["p16%d" % c, "ya%d" % c, key], [key], (), gc_(CL, CS))
         if t == TV - 1:
             dma("y", T.yx[:, 2048 * c:2048 * c + 2048], buf[:, o:o + 2048], [key], (), 1 << 19, 0.0 if c else 3500.0)
 
     def rewire_pre(t, c):
         L, J, kl, kj = state(t, c)
-        BE = B("BE", c)
-        be = ["BE%d_%d" % (c, s) for s in range(6)]
+        BE = B("BE", c)[:, 0:32]
+        be = ["BE%d_%d" % (c, s) for s in range(4)]
         n = lambda a: a + str(c)
-        w0k, w5k = ["w0%d_%d" % (c, k) for k in range(K)], ["w5%d_%d" % (c, k) for k in range(K)]
-        ts(B("LB", c)[:], BE[:], 4096.0, 8192.0, ALU.is_lt, ALU.mult, be, [n("LB")], 48)
-        scan(B("PP", c)[:], B("LB", c)[:], BE[:], ALU.add, ALU.min, be + [n("LB")], [n("PP")], 48)
-        scan(B("JJ", c)[:], B("LB", c)[:], T.IX[:], ALU.add, ALU.min, ["IX", n("LB")], [n("JJ")], 48)
-        for k in range(1, K):
-            ts(B("w0", c)[:, CW * k:CW * k + CW], B("PP", c)[:, k + 1::6], -2048.0, None, ALU.add, None, [n("PP")], [w0k[k]])
-            tt(B("w5", c)[:, CW * k:CW * k + CW], B("JJ", c)[:, k + 1::6], state(t, c, k)[1], ALU.subtract, [n("JJ")] + kj, [w5k[k]])
-        tt(B("w2", c)[:], B("w0", c)[:], B("D0", c)[:, 5::6], ALU.mult, w0k + ["D0%d_6" % c], [n("w2")], 64)
+        ts(B("LB", c)[:], BE, 4096.0, 8192.0, ALU.is_lt, ALU.mult, be, [n("LB")])
+        scan(B("PP", c)[:], B("LB", c)[:], BE, ALU.add, ALU.min, be + [n("LB")], [n("PP")], 32)
+        scan(B("JJ", c)[:], B("LB", c)[:], T.IX[:], ALU.add, ALU.min, ["IX", n("LB")], [n("JJ")], 32)
+        lin(PREP_ENG, B("w0", c)[:], B("PP", c)[:], 32.0, -65536.0, [n("PP")], [n("w0")])
+        tt(B("w2", c)[:], B("w0", c)[:], B("D0", c)[:, 13::16, :], ALU.mult, [n("w0"), n("D0") + "a", n("D0") + "b"], [n("w2")], 64)
         tt(B("w3", c)[:], B("w2", c)[:], B("K3", c)[:], ALU.add, [n("w2"), n("K3")], [n("w3")], 64)
-        ts(B("w4", c)[:], B("w3", c)[:], 5, W - 1, ALU.arith_shift_right, ALU.bitwise_and, [n("w3")], [n("w4")], 32)
+        ts(B("w4", c)[:], B("w3", c)[:], 5, W - 1, ALU.arith_shift_right, ALU.bitwise_and, [n("w3")], [n("w4")])
         tt(B("w1", c)[:], B("w4", c)[:], L, ALU.subtract, [n("w4")] + kl, [n("w1")], 64)
+        if t < TV - 1 and c in EARLY:
+            se, sk = B("se%d" % t, c)[:], "se%d_%d" % (t, c)
+            ts(A("s3", c), B("BE", c)[:, 1:33:4], 4096.0, None, ALU.is_ge, None, be, [n("s3")])
+            tt(se, A("s3", c), B("w1", c)[:, :, 0], ALU.mult, [n("s3"), n("w1")], [sk])
+            tt(se, se, B("st%d" % t, c)[:, 0, :, 0], ALU.add, [sk] + kl, [sk])
+            send(T.cores[(rank + 1) % NR], B("le%d" % t, c)[:], se, [sk], ["le%d_%d" % (t, c)])
 
     def rewire(t, c):
         L, J, kl, kj = state(t, c)
         n = lambda a: a + str(c)
-        w1k, w5k = [n("w1")], ["w5%d_%d" % (c, k) for k in range(K)]
-        D, dk = B("DD", c)[:], [n("DD")]
-        ts(D, B("y16", c)[:], 4096.0, None, ALU.is_ge, None, ["y16%d_%d" % (c, k) for k in range(K)], dk, 32)
-        tt(B("w2", c)[:], B("w1", c)[:], D, ALU.mult, w1k + dk, [n("w2")], 64)
-        tt(B("w6", c)[:], B("w5", c)[:], D, ALU.mult, w5k + dk, [n("w6")], 64)
+        BE, be = B("BE", c)[:, 1:33], ["BE%d_%d" % (c, s) for s in range(4)]
+        sb, sk = B("snd%d" % t, c), "snd%d_%d" % (t, c)
+        ts(B("DD", c)[:], BE, 4096.0, None, ALU.is_ge, None, be, [n("DD")])
+        tt(B("w2", c)[:], B("w1", c)[:], B("DD", c)[:], ALU.mult, [n("w1"), n("DD")], [n("w2")], 64)
+        tt(sb[:, 0], B("w2", c)[:], L, ALU.add, [n("w2")] + kl, [sk + "a"], 64)
+        tt(B("w5", c)[:], BE, J, ALU.max, be + kj, [n("w5")], 64)
+        tt(sb[:, 1], B("w5", c)[:], B("JJ", c)[:], ALU.min, [n("w5"), n("JJ")], [sk + "b"], 64)
         if t < TV - 1:
-            sb, sk = B("snd%d" % t, c), "snd%d_%d" % (t, c)
-            tt(sb[:, 0], B("w2", c)[:], L, ALU.add, [n("w2")] + kl, [sk + "a"], 64)
-            tt(sb[:, 1], B("w6", c)[:], J, ALU.add, [n("w6")] + kj, [sk + "b"], 64)
-            send(T.cores[(rank + 1) % NR], B("lnd%d" % t, c)[:], sb[:], [sk + "a", sk + "b"], ["lnd%d_%d" % (t, c)])
+            send(T.cores[(rank + 1) % NR], B("st%d" % (t + 1), c)[:], sb[:], [sk + "a", sk + "b"], ["st%d_%d" % (t + 1, c)])
         else:
-            tt(T.OUT[:, 0, :, CW * c:CW * c + CW], B("w2", c)[:], L, ALU.add, [n("w2")] + kl, ["OUT%d" % c], 64)
-            tt(T.OUT[:, 1, :, CW * c:CW * c + CW], B("w6", c)[:], J, ALU.add, [n("w6")] + kj, ["OUJ%d" % c], 64)
+            lin("s", sb[:, 1], sb[:, 1], 1.0, -float(W), [sk + "b"], [sk + "b"])
+            for k in range(K):
+                lin("sv"[k % 2], T.OUT[:, :, k, CW * c:CW * c + CW], sb[:, :, :, k], 1.0, 0.0, [sk + "a", sk + "b"], ["OUT%d_%d" % (c, k)])
 
     for t in range(TV):
+        XW, XK = XS[t % 2][:], ["X%d_0" % (t % 2), "X%d_1" % (t % 2), "XZ"]
         for c in range(NCH):
             prep(t, c)
-        if t == TV - 1:
-            dma("y", T.XO[:], X[:, 0:W // 2], ["X0"], ["XO"], 1 << 19)
+        dma("y", XS[(t + 1) % 2][:, 0:W], XS[t % 2][:, 0:W], XK + ["FA"] + state(t, 1)[2], ["X%d_0" % ((t + 1) % 2), "X%d_1" % ((t + 1) % 2)], 1 << 20)
         for k in range(K):
             for c in range(NCH):
                 chain(t, c, k)
@@ -377,8 +397,8 @@ def build_ops(g, core, T, topo):
             cp(T.cni[:, 0:1], T.cnt[:, 0:1], ["cn0"], ["cn1"])
             ts(T.cni[:, 1:2], T.cni[:, 0:1], 31, None, ALU.bitwise_and, None, ["cn1"], ["cn2"])
             cp(T.cnt[:, 1:2], T.cni[:, 1:2], ["cn2"], ["cn3"])
-            ts(T.tha[:, 4 * t + 4:4 * t + 8], T.thf[:], T.cnt[:, 1:2], 241.0, ALU.add, ALU.min, ["thf", "cn3"], ["tha%d" % (t + 1)])
-    send(T.cores[(rank - (TV - 1)) % NR], T.FIN[:], T.OUT[:], ["OUT0", "OUT1", "OUJ0", "OUJ1"], ["FIN"])
+            ts(T.TH[:, t + 1], T.thf[:], T.cnt[:, 1:2], 240.0, ALU.add, ALU.min, thk + ["cn3"], ["TH%d" % (t + 1)])
+    send(T.cores[(rank - (TV - 1)) % NR], T.FIN[:], T.OUT[:], ["OUT%d_%d" % (c, k) for c in range(NCH) for k in range(K)], ["FIN"])
     dma("y", T.yl[:], T.FIN[:, 0], ["FIN"], (), 32768)
     dma("s", T.yi[:], T.FIN[:, 1], ["FIN"], (), 32768)
     return ops, nload
@@ -459,8 +479,7 @@ def schedule(ops, nload):
     def topo_order(key, back):
         nb, left = (pred if back else succ), [len(succ[i] if back else pred[i]) for i in range(n)]
         rank_ = sorted(range(n), key=lambda i: key[i])
-        placed, seq = [False] * n, []
-        waiting = {}
+        seq, waiting = [], {}
         for i in rank_:
             stack = [i] if left[i] == 0 else []
             if left[i]:
@@ -504,18 +523,97 @@ def schedule(ops, nload):
         val = float(np.sum(WGT * ln / base))
         if best is None or val < best[0]:
             best = (val, seq, st, dur, ln)
-        elif r % 2 == 1 or r > CFG["free"]:
+        elif r % 2 == 1:
             st, dur = best[2], best[3]
-        lo = rnd() * max(st)
-        hi = lo + CFG["win"]
-        jit = [CFG["jit"] * rnd() * (1.0 if lo <= st[i] <= hi else 0.02) for i in range(n)]
-        if r > CFG["free"] and r % 3:
-            key = [st[i] + jit[i] for i in range(n)]
-            continue
-        bs, dur = pack(topo_order([-(st[i] + dur[i]) + jit[i] for i in range(n)], True), True, m)
+        bs, dur = pack(topo_order([-(st[i] + dur[i]) + CFG["jit"] * rnd() for i in range(n)], True), True, m)
         key = [-(bs[i] + dur[i]) for i in range(n)]
-    ORDER["len"] = best[4]
-    return best[1]
+    ms_ = CFG["models"]
+    qn = {e: a for a, e in enumerate(sorted(set(eng)))}
+    q = [qn[e] for e in eng]
+    dur = [[float(o["c"][m]) for o in ops] for m in ms_]
+    lag = [[float(o["l"][m] + LAT[m]) for o in ops] for m in ms_]
+    wp = [[j for j, kind in pred[i] if kind == 1] for i in range(n)]
+    ap = [[j for j, kind in pred[i]] for i in range(n)]
+    sp = [[j for j, kind in succ[i]] for i in range(n)]
+
+    marks = [i for i in range(n) if ops[i]["big"]]
+
+    def run(seq, lo=0, old=None):
+        out, tot = [], 0.0
+        for a in range(len(ms_)):
+            d, l, free = dur[a], lag[a], [0.0] * len(qn)
+            st, fin = (old[a][0][:], old[a][1][:]) if old else ([0.0] * n, [0.0] * n)
+            for i in seq[max(lo - 60, 0):lo] if lo > 60 and len({q[i] for i in seq[lo - 60:lo]}) == len(qn) else seq[:lo]:
+                free[q[i]] = st[i] + d[i]
+            for i in seq[lo:]:
+                t = free[q[i]]
+                for j in wp[i]:
+                    if fin[j] > t:
+                        t = fin[j]
+                st[i] = t
+                t += d[i]
+                free[q[i]] = t
+                fin[i] = t + l[i]
+            out.append((st, fin))
+            tot += float(WGT[ms_[a]] / base[ms_[a]]) * (max(fin) + CFG["eps"] * sum([fin[i] for i in marks]) / len(marks))
+        return tot, out
+
+    def move(seq, pos, a, b, early):
+        lo, hi = pos[a], pos[b]
+        take, stack = {b if early else a}, [b if early else a]
+        while stack:
+            for j in (ap if early else sp)[stack.pop()]:
+                if lo <= pos[j] <= hi and j not in take:
+                    if j == a or j == b:
+                        return None
+                    take.add(j)
+                    stack.append(j)
+        x = [i for i in seq[lo:hi + 1] if i in take]
+        y = [i for i in seq[lo:hi + 1] if i not in take]
+        return seq[:lo] + (x + y if early else y + x) + seq[hi + 1:]
+
+    seq = best[1]
+    val, out = run(seq)
+    top, fresh = (val, seq), True
+    for r in range(CFG["swaps"]):
+        if fresh:
+            pos, prev, nxt_, lastq = [0] * n, [-1] * n, [-1] * n, {}
+            for a, i in enumerate(seq):
+                pos[i] = a
+                if q[i] in lastq:
+                    prev[i] = lastq[q[i]]
+                    nxt_[prev[i]] = i
+                lastq[q[i]] = i
+            arcs = []
+            for a in range(len(ms_)):
+                st, fin = out[a]
+                i = max(range(n), key=lambda i: fin[i])
+                while st[i] > 0:
+                    j = prev[i]
+                    if j >= 0 and st[j] + dur[a][j] >= st[i] - 1e-6:
+                        arcs.append((j, i))
+                    else:
+                        j = max(wp[i], key=lambda j: fin[j])
+                    i = j
+            fresh = False
+        a, b = arcs[int(rnd() * len(arcs))]
+        early = rnd() < 0.5
+        while rnd() < 0.5:
+            if early and prev[a] >= 0:
+                a = prev[a]
+            if not early and nxt_[b] >= 0:
+                b = nxt_[b]
+        new = move(seq, pos, a, b, early)
+        if new is None:
+            continue
+        v2, o2 = run(new, pos[a], out)
+        if v2 <= val + CFG["temp"] * (1.0 - r / CFG["swaps"]) * -np.log(rnd() + 1e-12):
+            st, at = o2[0][0], {i: a for a, i in enumerate(new)}
+            seq, val, out, fresh = sorted(new, key=lambda i: (st[i], at[i])), v2, o2, True
+            if val < top[0]:
+                top = (val, seq)
+    ORDER["len"] = length(top[1])
+    return top[1]
 
 
 def rank_program(g, core, T, topo):
@@ -577,7 +675,7 @@ def rank_program(g, core, T, topo):
         if o["e"] == "p":
             gp, lst = o["grp"], o["fn"]
             for a, m in enumerate(lst):
-                ins = q.matmul(m[0], m[1], m[2], gp is None or (first[gp] == i and a == 0), gp is None or ((last[gp] == i or "stop" in o) and a == len(lst) - 1))
+                ins = q.matmul(m[0], m[1], m[2], gp is None or (first[gp] == i and a == 0), gp is None or (last[gp] == i and a == len(lst) - 1))
         else:
             ins = o["fn"]()
         if i in need:

@@ -7,30 +7,36 @@ NCH, CW = 2, 8
 CL = 16 * CW
 HC = CL // 2
 NENG = 8
-KM = 69632.0
+KM = 65536.0
+CEN = 1928.0 * 4096
+JO = 3072
+BE_ENG = "g"
 BIG = 1073741824.0
 MAGIC = 25769803776.0
 KW = 17 * CW
 NB = 5
 PIECES = {None: (("s", 2), ("s", 1), ("s", 1)), (0, 0): (("s", 1), ("v", 1), ("s", 1), ("s", 1))}
 ABS = [(1, 3, 1)]
-EARLY = (0,)
+TSPLIT = 2
+C_CALLS = (2, 2)
 Q_ENG = "g"
-XL_ENG = ("vs", "ss")
-Y0_ENG = "s"
-PREP_ENG = "s"
-CYC = 0.83 * np.array([1.25, 1.1, 1.4, 1.25, 1.25])
-CG = np.array([1.56, 1.2, 1.9, 1.56, 1.56])
-CS = np.array([3.8, 2.5, 5.0, 3.8, 3.8])
-PE = 0.5 * CYC * np.array([1.1, 1.0, 1.0, 1.0, 1.3])
-FIX = np.array([10.0, 0.0, 0.0, 30.0, 0.0])
-LAT = np.array([70.0, 60.0, 60.0, 100.0, 40.0])
+XL_CALLS = (("v", 1), ("s", 1), ("s", 2), ("s", 2), ("s", 2))
+Y0_ENG = "ss"
+OUT_ENG = ("ggggs", "vvsgv")
+PREP_ENG = "v"
+CYC = 0.83 * np.array([1.0, 1.25, 1.45, 1.4, 1.1])
+CG = np.array([1.56, 1.56, 1.35, 1.8, 1.9])
+CS = np.array([3.8, 3.8, 3.8, 3.8, 3.8])
+PE = 0.5 * CYC
+SFX = np.array([280.0, 280.0, 280.0, 280.0, 280.0])
+FIX = np.array([0.0, 0.0, 0.0, 0.0, 0.0])
+LAT = np.array([155.0, 155.0, 155.0, 130.0, 200.0])
 REM = np.array([3000.0, 1500.0, 3500.0, 3000.0, 2000.0])
 ISS = np.array([400.0, 100.0, 600.0, 300.0, 100.0])
 DFX = np.array([800.0, 800.0, 1800.0, 1000.0, 1200.0])
 DBW = np.array([400.0, 350.0, 180.0, 350.0, 250.0])
-WGT = np.array([2.0, 0.5, 2.0, 0.5, 0.5])
-CFG = {"rounds": 80, "jit": 30.0, "seed": 1, "swaps": 25000, "temp": 0.0005, "models": (0, 2), "eps": 0.1}
+WGT = np.array([1.0, 1.0, 1.0, 1.0, 1.0])
+CFG = {"rounds": 80, "jit": 30.0, "seed": 1, "swaps": 40000, "temp": 0.0005, "models": (0, 2, 3), "eps": 0.1, "jump": 0.7}
 ORDER = {}
 
 SCRATCH = {
@@ -45,34 +51,38 @@ SCRATCH = {
     "ID": ("sbuf", [128, 128], "bfloat16"), "NQ": ("sbuf", [128, 128], "bfloat16"), "I2": ("sbuf", [128, 128], "bfloat16"),
     "ZV": ("sbuf", [128, 144], "bfloat16"), "ZM": ("sbuf", [128, 144], "bfloat16"), "ZW": ("sbuf", [128, 144], "bfloat16"),
     "G0": ("sbuf", [128, 160], "float16"), "G1": ("sbuf", [128, 160], "float16"),
-    "RS": ("sbuf", [128, KW], "float32"), "IX": ("sbuf", [128, 4 * CW], "float32"), "KC": ("sbuf", [128, CW, 4], "float32"),
+    "RS": ("sbuf", [128, KW], "float32"), "IX": ("sbuf", [128, 64], "float32"), "KC": ("sbuf", [128, 16, 4], "float32"),
     "BASE": ("sbuf", [128, CW], "float32"),
     "OUT": ("sbuf", [128, 2, 4, 16], "float32"), "FIN": ("sbuf", [128, 2, 4, 16], "float32"),
     "cnt": ("sbuf", [128, 4], "float32"), "cni": ("sbuf", [128, 4], "int32"),
 }
+for _n, _s, _d in (
+    ("XL", [4 * 256], "bfloat16"), ("L16", [64], "uint16"), ("exf", [16], "float32"), ("ed", [16], "float32"),
+    ("BE", [68], "float32"), ("MK", [64, 4], "float32"), ("D0", [256, 5], "float32"), ("D1", [256, 5], "float32"),
+    ("IY", [16, 4], "float32"), ("PZ", [32], "float32"),
+    ("se0", [16], "float32"), ("se1", [16], "float32"), ("le1", [16], "float32"), ("le2", [16], "float32"),
+    ("LB", [64], "float32"), ("DD", [64], "bfloat16"), ("PP", [64], "float32"), ("JJ", [64], "float32"),
+    ("K3", [16, 4], "float32"), ("w0", [64], "float32"), ("w1", [16, 4], "float32"), ("w2", [16, 4], "float32"),
+    ("w3", [64], "int32"), ("w4", [64], "int32"), ("w5", [64], "float32"), ("w7", [16, 4], "float32"),
+    ("st0", [2, 16, 4], "float32"), ("st1", [2, 16, 4], "float32"), ("st2", [2, 16, 4], "float32"),
+    ("snd0", [2, 16, 4], "float32"), ("snd1", [2, 16, 4], "float32"), ("snd2", [2, 16, 4], "float32"),
+):
+    SCRATCH[_n] = ("sbuf", [128] + _s, _d)
 for _c in range(NCH):
     for _n, _s, _d in (
-        ("V", [16 * CL], "bfloat16"), ("M", [CL, 18], "bfloat16"), ("Ma", [CL, 18], "bfloat16"), ("XL", [4 * CL], "bfloat16"),
+        ("V", [16 * CL], "bfloat16"), ("M", [CL, 18], "bfloat16"), ("Ma", [CL, 18], "bfloat16"),
         ("ya", [CL], "bfloat16"), ("yb", [CL], "bfloat16"),
         ("c16", [CL], "uint16"), ("cf", [4, 2, 16], "float16"), ("ct", [4, 2, 17], "float16"), ("SK", [KW], "float32"),
-        ("BE", [4 * CW + 4], "float32"), ("MK", [4 * CW, 4], "float32"), ("D0", [16 * CW, 4], "float32"), ("D1", [16 * CW, 4], "float32"),
-        ("se0", [CW], "float32"), ("se1", [CW], "float32"), ("le0", [CW], "float32"), ("le1", [CW], "float32"),
-        ("SN", [32 * CW], "float32"), ("si", [6 * CW], "int32"), ("so", [4 * CW], "uint16"), ("L16", [4 * CW], "uint16"),
-        ("sf", [3 * CW], "float32"),
-        ("LB", [4 * CW], "float32"), ("DD", [CW, 4], "bfloat16"), ("PP", [4 * CW], "float32"), ("JJ", [4 * CW], "float32"),
-        ("K3", [CW, 4], "float32"), ("w0", [CW, 4], "float32"), ("w1", [CW, 4], "float32"), ("w2", [CW, 4], "float32"),
-        ("w3", [CW, 4], "int32"), ("w4", [CW, 4], "int32"), ("w5", [CW, 4], "float32"), ("w7", [CW, 4], "float32"),
-        ("st0", [2, CW, 4], "float32"), ("st1", [2, CW, 4], "float32"), ("st2", [2, CW, 4], "float32"),
-        ("snd0", [2, CW, 4], "float32"), ("snd1", [2, CW, 4], "float32"), ("snd2", [2, CW, 4], "float32"),
+        ("SN", [32 * CW], "float32"), ("SE", [16 * CW], "float32"), ("si", [2 * CW], "int32"), ("so", [7 * CW], "uint16"), ("sf", [5 * CW], "float32"),
     ):
         SCRATCH["%s_%d" % (_n, _c)] = ("sbuf", [128] + _s, _d)
     SCRATCH["KT_%d" % _c] = ("psum", [128, 512], "float32")
 for _p in range(NB):
     SCRATCH["PB_%d" % _p] = ("psum", [128, 32, 8, 2], "float32")
 SCRATCH["MS"] = ("psum", [128, 512], "float32")
-SI = {"r": 0, "c": 1, "s1": 2, "s2": 3}
-SO = {"b16": 0, "n16": 1, "p16": 2, "y16": 3}
-SF = {"s3": 0, "ex": 1}
+SI = {"s1": 0, "s2": 1}
+SO = {"b16": 0, "n16": 1, "p16": 2, "y0": 3, "y1": 4, "y2": 5, "y3": 6}
+SF = {"s3": 0, "pre": 1}
 
 SEMAPHORES = ["sv", "ss", "sp", "sg", "sent"] + ["d%d" % _i for _i in range(28)]
 ESEM = {"v": "sv", "s": "ss", "p": "sp", "g": "sg"}
@@ -100,9 +110,9 @@ def build_ops(g, core, T, topo):
         if eng == "v":
             ts(out, in0, a, b, ALU.mult, ALU.add, r, w, n)
         elif eng == "g":
-            op("g", lambda: g.affine_select(out, in0, [[0, CW]], ALU.is_ge, 0.0, 0, 0), r, w, (), 170 + 2 * CW * CYC)
+            op("g", lambda: g.affine_select(out, in0, [[0, n]], ALU.is_ge, 0.0, 0, 0), r, w, (), 170 + 2 * n * CYC)
         else:
-            op("s", lambda: S.activation(out, in0, ACT.Identity, b, a), r, w, (), vc(n))
+            op("s", lambda: S.activation(out, in0, ACT.Identity, b, a), r, w, (), vc(n) + SFX)
 
     def tt(out, a, b, o, r, w, n=16, x=()):
         op("v", lambda: V.tensor_tensor(out, a, b, o), r, w, x, vc(n))
@@ -167,8 +177,8 @@ def build_ops(g, core, T, topo):
     op("g", lambda: g.iota(T.pci[:, 0:1], [[1, 1]], 0, 1), (), ["pc0"], (), 150)
     iota(T.IO[:], [[1, 160]], -16, ["IO"], 450)
     iota(T.E8i[0:8, :], [[1, 8], [0, 16]], 0, ["E8i"], 400)
-    iota(T.KC[:], [[0, CW], [32, 4]], 65536 - 4194304, ["KC"], 200)
-    iota(T.IX[:], [[0, CW], [1, 4]], W - 1, ["IX"], 200)
+    iota(T.KC[:], [[0, 16], [32, 4]], 65536 - 4194304, ["KC"], 270)
+    iota(T.IX[:], [[0, 16], [1, 4]], JO - 1, ["IX"], 270)
     iota(T.BASE[:], [[256, CW]], 0, ["BASE"], 150)
     col = T.col
     cP, cG, cH1, cH0, c16_, cW = (col[:, j:j + 1] for j in range(6))
@@ -199,7 +209,7 @@ def build_ops(g, core, T, topo):
         ms(X[:, W:W + 16], 0.0, ["XZ"])
         ms(X[:, W + 1:W + 2], 31.0, ["XZ"])
     cp(T.LJ[:, 0], T.lci[:], ["lci"], ["LJ0"])
-    ts(T.LJ[:, 1], T.upi[:], float(W), None, ALU.add, None, ["upi"], ["LJ1"])
+    ts(T.LJ[:, 1], T.upi[:], float(JO), None, ALU.add, None, ["upi"], ["LJ1"])
     ts(T.E8[0:8, :], T.E8i[0:8, :], col[0:8, 0:1], None, ALU.is_equal, None, ["E8i", "cP"], ["E8"], 128)
     ts(T.thb[0:8, :], T.thi[0:8, :], -1.0, None, ALU.add, None, ["thi"], ["thb"])
     mm([(MS[:, 0:4], T.E8[0:8, :], T.thb[0:8, :], 4)], ["E8", "thb"], ["MS"], ["MS"], None)
@@ -207,66 +217,84 @@ def build_ops(g, core, T, topo):
         ts(T.thf[:, k, :], T.IO[:, 0:CW], 0.0, MS[:, k:k + 1], ALU.mult, ALU.add, ["MS", "IO"], ["thf%d" % k], x=["MS"])
     thk = ["thf%d" % k for k in range(K)]
     ts(T.TH[:, 0], T.thf[:], 240.0, None, ALU.min, None, thk, ["TH0"])
+    D0, D1, BE, MK = T.D0, T.D1, T.BE, T.MK
+    bek = ["BE%d_%d" % (c, s) for c in range(NCH) for s in range(4)]
+    for k in range(K):
+        lin("sv"[k % 2], T.st0[:, :, :, k], T.LJ[:, :, k, :], 1.0, 0.0, ["LJ0", "LJ1"], ["st0_%d" % k])
+    ts(T.exf[:], T.exi[:], -1024.0, None, ALU.add, None, ["exi"], ["exf"])
+    iota(BE[:], [[0, 68]], 0, bek, 280)
+    iota(MK[:], [[0, 256]], 0, ["MK0", "MK1", "MK2"], 600)
+    iota(T.IY[:], [[0, 16], [1, 4]], JO - 1, ["IY"], 270)
+    ms(T.PZ[:], 1.0, ["PZ"])
+    ms(T.PZ[:, 0::4], 0.0, ["PZ"])
+    d1k = lambda c, k: ["D1%d_%d_%d" % (c, k, s) for s in range(4)]
+    ms(D0[:, 0:128], 1.0, ["D0x"], 640)
+    lin("s", D1[:, 0:128], D0[:, 0:128], 0.0, 0.0, ["D0x"], ["D1x"], 640)
+    ms(D0[:, 128:256], 1.0, ["D0y"], 640)
+    iota(D1[:, 128:256], [[0, 640]], 0, ["D1y"], 1460)
+    op("v", lambda: V.memset(D0[:, 0::16, :], 0.0), ["D0y"], ["D0x", "D0a", "D0b", "D0c", "D0m"], (), vc(80))
+    op("v", lambda: V.memset(D1[:, 1::16, :], CEN - 2047.5), ["D1x", "D1y"], ["D1c", "D1a", "D1b"] + [a for c in range(NCH) for k in range(K + 1) for a in d1k(c, k)], (), vc(80))
+    for s, val in ((4, -1.0), (8, 1.0 / 8192), (11, 8192.0)):
+        ms(D0[:, s::16, :], val, ["D0c"], 80)
+    ms(D0[:, 12::16, 0], 0.0, ["D0c"])
+    for s, val in ((2, 2 * MAGIC), (3, -2 * MAGIC), (5, CEN), (11, -1024.0), (14, MAGIC), (15, -MAGIC)):
+        ms(D1[:, s::16, :], val, ["D1c"], 80)
+    lin("v", D1[:, 12::16, 0], T.exf[:], 1.0, 0.0, ["exf"], d1k(0, 0) + d1k(1, 0))
     for c in range(NCH):
-        ex = T.exi[:, CW * c:CW * c + CW]
-        D0, D1 = B("D0", c), B("D1", c)
-        for k in range(K):
-            lin("sv"[k % 2], B("st0", c)[:, :, :, k], T.LJ[:, :, k, CW * c:CW * c + CW], 1.0, 0.0, ["LJ0", "LJ1"], ["st0_%d_%d" % (c, k)])
-        cp(A("ex", c), ex, ["exi"], ["ex%d" % c])
-        iota(B("BE", c)[:], [[0, 4 * CW + 4]], 0, ["BE%d_%d" % (c, s) for s in range(4)], 210)
-        k0 = ["D0%da" % c, "D0%db" % c, "D0c%d" % c]
-        k1 = ["D1c%d" % c, "D1k%da" % c, "D1k%db" % c] + ["D1%d_%d" % (c, k) for k in range(K)]
-        ms(D0[:], 1.0, k0, 512)
-        lin("s", D1[:], D0[:], 0.0, 0.0, k0, k1, 512)
-        ms(D0[:, 0::16, :], 0.0, ["D0c%d" % c])
-        ms(D1[:, 1::16, :], -1024.0, ["D1c%d" % c])
-        ms(D1[:, 14::16, :], MAGIC, ["D1c%d" % c])
-        ms(D1[:, 15::16, :], -MAGIC, ["D1c%d" % c])
-        cp(D1[:, 0::16, 0], ex, ["exi"], ["D1%d_0" % c])
         iota(B("Ma", c)[:, :, 1], [[0, CL]], 0, ["Mz%d" % c], 400)
-        ts(B("ct", c)[:, :, :, 0], T.IO[:, 0:CW], 0.0, -2048.0, ALU.mult, ALU.add, ["IO"], ["cz%d" % c])
+        ts(B("ct", c)[:, :, :, 0], T.IO[:, 0:CW], 0.0, 2048.0, ALU.mult, ALU.add, ["IO"], ["cz%d" % c])
 
     nbank = [0]
 
-    def state(t, c):
-        a = B("st%d" % t, c)
-        if t == 0:
-            return a[:, 0], a[:, 1], ["st0_%d_%d" % (c, k) for k in range(K)], ["st0_%d_%d" % (c, k) for k in range(K)]
-        return a[:, 0], a[:, 1], ["st%d_%d" % (t, c)], ["st%d_%d" % (t, c)]
+    def state(t):
+        return T["st%d" % t], ["st0_%d" % k for k in range(K)] if t == 0 else ["st%d" % t]
 
-    def prep(t, c):
-        L, J, kl, kj = state(t, c)
-        st = B("st%d" % t, c)
-        L0, k0 = (B("le%d" % (t - 1), c)[:], ["le%d_%d" % (t - 1, c)]) if t and c in EARLY else (st[:, 0, :, 0], kl)
-        if t and c in EARLY:
-            parts = ((slice(0, 1), L0, k0, ["a"]), (slice(1, K), st[:, 0, :, 1:K], kl, ["b"]))
-        else:
-            parts = ((slice(0, K), L, kl, ["a", "b"]),)
-        for rows, src, ks, ab in parts:
-            lin(PREP_ENG, B("D0", c)[:, 13::16, rows], src, 1.0 / 32, 37.0, ks, ["D0%d%s" % (c, a) for a in ab])
-            lin(PREP_ENG, B("D1", c)[:, 13::16, rows], src, 33.0, float(77 * t + 37 * 1024 - 80 * F - 1024), ks, ["D1k%d%s" % (c, a) for a in ab])
-        lin("g", B("BE", c)[:, 0:32:4], A("ex", c), 1.0, 0.0, ["ex%d" % c], ["BE%d_0" % c])
-        for s in range(4):
-            ts(B("MK", c)[:, s::4, :], J, float(W - 1 + s), None, ALU.is_equal, None, kj, ["MK%d_%d" % (c, s)])
+    def prep(t):
+        st, ks = state(t)
+        L0, k0 = (T["le%d" % t][:], ["le%d" % t]) if t else (st[:, 0, :, 0], ks[:1])
+        for rows, src, kk, a in ((slice(0, 1), L0, k0, "a"), (slice(1, K), st[:, 0, :, 1:K], ks, "b")):
+            lin(PREP_ENG, D0[:, 13::16, rows], src,  1.0 / 32, 37.0, kk, ["D0" + a])
+            lin(PREP_ENG, D1[:, 13::16, rows], src, 33.0, float(77 * t + 37 * 1024 - 80 * F - 1024), kk, ["D1" + a])
+        lin("g", BE[:, 0:64:4], T.exf[:], 1.0, 0.0, ["exf"], ["BE0_0", "BE1_0"], 16)
+        tt(D0[:, 12::16, 1:K], st[:, 1, :, 1:K], T.IY[:, :, 1:K], ALU.is_equal, ks + ["IY"], ["D0m"], 96)
+        for s in range(3):
+            ts(MK[:, s::4, s + 1:K], st[:, 1, :, s + 1:K], float(JO - 1 + s), None, ALU.is_equal, None, ks, ["MK%d" % s])
         for k in range(K):
-            cp(B("L16", c)[:, CW * k:CW * k + CW], st[:, 0, :, k] if k else L0, kl if k else k0, ["L16%d_%d" % (c, k)])
-        lin(PREP_ENG, B("w7", c)[:], L, 2048.0, 0.0, kl, ["w7%d" % c])
-        tt(B("K3", c)[:], B("w7", c)[:], T.KC[:], ALU.add, ["w7%d" % c, "KC"], ["K3%d" % c], 64)
-        gather(XL_ENG[c][0], B("XL", c)[:, 0:CL], XW.indirect(B("L16", c)[:, 0:CW]), XK + ["L16%d_0" % c], ["XL%d_0" % c], CL)
-        gather(XL_ENG[c][1], B("XL", c)[:, CL:4 * CL], XW.indirect(B("L16", c)[:, CW:4 * CW]), XK + ["L16%d_%d" % (c, k) for k in range(1, K)], ["XL%d_1" % c], 3 * CL)
+            cp(T.L16[:, 16 * k:16 * k + 16], st[:, 0, :, k] if k else L0, ks if k else k0, ["L16_%d" % k])
+        lin(PREP_ENG, T.w7[:], st[:, 0], 2048.0, 0.0, ks, ["w7"])
+        tt(T.K3[:], T.w7[:], T.KC[:], ALU.add, ["w7", "KC"], ["K3"], 128)
+        lo = 0
+        for eng, n in XL_CALLS:
+            gather(eng, T.XL[:, CL * lo:CL * (lo + n)], XW.indirect(T.L16[:, CW * lo:CW * (lo + n)]),
+                   XK + ["L16_%d" % (j // 2) for j in range(lo, lo + n)], ["XL%d" % j for j in range(lo, lo + n)], CL * n)
+            lo += n
 
     def chain(t, c, k):
-        SN, D1 = B("SN", c), B("D1", c)
+        SN, sn = (B("SN", c), "SN%d" % c) if k < K else (B("SE", c), "SE%d" % c)
+        scan(SN[:, 0:128], D0[:, CL * c:CL * c + CL, k], D1[:, CL * c:CL * c + CL, k], ALU.mult, ALU.add,
+             ["D0c", "D1c"] + d1k(c, k) + ([] if k == K else ["D0b", "D1b", "D0m"] if k else ["D0a", "D1a"]), [sn], 128)
         if k:
-            tt(D1[:, 0::4, k], B("BE", c)[:, 0:32], B("MK", c)[:, :, k], ALU.mult,
-               ["BE%d_%d" % (c, s) for s in range(4)] + ["MK%d_%d" % (c, s) for s in range(4)], ["D1%d_%d" % (c, k)], 64)
-        scan(SN[:, 0:128], B("D0", c)[:, :, k], D1[:, :, k], ALU.mult, ALU.add,
-             ["D0%d%s" % (c, "ab"[k > 0]), "D0c%d" % c, "D1c%d" % c, "D1k%d%s" % (c, "ab"[k > 0]), "D1%d_%d" % (c, k)], ["SN%d" % c], 128)
+            lin(BE_ENG if k < K else "v", BE[:, 32 * c + k:32 * c + k + 32:4], SN[:, 11:128:16], 1.0, 0.0, [sn],
+                ["BE%d_%d" % (c, k % 4)] + (["BE1_0"] if (c, k) == (0, K) else []), CW)
+            yk, yl_ = "y16%d_%d" % (c, k - 1), A("y%d" % (k - 1), c)
+            ts(yl_, SN[:, 8:128:16], 8192.0, float(W), ALU.mult, ALU.min, [sn], [yk])
+            ysrc = XW.indirect(yl_)
+            yo, yi_ = ("yb", "ya") if k % 2 else ("ya", "yb")
+            if k == 1:
+                gather(Y0_ENG[c], B(yo, c)[:], ysrc, XK + [yk], [yo + str(c)], CL)
+            else:
+                op("v", lambda: V.tensor_tensor(B(yo, c)[:], ysrc, B(yi_, c)[:], ALU.max), XK + [yk, yi_ + str(c)], [yo + str(c)], (), gc_(CL))
+        if k == K:
+            return
         tt(SN[:, 140::16], SN[:, 13:128:16], SN[:, 15:128:16], ALU.subtract, ["SN%d" % c], ["w%d" % c])
         ts(B("so", c)[:, 0:2 * CW], SN[:, 12::16], 1024.0 - 31.0 / 64, float(W + 1), ALU.add, ALU.min, ["SN%d" % c, "w%d" % c], ["n16%d" % c, "b16%d" % c])
-        gather("v", B("c16", c)[:], T.FA[:].indirect(A("n16", c)), ["FA", "FB", "n16%d" % c], ["c16%d" % c], CL)
+        lo = 0
+        for n in C_CALLS:
+            gather("v", B("c16", c)[:, 32 * lo:32 * (lo + n)], T.FA[:].indirect(A("n16", c, 2 * lo, 2 * (lo + n))), ["FA", "FB", "n16%d" % c],
+                   ["c16%d_%d" % (c, j) for j in range(lo, lo + n)], 32 * n)
+            lo += n
         for h in range(2):
-            ts(B("cf", c)[:, :, h, :], B("c16", c)[:, HC * h:HC * h + HC], -2048.0, None, ALU.add, None, ["c16%d" % c], ["cf%d_%d" % (c, h)])
+            ts(B("cf", c)[:, :, h, :], B("c16", c)[:, HC * h:HC * h + HC], -2048.0, None, ALU.add, None, ["c16%d_%d" % (c, 2 * h), "c16%d_%d" % (c, 2 * h + 1)], ["cf%d_%d" % (c, h)])
         op("v", lambda: V.transpose(B("ct", c)[:, :, :, 1:17], B("cf", c)[:]), ["cf%d_0" % c, "cf%d_1" % c], ["ct%d" % c], (), vc(64))
 
     def row(t, c, k):
@@ -274,8 +302,8 @@ def build_ops(g, core, T, topo):
         Vt, Mt, Ma = B("V", c), B("M", c), B("Ma", c)
         ok = "b16%d" % c
         qsrc = XW.indirect(A("b16", c))
-        op("v", lambda: V.tensor_tensor(Mt[:, :, 0], qsrc, B("XL", c)[:, CL * k:CL * k + CL], ALU.max),
-           XK + [ok, "XL%d_%d" % (c, min(k, 1))], ["q%d" % c], (), gc_(CL))
+        op("v", lambda: V.tensor_tensor(Mt[:, :, 0], qsrc, T.XL[:, CL * (2 * k + c):CL * (2 * k + c + 1)], ALU.max),
+           XK + [ok, "XL%d" % (2 * k + c)], ["q%d" % c], (), gc_(CL))
         if Q_ENG == "v":
             cp(Mt[:, :, 1], Mt[:, :, 0], ["q%d" % c], ["qq%d" % c], 64)
         elif Q_ENG == "s":
@@ -286,7 +314,7 @@ def build_ops(g, core, T, topo):
         vks = ["V%d_%d" % (c, j) for j in range(4)]
         lo = 0
         for eng, n in PIECES.get((c, k), PIECES[None]):
-            gather(eng, Vt[:, 512 * lo:512 * (lo + n)], XW.indirect(B("c16", c)[:, 32 * lo:32 * (lo + n)]), XK + ["c16%d" % c], vks[lo:lo + n], 512 * n, big=eng == "s")
+            gather(eng, Vt[:, 512 * lo:512 * (lo + n)], XW.indirect(B("c16", c)[:, 32 * lo:32 * (lo + n)]), XK + ["c16%d_%d" % (c, j) for j in range(lo, lo + n)], vks[lo:lo + n], 512 * n, big=eng == "s")
             lo += n
         mm([(KT[:, 68 * h:68 * h + 68], T["G%d" % h][:, 16 - 16 * (gp - h):144 - 16 * (gp - h)], B("ct", c)[:, :, gp, :], 68) for h in range(2) for gp in range(2)],
            ["G0", "G1", "ct%d" % c, "cz%d" % c], [kt + "c"], [kt], grp)
@@ -301,25 +329,22 @@ def build_ops(g, core, T, topo):
                 mm([(bank[:, :, a, :], (T.NQ if ab else T.I2)[:], Mt[:, a0:a0 + 32, 0:2], 64) for a in range(8)], ["NQ", "I2"] + qk, [bn], [bn], grp + bn)
                 mm([(bank[:], (T.ID if ab else T.NQ)[:], Vt[:, vo:vo + 512], 512)], ["ID", "NQ", vk], [bn], [bn], grp + bn)
                 if ab:
-                    op("s", lambda a0=a0, bank=bank: S.activation(Ma[:, a0:a0 + 32, 2:18], bank[:], ACT.Abs), [bn], [mks[j]], [bn], vc(512))
+                    op("s", lambda a0=a0, bank=bank: S.activation(Ma[:, a0:a0 + 32, 2:18], bank[:], ACT.Abs), [bn], [mks[j]], [bn], vc(512) + SFX)
                 else:
-                    tt(Mt[:, a0:a0 + 32, 2:18], Vt[:, vo:vo + 512], bank[:], ALU.min, [vk, bn], [mks[j]], 512, x=[bn])
+                    e = 32 // TSPLIT
+                    for a in range(TSPLIT):
+                        tt(Mt[:, a0 + e * a:a0 + e * a + e, 2:18], Vt[:, vo + 16 * e * a:vo + 16 * e * (a + 1)], bank[:, e * a:e * a + e], ALU.min,
+                           [vk, bn], [mks[j] + "_%d" % a], 16 * e, x=[bn])
             Z, Ms = (T.ZV, Ma) if ab else (T.ZM, Mt)
             mm([(KT[:, 68 * p:68 * p + 68], Z[:, 15 - i:143 - i], Ms[:, HC * p + i:HC * p + HC:16, 1:18], 68) for i in range(16)],
-               ["ZV", "ZM", "Mz%d" % c, kt + "c"] + mks + qk, [kt + "m%d" % p], [kt], grp)
+               ["ZV", "ZM", "Mz%d" % c, kt + "c"] + (mks if ab else [m + "_%d" % a for m in mks for a in range(TSPLIT)]) + qk, [kt + "m%d" % p], [kt], grp)
+        if k < K - 1:
+            tt(A("pre", c, 0, 32), BE[:, 32 * c:32 * c + 32], MK[:, 32 * c:32 * c + 32, k + 1], ALU.mult, bek[4 * c:4 * c + 4] + ["MK0", "MK1", "MK2"], ["pre%d" % c], 64)
+            scan(D1[:, CL * c:CL * c + CL:4, k + 1], T.PZ[:], A("pre", c, 0, 32), ALU.mult, ALU.add, ["PZ", "pre%d" % c], d1k(c, k + 1), 32)
         SK = B("SK", c)
         scan(SK[:], T.RS[:], KT[:, 0:KW], ALU.add, ALU.min, ["RS"] + [kt + a for a in ("c", "t", "m0", "m1")], ["SK%d" % c], KW, x=[kt])
-        tt(A("r", c), SK[:, 16::17], SK[:, 0::17], ALU.subtract, ["SK%d" % c], ["r%d" % c])
-        ts(A("c", c), A("r", c), W - 1, None, ALU.bitwise_and, None, ["r%d" % c], ["c%d" % c])
-        bk, Bk = "BE%d_%d" % (c, (k + 1) % 4), B("BE", c)[:, k + 1:k + 33:4]
-        tt(Bk, A("c", c), A("r", c), ALU.max, ["c%d" % c, "r%d" % c], [bk])
-        ts(A("y16", c), Bk, float(W), None, ALU.min, None, [bk], ["y16%d" % c])
-        ysrc = XW.indirect(A("y16", c))
-        yo, yi_ = ("yb", "ya") if k % 2 == 0 else ("ya", "yb")
-        if k == 0:
-            gather(Y0_ENG, B(yo, c)[:], ysrc, XK + ["y16%d" % c], [yo + str(c)], CL)
-        else:
-            op("v", lambda: V.tensor_tensor(B(yo, c)[:], ysrc, B(yi_, c)[:], ALU.max), XK + ["y16%d" % c, yi_ + str(c)], [yo + str(c)], (), gc_(CL))
+        for s, o in enumerate((ALU.subtract, ALU.subtract, ALU.is_ge)):
+            tt(D1[:, CL * c + 4 * s:CL * c + CL:16, k + 1], SK[:, 16::17], SK[:, 0::17], o, ["SK%d" % c], d1k(c, k + 1)[s:s + 1])
 
     def place(t, c):
         so, kt = B("KT", c)[:, 256:256 + CW], "KT%d" % c
@@ -337,67 +362,66 @@ def build_ops(g, core, T, topo):
         if t == TV - 1:
             dma("y", T.yx[:, 2048 * c:2048 * c + 2048], buf[:, o:o + 2048], [key], (), 1 << 19, 0.0 if c else 3500.0)
 
-    def rewire_pre(t, c):
-        L, J, kl, kj = state(t, c)
-        BE = B("BE", c)[:, 0:32]
-        be = ["BE%d_%d" % (c, s) for s in range(4)]
-        n = lambda a: a + str(c)
-        ts(B("LB", c)[:], BE, 4096.0, 8192.0, ALU.is_lt, ALU.mult, be, [n("LB")])
-        scan(B("PP", c)[:], B("LB", c)[:], BE, ALU.add, ALU.min, be + [n("LB")], [n("PP")], 32)
-        scan(B("JJ", c)[:], B("LB", c)[:], T.IX[:], ALU.add, ALU.min, ["IX", n("LB")], [n("JJ")], 32)
-        lin(PREP_ENG, B("w0", c)[:], B("PP", c)[:], 32.0, -65536.0, [n("PP")], [n("w0")])
-        tt(B("w2", c)[:], B("w0", c)[:], B("D0", c)[:, 13::16, :], ALU.mult, [n("w0"), n("D0") + "a", n("D0") + "b"], [n("w2")], 64)
-        tt(B("w3", c)[:], B("w2", c)[:], B("K3", c)[:], ALU.add, [n("w2"), n("K3")], [n("w3")], 64)
-        ts(B("w4", c)[:], B("w3", c)[:], 5, W - 1, ALU.arith_shift_right, ALU.bitwise_and, [n("w3")], [n("w4")])
-        tt(B("w1", c)[:], B("w4", c)[:], L, ALU.subtract, [n("w4")] + kl, [n("w1")], 64)
-        if t < TV - 1 and c in EARLY:
-            se, sk = B("se%d" % t, c)[:], "se%d_%d" % (t, c)
-            ts(A("s3", c), B("BE", c)[:, 1:33:4], 4096.0, None, ALU.is_ge, None, be, [n("s3")])
-            tt(se, A("s3", c), B("w1", c)[:, :, 0], ALU.mult, [n("s3"), n("w1")], [sk])
-            tt(se, se, B("st%d" % t, c)[:, 0, :, 0], ALU.add, [sk] + kl, [sk])
-            send(T.cores[(rank + 1) % NR], B("le%d" % t, c)[:], se, [sk], ["le%d_%d" % (t, c)])
-
-    def rewire(t, c):
-        L, J, kl, kj = state(t, c)
-        n = lambda a: a + str(c)
-        BE, be = B("BE", c)[:, 1:33], ["BE%d_%d" % (c, s) for s in range(4)]
-        sb, sk = B("snd%d" % t, c), "snd%d_%d" % (t, c)
-        ts(B("DD", c)[:], BE, 4096.0, None, ALU.is_ge, None, be, [n("DD")])
-        tt(B("w2", c)[:], B("w1", c)[:], B("DD", c)[:], ALU.mult, [n("w1"), n("DD")], [n("w2")], 64)
-        tt(sb[:, 0], B("w2", c)[:], L, ALU.add, [n("w2")] + kl, [sk + "a"], 64)
-        tt(B("w5", c)[:], BE, J, ALU.max, be + kj, [n("w5")], 64)
-        tt(sb[:, 1], B("w5", c)[:], B("JJ", c)[:], ALU.min, [n("w5"), n("JJ")], [sk + "b"], 64)
+    def rewire_pre(t):
+        st, ks = state(t)
+        ts(T.LB[:], BE[:, 0:64], float(JO), 8192.0, ALU.is_lt, ALU.mult, bek, ["LB"])
+        scan(T.PP[:], T.LB[:], BE[:, 0:64], ALU.add, ALU.min, bek + ["LB"], ["PP"], 64)
+        scan(T.JJ[:], T.LB[:], T.IX[:], ALU.add, ALU.min, ["IX", "LB"], ["JJ"], 64)
+        lin(PREP_ENG, T.w0[:], T.PP[:], 32.0, -32768.0, ["PP"], ["w0"])
+        tt(T.w2[:], T.w0[:], D0[:, 13::16, 0:K], ALU.mult, ["w0", "D0a", "D0b"], ["w20", "w21"], 128)
+        tt(T.w3[:], T.w2[:], T.K3[:], ALU.add, ["w20", "w21", "K3"], ["w3"], 128)
+        ts(T.w4[:], T.w3[:], 5, W - 1, ALU.arith_shift_right, ALU.bitwise_and, ["w3"], ["w4"])
+        tt(T.w1[:], T.w4[:], st[:, 0], ALU.subtract, ["w4"] + ks, ["w1"], 128)
         if t < TV - 1:
-            send(T.cores[(rank + 1) % NR], B("st%d" % (t + 1), c)[:], sb[:], [sk + "a", sk + "b"], ["st%d_%d" % (t + 1, c)])
+            se, sk = T["se%d" % t][:], "se%d" % t
+            ts(T.ed[:], BE[:, 1:65:4], float(JO), None, ALU.is_ge, None, ["BE0_1", "BE1_1"], ["ed"])
+            tt(se, T.ed[:], T.w1[:, :, 0], ALU.mult, ["ed", "w1"], [sk])
+            tt(se, se, st[:, 0, :, 0], ALU.add, [sk] + ks, [sk])
+            send(T.cores[(rank + 1) % NR], T["le%d" % (t + 1)][:], se, [sk], ["le%d" % (t + 1)])
+
+    def rewire(t, cs):
+        st, ks = state(t)
+        lo, hi = CW * cs[0], CW * cs[-1] + CW
+        n = lambda a: [a + str(c) for c in cs]
+        Bs, be, sb = BE[:, 4 * lo + 1:4 * hi + 1], bek[lo // 2:hi // 2] + ["BE1_0"], T["snd%d" % t]
+        ts(T.DD[:, 4 * lo:4 * hi], Bs, float(JO), None, ALU.is_ge, None, be, n("DD"))
+        tt(T.w2[:, lo:hi], T.w1[:, lo:hi], T.DD[:, 4 * lo:4 * hi], ALU.mult, ["w1"] + n("DD"), n("w2"), 8 * (hi - lo))
+        tt(sb[:, 0, lo:hi], T.w2[:, lo:hi], st[:, 0, lo:hi], ALU.add, n("w2") + ks, n("sa%d" % t), 8 * (hi - lo))
+        tt(T.w5[:, 4 * lo:4 * hi], Bs, st[:, 1, lo:hi], ALU.max, be + ks, n("w5"), 8 * (hi - lo))
+        tt(sb[:, 1, lo:hi], T.w5[:, 4 * lo:4 * hi], T.JJ[:, 4 * lo:4 * hi], ALU.min, n("w5") + ["JJ"], n("sb%d" % t), 8 * (hi - lo))
+        if t < TV - 1:
+            send(T.cores[(rank + 1) % NR], T["st%d" % (t + 1)][:], sb[:], n("sa%d" % t) + n("sb%d" % t), ["st%d" % (t + 1)])
         else:
-            lin("s", sb[:, 1], sb[:, 1], 1.0, -float(W), [sk + "b"], [sk + "b"])
+            lin(OUT_ENG[cs[0]][K], sb[:, 1, lo:hi], sb[:, 1, lo:hi], 1.0, -float(JO), n("sb%d" % t), n("sb%d" % t))
             for k in range(K):
-                lin("sv"[k % 2], T.OUT[:, :, k, CW * c:CW * c + CW], sb[:, :, :, k], 1.0, 0.0, [sk + "a", sk + "b"], ["OUT%d_%d" % (c, k)])
+                lin(OUT_ENG[cs[0]][k], T.OUT[:, :, k, lo:hi], sb[:, :, lo:hi, k], 1.0, 0.0, n("sa%d" % t) + n("sb%d" % t), ["OUT%d_%d" % (cs[0], k)], 16)
 
     for t in range(TV):
         XW, XK = XS[t % 2][:], ["X%d_0" % (t % 2), "X%d_1" % (t % 2), "XZ"]
-        for c in range(NCH):
-            prep(t, c)
-        dma("y", XS[(t + 1) % 2][:, 0:W], XS[t % 2][:, 0:W], XK + ["FA"] + state(t, 1)[2], ["X%d_0" % ((t + 1) % 2), "X%d_1" % ((t + 1) % 2)], 1 << 20)
+        prep(t)
+        dma("y", XS[(t + 1) % 2][:, 0:W], XS[t % 2][:, 0:W], XK + ["FA"] + state(t)[1], ["X%d_0" % ((t + 1) % 2), "X%d_1" % ((t + 1) % 2)], 1 << 20)
         for k in range(K):
             for c in range(NCH):
                 chain(t, c, k)
-                if k == K - 1:
-                    rewire_pre(t, c)
+            if k == K - 1:
+                rewire_pre(t)
+            for c in range(NCH):
                 row(t, c, k)
+                if k == K - 1:
+                    chain(t, c, K)
+                if k == K - 1 and t == TV - 1:
+                    rewire(t, [c])
+        if t < TV - 1:
+            rewire(t, range(NCH))
         for c in range(NCH):
             place(t, c)
-            rewire(t, c)
-        for c in range(NCH):
             scatter(t, c)
         if t < TV - 1:
-            mm([(MS[:, 0:32], T.ON[:], B("DD", c)[:], 32) for c in range(NCH)],
-               ["ON", "DD0", "DD1"], ["MS"], ["MS"], "d%d" % t)
-            op("v", lambda: V.tensor_reduce(T.cnt[:, 0:1], MS[:, 0:32], AxisListType.X, ALU.add), ["MS"], ["cn0"], ["MS"], vc(32))
-            cp(T.cni[:, 0:1], T.cnt[:, 0:1], ["cn0"], ["cn1"])
-            ts(T.cni[:, 1:2], T.cni[:, 0:1], 31, None, ALU.bitwise_and, None, ["cn1"], ["cn2"])
-            cp(T.cnt[:, 1:2], T.cni[:, 1:2], ["cn2"], ["cn3"])
-            ts(T.TH[:, t + 1], T.thf[:], T.cnt[:, 1:2], 240.0, ALU.add, ALU.min, thk + ["cn3"], ["TH%d" % (t + 1)])
+            mm([(MS[:, 0:64], T.ON[:], T.DD[:], 64)], ["ON", "DD0", "DD1"], ["MS"], ["MS"], None)
+            op("v", lambda: V.tensor_reduce(T.cnt[:, 0:1], MS[:, 0:64], AxisListType.X, ALU.add), ["MS"], ["cn0"], ["MS"], vc(64))
+            ts(T.cni[:, 0:1], T.cnt[:, 0:1], 1.0 / 32, -31.0 / 64, ALU.mult, ALU.add, ["cn0"], ["cn1"])
+            ts(T.cnt[:, 1:2], T.cni[:, 0:1], -32.0, T.cnt[:, 0:1], ALU.mult, ALU.add, ["cn0", "cn1"], ["cn2"])
+            ts(T.TH[:, t + 1], T.thf[:], T.cnt[:, 1:2], 240.0, ALU.add, ALU.min, thk + ["cn2"], ["TH%d" % (t + 1)])
     send(T.cores[(rank - (TV - 1)) % NR], T.FIN[:], T.OUT[:], ["OUT%d_%d" % (c, k) for c in range(NCH) for k in range(K)], ["FIN"])
     dma("y", T.yl[:], T.FIN[:, 0], ["FIN"], (), 32768)
     dma("s", T.yi[:], T.FIN[:, 1], ["FIN"], (), 32768)
@@ -598,7 +622,7 @@ def schedule(ops, nload):
             fresh = False
         a, b = arcs[int(rnd() * len(arcs))]
         early = rnd() < 0.5
-        while rnd() < 0.5:
+        while rnd() < CFG["jump"]:
             if early and prev[a] >= 0:
                 a = prev[a]
             if not early and nxt_[b] >= 0:

@@ -5,451 +5,557 @@ ALU, ACT = AluOpType, ActivationFunctionType
 W, F, K, TV, NR = 4096, 2048, 4, 3, 4
 NCH, CW = 2, 8
 CL = 16 * CW
-HC = CL // 2
 NENG = 8
 KM = 65536.0
 CEN = 1928.0 * 4096
 JO = 3072
-BE_ENG = "g"
+RAMP = 16384
 BIG = 1073741824.0
 MAGIC = 25769803776.0
-KW = 17 * CW
-NB = 5
-PIECES = {None: (("s", 2), ("s", 1), ("s", 1)), (0, 0): (("s", 1), ("v", 1), ("s", 1), ("s", 1))}
+ODD = 12582913.0
+KW = 17
+PIECES = {None: (("s", 2), ("s", 2), ("s", 2), ("s", 2)), (0, 0): (("s", 2), ("v", 2), ("s", 2), ("s", 2)), (1, 3): (("s", 4), ("s", 2), ("s", 2))}
 ABS = [(1, 3, 1)]
-TSPLIT = 2
-C_CALLS = (2, 2)
-Q_ENG = "g"
-XL_CALLS = (("v", 1), ("s", 1), ("s", 2), ("s", 2), ("s", 2))
-Y0_ENG = "ss"
-OUT_ENG = ("ggggs", "vvsgv")
-PREP_ENG = "v"
-CYC = 0.83 * np.array([1.0, 1.25, 1.45, 1.4, 1.1])
-CG = np.array([1.56, 1.56, 1.35, 1.8, 1.9])
+C_CALLS = (8,)
+NB = 5
+TSPLIT = (16,) * 12 + (8, 8, 8, 8)
+SUMS = ((0, 16), (0, 8, 16))
+XL_CALLS = (("v", 1), ("v", 1), ("v", 1), ("v", 1), ("s", 4))
+Y0_ENG = "s"
+Y_SCAN = ""
+AHEAD = 1
+ONE_CAST = False
+SINGLE_Q = 0
+KEY_V = 3
+Q_FIRST = 128
+V_FIRST = {None: 1}
+Q_ENG = "v"
+Y_AFTER = (None, (1, 2), (1, 2))
+L16_G = True
+CYC = 0.83 * np.array([1.0, 1.25, 1.4, 1.25, 1.1])
+CG = np.array([1.56, 1.56, 1.3, 1.9, 1.9])
 CS = np.array([3.8, 3.8, 3.8, 3.8, 3.8])
 PE = 0.5 * CYC
 SFX = np.array([280.0, 280.0, 280.0, 280.0, 280.0])
-FIX = np.array([0.0, 0.0, 0.0, 0.0, 0.0])
-LAT = np.array([155.0, 155.0, 155.0, 130.0, 200.0])
-REM = np.array([3000.0, 1500.0, 3500.0, 3000.0, 2000.0])
+FIX = np.array([4.0, 4.0, 4.0, 4.0, 4.0])
+LAT = np.array([205.0, 155.0, 170.0, 220.0, 200.0])
+REM = np.array([3900.0, 2000.0, 4500.0, 3900.0, 2600.0])
 ISS = np.array([400.0, 100.0, 600.0, 300.0, 100.0])
 DFX = np.array([800.0, 800.0, 1800.0, 1000.0, 1200.0])
 DBW = np.array([400.0, 350.0, 180.0, 350.0, 250.0])
 WGT = np.array([1.0, 1.0, 1.0, 1.0, 1.0])
-CFG = {"rounds": 80, "jit": 30.0, "seed": 1, "swaps": 40000, "temp": 0.0005, "models": (0, 2, 3), "eps": 0.1, "jump": 0.7}
+CFG = {"rounds": 2, "jit": 30.0, "seed": 1, "swaps": 400, "sweeps": (32, 0, 0, 0), "ends": 200, "asap": ("late", "count", "ahead"), "whole": 20000, "apart": (0, 1, 6, 7), "ending": {"y": 7.5, "early": 7.6, "finish": 8.0}, "pattern": 4000, "heat": 0.0003, "span": 100, "temp": 0.00015, "models": (0, 2, 3), "eps": 0.02, "near": 600.0, "jump": (0.5, 0.9)}
 ORDER = {}
-
-SCRATCH = {
-    "XA": ("sbuf", [128, W + 16], "bfloat16"), "XB": ("sbuf", [128, W + 16], "bfloat16"),
-    "FA": ("sbuf", [128, F + 8], "int32"), "LJ": ("sbuf", [128, 2, 4, 16], "float32"),
-    "lci": ("sbuf", [128, 4, 16], "int32"), "upi": ("sbuf", [128, 4, 16], "int32"), "exi": ("sbuf", [128, 16], "int32"),
-    "thi": ("sbuf", [128, 4], "int32"), "wti": ("sbuf", [128, 4], "int32"),
-    "thb": ("sbuf", [128, 4], "bfloat16"), "thf": ("sbuf", [128, 4, CW], "float32"), "TH": ("sbuf", [128, TV, 4, CW], "bfloat16"),
-    "IO": ("sbuf", [128, 160], "float32"), "pci": ("sbuf", [128, 4], "int32"), "col": ("sbuf", [128, 12], "float32"),
-    "E8": ("sbuf", [128, 128], "bfloat16"), "E8i": ("sbuf", [128, 128], "float32"),
-    "NI": ("sbuf", [128, 128], "bfloat16"), "ON": ("sbuf", [128, 128], "bfloat16"),
-    "ID": ("sbuf", [128, 128], "bfloat16"), "NQ": ("sbuf", [128, 128], "bfloat16"), "I2": ("sbuf", [128, 128], "bfloat16"),
-    "ZV": ("sbuf", [128, 144], "bfloat16"), "ZM": ("sbuf", [128, 144], "bfloat16"), "ZW": ("sbuf", [128, 144], "bfloat16"),
-    "G0": ("sbuf", [128, 160], "float16"), "G1": ("sbuf", [128, 160], "float16"),
-    "RS": ("sbuf", [128, KW], "float32"), "IX": ("sbuf", [128, 64], "float32"), "KC": ("sbuf", [128, 16, 4], "float32"),
-    "BASE": ("sbuf", [128, CW], "float32"),
-    "OUT": ("sbuf", [128, 2, 4, 16], "float32"), "FIN": ("sbuf", [128, 2, 4, 16], "float32"),
-    "cnt": ("sbuf", [128, 4], "float32"), "cni": ("sbuf", [128, 4], "int32"),
+PLAN = {
+    ("keys", "v", "D1"): (0.08, 0.09, 0.10), ("chain", "v", "SN"): (0.19, 0.28), ("chain", "v", "so"): (0.37,), ("chain", "v", "c1"): (0.45,),
+    ("chain", "g", "BR"): (0.25,), ("chain", "g", "BE"): (0.30,), ("chain", "g", "DD"): (0.35,),
+    ("chain", "v", "cf"): (0.95, 0.965), ("chain", "v", "ct"): (1.04,),
+    ("row", "v", "M_"): (0.80, 0.93, 1.15, 1.245, 1.33, 1.41, 1.54, 1.605, 1.67, 1.77, 1.70, 1.735),
+    ("row", "s", "V_"): (0.60, 0.82, 1.04, 1.26), ("row", "v", "V_"): (0.54,), ("row", "s", "Ma"): (1.40, 1.60),
+    ("row", "p", "PB"): (0.94, 1.008, 1.075, 1.14, 1.21, 1.30, 1.40, 1.50), ("row", "p", "KT"): (1.35, 1.36, 1.65, 1.797, 1.868), ("row", "v", "SK"): (2.0,),
 }
+
+SCRATCH = {}
 for _n, _s, _d in (
-    ("XL", [4 * 256], "bfloat16"), ("L16", [64], "uint16"), ("exf", [16], "float32"), ("ed", [16], "float32"),
-    ("BE", [68], "float32"), ("MK", [64, 4], "float32"), ("D0", [256, 5], "float32"), ("D1", [256, 5], "float32"),
-    ("IY", [16, 4], "float32"), ("PZ", [32], "float32"),
-    ("se0", [16], "float32"), ("se1", [16], "float32"), ("le1", [16], "float32"), ("le2", [16], "float32"),
-    ("LB", [64], "float32"), ("DD", [64], "bfloat16"), ("PP", [64], "float32"), ("JJ", [64], "float32"),
+    ("XA", [W + 16], "bfloat16"), ("XB", [W + 16], "bfloat16"), ("FA", [F + 8], "int32"),
+    ("LI", [2, 4, 16], "int32"), ("exi", [16], "int32"), ("thi", [4], "int32"), ("wti", [4], "int32"),
+    ("thb", [4], "bfloat16"), ("thf", [4, CW], "float32"), ("TH", [TV, 4, CW], "bfloat16"),
+    ("IO", [160], "float32"), ("pci", [4], "int32"), ("col", [12], "float32"),
+    ("E8", [128], "bfloat16"), ("E8i", [128], "float32"), ("NI", [128], "bfloat16"), ("NQ", [128], "bfloat16"), ("ON", [128], "bfloat16"), ("ID", [128], "bfloat16"),
+    ("ZI", [144], "bfloat16"), ("ZV", [144], "bfloat16"), ("ZM", [144], "bfloat16"), ("ZW", [144], "bfloat16"),
+    ("G0", [160], "float16"), ("G1", [160], "float16"),
+    ("RS", [CW * KW], "float32"), ("IX", [64], "float32"), ("KC", [16, 4], "float32"), ("NB", [CW], "float32"), ("IY", [16, 2], "float32"),
+    ("cnt", [4], "float32"), ("cni", [4], "int32"),
+    ("XL", [1024], "bfloat16"), ("L16", [64], "uint16"), ("I2", [128], "bfloat16"),
+    ("exf", [16], "float32"), ("BE", [68], "float32"), ("BR", [64], "float32"), ("MK", [64, 2], "float32"),
+    ("D0", [256, 5], "float32"), ("D1", [256, 5], "float32"), ("SE", [256], "float32"),
+    ("LB", [64], "float32"), ("DD", [16, 4], "bfloat16"), ("PP", [64], "float32"), ("JJ", [64], "float32"),
     ("K3", [16, 4], "float32"), ("w0", [64], "float32"), ("w1", [16, 4], "float32"), ("w2", [16, 4], "float32"),
-    ("w3", [64], "int32"), ("w4", [64], "int32"), ("w5", [64], "float32"), ("w7", [16, 4], "float32"),
+    ("w3", [64], "int32"), ("w4", [64], "int32"), ("w5", [16, 4], "float32"), ("w6", [2, 16], "float32"), ("w7", [16, 4], "float32"),
+    ("w8", [2, 16], "float32"), ("ex32", [16], "float32"), ("a0", [16], "float32"), ("a1", [16], "float32"), ("a2", [16], "int32"), ("a3", [16], "int32"),
+    ("se0", [16], "float32"), ("se1", [16], "float32"), ("le1", [16], "float32"), ("le2", [16], "float32"),
     ("st0", [2, 16, 4], "float32"), ("st1", [2, 16, 4], "float32"), ("st2", [2, 16, 4], "float32"),
     ("snd0", [2, 16, 4], "float32"), ("snd1", [2, 16, 4], "float32"), ("snd2", [2, 16, 4], "float32"),
+    ("lt1", [2, 16], "float32"), ("lt2", [2, 16], "float32"), ("lt3", [2, 16], "float32"),
+    ("sl0", [2, 16], "float32"), ("sl1", [2, 16], "float32"), ("sl2", [2, 16], "float32"),
+    ("OUT", [2, 3, 16], "float32"), ("FIN", [2, 3, 16], "float32"),
+    ("ya", [256], "bfloat16"), ("yb", [256], "bfloat16"), ("y16", [64], "uint16"), ("p16", [16], "uint16"),
+    ("yg", [768], "bfloat16"), ("ys", [768], "bfloat16"), ("yz", [768], "bfloat16"), ("pk", [16], "int32"), ("pf", [16], "float32"),
 ):
     SCRATCH[_n] = ("sbuf", [128] + _s, _d)
 for _c in range(NCH):
     for _n, _s, _d in (
-        ("V", [16 * CL], "bfloat16"), ("M", [CL, 18], "bfloat16"), ("Ma", [CL, 18], "bfloat16"),
-        ("ya", [CL], "bfloat16"), ("yb", [CL], "bfloat16"),
-        ("c16", [CL], "uint16"), ("cf", [4, 2, 16], "float16"), ("ct", [4, 2, 17], "float16"), ("SK", [KW], "float32"),
-        ("SN", [32 * CW], "float32"), ("SE", [16 * CW], "float32"), ("si", [2 * CW], "int32"), ("so", [7 * CW], "uint16"), ("sf", [5 * CW], "float32"),
+        ("V", [16 * CL], "bfloat16"), ("M", [CL, 18], "bfloat16"), ("Ma", [CL, 17], "bfloat16"), ("c16", [CL], "uint16"), ("cf", [4, 2, 16], "float16"),
+        ("ct", [4, 2, 17], "float16"), ("SK", [CW * KW], "float32"), ("SN", [2 * CL], "float32"), ("so", [2 * CW], "uint16"),
     ):
         SCRATCH["%s_%d" % (_n, _c)] = ("sbuf", [128] + _s, _d)
     SCRATCH["KT_%d" % _c] = ("psum", [128, 512], "float32")
 for _p in range(NB):
     SCRATCH["PB_%d" % _p] = ("psum", [128, 32, 8, 2], "float32")
 SCRATCH["MS"] = ("psum", [128, 512], "float32")
-SI = {"s1": 0, "s2": 1}
-SO = {"b16": 0, "n16": 1, "p16": 2, "y0": 3, "y1": 4, "y2": 5, "y3": 6}
-SF = {"s3": 0, "pre": 1}
 
-SEMAPHORES = ["sv", "ss", "sp", "sg", "sent"] + ["d%d" % _i for _i in range(28)]
+SEMAPHORES = ["sv", "ss", "sp", "sg", "sent"] + ["d%d" % _i for _i in range(32)]
 ESEM = {"v": "sv", "s": "ss", "p": "sp", "g": "sg"}
+ALL = slice(None)
+
+
+def sl(a, b, c=None):
+    return slice(a, b, c)
 
 
 def build_ops(g, core, T, topo):
     rank = T.rank_of(core)
     ops = []
     V, S = g.vector, g.scalar
+    tag = [(-1, "setup"), 0]
 
-    def op(eng, fn, r=(), w=(), x=(), cost=0.0, dma=None, grp=None, inc=16, big=False):
-        ops.append({"big": big, "e": eng, "fn": fn, "r": list(r), "w": list(w), "x": list(x), "c": cost + 0 * CG, "dma": dma is not None,
+    def do(fn, name, t, *a):
+        tag[0], tag[1] = (t, name) + a, 0
+        fn(t, *a)
+
+    def P(name, *idx, p=ALL):
+        shape = SCRATCH[name][1][1:]
+        bits = np.zeros(int(np.prod(shape)), np.uint8)
+        bits[np.arange(len(bits)).reshape(shape)[idx].reshape(-1)] = 1
+        return (T[name][(p,) + idx], [(name, int.from_bytes(np.packbits(bits).tobytes(), "big"))], int(bits.sum()))
+
+    def ind(win, off):
+        return (win[0].indirect(off[0]), win[1], 16 * off[2], off[1])
+
+    def ap(a):
+        return a[0] if isinstance(a, tuple) else a
+
+    def op(eng, fn, out, ins, cost, dma=None, grp=None, inc=16, big=False):
+        r, w = [], []
+        for a in ins:
+            if isinstance(a, tuple):
+                r += a[1] + (a[3] if len(a) > 3 else [])
+        for a in out:
+            if isinstance(a, tuple):
+                w += a[1]
+                r += a[3] if len(a) > 3 else []
+        x = sorted({n for n, _ in r + w if SCRATCH[n][0] == "psum"})
+        if eng == "v" and not [1 for a in list(out) + list(ins) if isinstance(a, tuple) and len(a) > 3]:
+            cost = cost + FIX
+        tag[1] += 1
+        ops.append({"tag": tag[0] + (tag[1] - 1,), "big": big, "e": eng, "fn": fn, "r": r, "w": w, "x": x, "c": cost + 0 * CG, "dma": dma is not None,
                     "l": (0.0 if dma is None else dma) + 0 * CG, "grp": grp, "inc": inc})
 
-    def vc(n):
-        return (max(64, n) + FIX) * CYC
+    def narrow(*a):
+        return all(SCRATCH[x[1][0][0]][2] in ("bfloat16", "float16", "uint16") for x in a)
 
-    def ts(out, in0, s1, s2, o0, o1, r, w, n=8, x=()):
+    def vc(out, *ins):
+        if len(out) > 3:
+            return 55 + out[2] * CS * CYC
+        if ins and len(ins[0]) > 3:
+            return 55 + out[2] * CG * CYC
+        return max(64, out[2] * (0.5 if narrow(out, *ins) else 1)) * CYC
+
+    def ts(out, in0, s1, s2, o0, o1=None):
         if o1 is None:
-            op("v", lambda: V.tensor_scalar(out, in0, s1, None, o0), r, w, x, vc(n))
+            op("v", lambda: V.tensor_scalar(out[0], in0[0], ap(s1), None, o0), [out], [in0, s1], vc(out, in0))
         else:
-            op("v", lambda: V.tensor_scalar(out, in0, s1, s2, o0, o1), r, w, x, vc(n))
+            op("v", lambda: V.tensor_scalar(out[0], in0[0], ap(s1), ap(s2), o0, o1), [out], [in0, s1, s2], vc(out, in0))
 
-    def lin(eng, out, in0, a, b, r, w, n=64):
+    def lin(eng, out, in0, a, b):
         if eng == "v":
-            ts(out, in0, a, b, ALU.mult, ALU.add, r, w, n)
-        elif eng == "g":
-            op("g", lambda: g.affine_select(out, in0, [[0, n]], ALU.is_ge, 0.0, 0, 0), r, w, (), 170 + 2 * n * CYC)
+            ts(out, in0, a, b, ALU.mult, ALU.add)
         else:
-            op("s", lambda: S.activation(out, in0, ACT.Identity, b, a), r, w, (), vc(n) + SFX)
+            op("s", lambda: S.activation(out[0], in0[0], ACT.Identity, b, ap(a)), [out], [in0, a], max(64, out[2]) * CYC + SFX)
 
-    def tt(out, a, b, o, r, w, n=16, x=()):
-        op("v", lambda: V.tensor_tensor(out, a, b, o), r, w, x, vc(n))
+    def gcp(out, in0):
+        op("g", lambda: g.affine_select(out[0], in0[0], [[0, out[2]]], ALU.is_ge, 0.0, 0, 0), [out], [in0], 170 + 2 * out[2] * CYC)
 
-    def cp(out, in_, r, w, n=8, x=()):
-        op("v", lambda: V.tensor_copy(out, in_), r, w, x, vc(n))
+    def tt(out, a, b, o):
+        two = len(a) == 3 and SCRATCH[a[1][0][0]][0] == SCRATCH[b[1][0][0]][0]
+        op("v", lambda: V.tensor_tensor(out[0], a[0], b[0], o), [out], [a, b], max(64, out[2] * (2 if two else 1)) * CYC if len(a) == 3 else vc(out, a))
 
-    def ms(ap, val, w, n=8):
-        op("v", lambda: V.memset(ap, val), (), w, (), vc(n))
+    def cp(out, in_):
+        op("v", lambda: V.tensor_copy(out[0], in_[0]), [out], [in_], vc(out, in_))
 
-    def scan(out, d0, d1, o0, o1, r, w, n, x=()):
-        op("v", lambda: V.tensor_tensor_scan(out, d0, d1, 0.0, o0, o1), r, w, x, vc(n))
+    def ms(out, val):
+        op("v", lambda: V.memset(out[0], val), [out], [], vc(out))
 
-    def gc_(n, c=None):
-        return 55 + n * (CG if c is None else c) * CYC
+    def scan(out, d0, d1, o0, o1):
+        op("v", lambda: V.tensor_tensor_scan(out[0], d0[0], d1[0], 0.0, o0, o1), [out], [d0, d1], vc(out, d0, d1))
 
-    def gather(eng, out, src, r, w, n, add=0.0, big=False):
-        if eng == "v" and add:
-            op("v", lambda: V.tensor_scalar(out, src, add, None, ALU.add), r, w, (), gc_(n), big=big)
-        elif eng == "v":
-            op("v", lambda: V.tensor_copy(out, src), r, w, (), gc_(n), big=big)
-        elif add:
-            op("s", lambda: S.activation(out, src, ACT.Identity, add), r, w, (), gc_(n) + 10, big=big)
+    def gather(eng, out, src, big=False):
+        if eng == "v":
+            op("v", lambda: V.tensor_copy(out[0], src[0]), [out], [src], vc(out, src), big=big)
         else:
-            op("s", lambda: S.activation(out, src, ACT.Copy), r, w, (), gc_(n) + 10, big=big)
+            op("s", lambda: S.activation(out[0], src[0], ACT.Copy), [out], [src], vc(out, src) + 10, big=big)
 
-    def mm(lst, r, w, x, grp):
-        op("p", lst, r, w, x, 10 + sum(max(64, a[3]) for a in lst) * PE, grp=grp)
+    def mm(lst, grp=None):
+        op("p", [(o[0], l[0], r[0]) for o, l, r in lst], [a[0] for a in lst], [a[j] for a in lst for j in (1, 2)],
+           10 + sum(max(64, a[2][2]) for a in lst) * PE, grp=grp)
 
-    def dma(eng, out, in_, r, w, nbytes, after=0.0):
+    def dma(eng, out, in_, nbytes, after=0.0, also=()):
         q = {"y": g.sync, "s": g.scalar}[eng]
-        op(eng, lambda: q.dma_start(out, in_), r, w, (), 60.0, dma=DFX + nbytes / DBW + after)
+        op(eng, lambda: q.dma_start(ap(out), ap(in_)), [out], [in_] + list(also), 60.0, dma=DFX + nbytes / DBW + after)
 
-    def iota(out, pat, base, w, cost, r=()):
-        op("g", lambda: g.iota(out, pat, base, 0, allow_small_or_imprecise_dtypes=True), r, w, (), cost)
+    def iota(out, pat, base, mult=0):
+        op("g", lambda: g.iota(out[0], pat, base, mult, allow_small_or_imprecise_dtypes=True), [out], [], 130 + 2 * out[2] * CYC)
 
-    def send(dst, out, in_, r, w):
+    def send(dst, out, in_, share=1.0):
         rid, pid = topo.addr(dst)[0], topo.addr(dst)[1]
         m = 0
         for e in topo.engines(core, dst)[:NENG]:
             m += 1 << e
-        op("g", lambda sem: g.remote_dma(out, in_, sem, T.sem.sent, pid, rid, m), r, w, (), ISS, dma=REM + (2000.0 if not [1 for o in ops if o["dma"] and o["e"] == "g"] else 0.0), inc=NENG)
+        first = not [1 for o in ops if o["dma"] and o["e"] == "g"]
+        op("g", lambda sem: g.remote_dma(out[0], in_[0], sem, T.sem.sent, pid, rid, m), [out], [in_], ISS * share, dma=REM * share + (2000.0 if first else 0.0), inc=NENG)
 
-    def B(n, c):
-        return T["%s_%d" % (n, c)]
+    def B(n, c, *idx):
+        return P("%s_%d" % (n, c), *idx)
 
-    def A(n, c, lo=0, hi=CW):
-        buf, tab = ("si", SI) if n in SI else ("so", SO) if n in SO else ("sf", SF)
-        return B(buf, c)[:, CW * tab[n] + lo:CW * tab[n] + hi]
-
-    MS = T.MS
-    XS = (T.XA, T.XB)
-    dma("y", T.lci[:], T.lc[:], (), ["lci"], 32768)
-    dma("s", T.exi[:], T.ex[:], (), ["exi"], 8192)
-    dma("y", T.upi[:], T.up[:], (), ["upi"], 32768)
-    dma("s", T.thi[0:8, :], T.th[:], (), ["thi"], 128)
-    dma("y", T.XA[:, 0:W], T.xs[:], (), ["X0_0", "X0_1"], 1 << 20)
-    dma("s", T.wti[:, 0:1], T.wt[:], (), ["wti"], 512)
-    dma("s", T.FA[:, F:F + 8], T.fa[:, 0:8], (), ["FB"], 4096)
-    dma("s", T.FA[:, 0:F], T.fa[:], (), ["FA"], 2 << 20)
+    XS = ("XA", "XB")
+    dma("y", P("LI", 0), T.lc[:], 32768)
+    dma("s", P("exi"), T.ex[:], 8192)
+    dma("y", P("LI", 1), T.up[:], 32768)
+    dma("s", P("thi", p=sl(0, 8)), T.th[:], 128)
+    dma("y", P("XA", sl(0, W)), T.xs[:], 1 << 20)
+    dma("s", P("wti", sl(0, 1)), T.wt[:], 512)
+    dma("s", P("FA", sl(F, F + 8)), T.fa[:, 0:8], 4096)
+    dma("s", P("FA", sl(0, F)), T.fa[:], 2 << 20)
     nload = len(ops)
-    op("g", lambda: g.iota(T.pci[:, 0:1], [[1, 1]], 0, 1), (), ["pc0"], (), 150)
-    iota(T.IO[:], [[1, 160]], -16, ["IO"], 450)
-    iota(T.E8i[0:8, :], [[1, 8], [0, 16]], 0, ["E8i"], 400)
-    iota(T.KC[:], [[0, 16], [32, 4]], 65536 - 4194304, ["KC"], 270)
-    iota(T.IX[:], [[0, 16], [1, 4]], JO - 1, ["IX"], 270)
-    iota(T.BASE[:], [[256, CW]], 0, ["BASE"], 150)
-    col = T.col
-    cP, cG, cH1, cH0, c16_, cW = (col[:, j:j + 1] for j in range(6))
-    cp(cP, T.pci[:, 0:1], ["pc0"], ["cP"])
-    ts(T.pci[:, 1:2], T.pci[:, 0:1], 4, None, ALU.arith_shift_right, None, ["pc0"], ["pc1"])
-    ts(T.pci[:, 2:3], T.pci[:, 0:1], 4, 1, ALU.arith_shift_right, ALU.bitwise_and, ["pc0"], ["pc2"])
-    ts(T.pci[:, 3:4], T.pci[:, 0:1], 15, None, ALU.bitwise_and, None, ["pc0"], ["pc3"])
-    cp(cG, T.pci[:, 1:2], ["pc1"], ["cG"])
-    cp(cH1, T.pci[:, 2:3], ["pc2"], ["cH1"])
-    ts(cH0, T.pci[:, 2:3], -1.0, 1.0, ALU.mult, ALU.add, ["pc2"], ["cH0"])
-    ts(c16_, T.pci[:, 3:4], 16.0, None, ALU.mult, None, ["pc3"], ["c16_"])
-    cp(cW, T.wti[:, 0:1], ["wti"], ["cW"])
-    ts(T.ID[:], T.IO[:, 16:144], cP, None, ALU.is_equal, None, ["IO", "cP"], ["ID"], 128)
-    for nm, sc in (("NQ", -1.0), ("I2", 2.0), ("NI", KM)):
-        lin("s", T[nm][:], T.ID[:], sc, 0.0, ["ID"], [nm], 128)
-    lin("s", T.ON[:], T.ID[:], 0.0, 1.0, ["ID"], ["ON"], 128)
-    ms(T.ZW[:], 0.0, ["ZW"], 72)
-    ts(T.ZW[:, 15:128:16], T.IO[:, 16:24], cG, None, ALU.is_equal, None, ["IO", "cG", "ZW"], ["ZW"])
-    lin("s", T.ZM[:], T.ZW[:], -KM, 0.0, ["ZW"], ["ZM"], 144)
-    lin("s", T.ZV[:], T.ZW[:], KM, 0.0, ["ZW"], ["ZV"], 144)
-    lin("s", T.ZW[:], T.ZW[:], cW, 0.0, ["ZW", "cW"], ["ZW"], 144)
-    ts(T.G0[:], T.IO[:], cP, cH0, ALU.is_equal, ALU.mult, ["IO", "cP", "cH0"], ["G0"], 160)
-    ts(T.G1[:], T.IO[:], cP, cH1, ALU.is_equal, ALU.mult, ["IO", "cP", "cH1"], ["G1"], 160)
-    iota(T.RS[:], [[0, KW]], -W, ["RS"], 420)
+    op("g", lambda: g.iota(T.pci[:, 0:1], [[1, 1]], 0, 1), [P("pci", sl(0, 1))], [], 150)
+    iota(P("IO"), [[1, 160]], -16)
+    iota(P("E8i", p=sl(0, 8)), [[1, 8], [0, 16]], 0)
+    cP, cG, cH1, cH0, c16_, cW = (P("col", sl(j, j + 1)) for j in range(6))
+    pc = [P("pci", sl(j, j + 1)) for j in range(4)]
+    cp(cP, pc[0])
+    ts(pc[1], pc[0], 4, None, ALU.arith_shift_right)
+    ts(pc[2], pc[0], 4, 1, ALU.arith_shift_right, ALU.bitwise_and)
+    ts(pc[3], pc[0], 15, None, ALU.bitwise_and)
+    cp(cG, pc[1])
+    cp(cH1, pc[2])
+    ts(cH0, pc[2], -1.0, 1.0, ALU.mult, ALU.add)
+    ts(c16_, pc[3], 16.0, None, ALU.mult)
+    ts(cW, P("wti", sl(0, 1)), 1.0 / 16, None, ALU.mult)
+    ts(P("ID"), P("IO", sl(16, 144)), cP, None, ALU.is_equal)
+    for n, a in (("NQ", -1.0), ("I2", 2.0), ("NI", KM)):
+        lin("s", P(n), P("ID"), a, 0.0)
+    iota(P("ON"), [[0, 128]], 1)
+    ms(P("ZI"), 0.0)
+    ts(P("ZI", sl(15, 128, 16)), P("IO", sl(16, 24)), cG, None, ALU.is_equal)
+    lin("s", P("ZV"), P("ZI"), KM, 0.0)
+    lin("s", P("ZM"), P("ZI"), -KM, 0.0)
+    lin("s", P("ZW"), P("ZI"), cW, 0.0)
+    ts(P("G0"), P("IO"), cP, cH0, ALU.is_equal, ALU.mult)
+    ts(P("G1"), P("IO"), cP, cH1, ALU.is_equal, ALU.mult)
+    iota(P("RS"), [[0, CW * KW]], -W)
     for j in range(2):
-        ms(T.RS[:, j::17], BIG, ["RS"])
+        ms(P("RS", sl(j, None, KW)), BIG)
     for X in XS:
-        ms(X[:, W:W + 16], 0.0, ["XZ"])
-        ms(X[:, W + 1:W + 2], 31.0, ["XZ"])
-    cp(T.LJ[:, 0], T.lci[:], ["lci"], ["LJ0"])
-    ts(T.LJ[:, 1], T.upi[:], float(JO), None, ALU.add, None, ["upi"], ["LJ1"])
-    ts(T.E8[0:8, :], T.E8i[0:8, :], col[0:8, 0:1], None, ALU.is_equal, None, ["E8i", "cP"], ["E8"], 128)
-    ts(T.thb[0:8, :], T.thi[0:8, :], -1.0, None, ALU.add, None, ["thi"], ["thb"])
-    mm([(MS[:, 0:4], T.E8[0:8, :], T.thb[0:8, :], 4)], ["E8", "thb"], ["MS"], ["MS"], None)
+        ms(P(X, sl(W, W + 16)), 0.0)
+        ms(P(X, sl(W + 1, W + 2)), 31.0)
     for k in range(K):
-        ts(T.thf[:, k, :], T.IO[:, 0:CW], 0.0, MS[:, k:k + 1], ALU.mult, ALU.add, ["MS", "IO"], ["thf%d" % k], x=["MS"])
-    thk = ["thf%d" % k for k in range(K)]
-    ts(T.TH[:, 0], T.thf[:], 240.0, None, ALU.min, None, thk, ["TH0"])
-    D0, D1, BE, MK = T.D0, T.D1, T.BE, T.MK
-    bek = ["BE%d_%d" % (c, s) for c in range(NCH) for s in range(4)]
+        cp(P("st0", ALL, ALL, k), P("LI", ALL, k))
+    ts(P("st0", 1), P("st0", 1), float(JO), None, ALU.add)
+    ts(P("E8", p=sl(0, 8)), P("E8i", p=sl(0, 8)), P("col", sl(0, 1), p=sl(0, 8)), None, ALU.is_equal)
+    ts(P("thb", p=sl(0, 8)), P("thi", p=sl(0, 8)), -1.0, None, ALU.add)
+    mm([(P("MS", sl(0, 4)), P("E8", p=sl(0, 8)), P("thb", p=sl(0, 8)))])
     for k in range(K):
-        lin("sv"[k % 2], T.st0[:, :, :, k], T.LJ[:, :, k, :], 1.0, 0.0, ["LJ0", "LJ1"], ["st0_%d" % k])
-    ts(T.exf[:], T.exi[:], -1024.0, None, ALU.add, None, ["exi"], ["exf"])
-    iota(BE[:], [[0, 68]], 0, bek, 280)
-    iota(MK[:], [[0, 256]], 0, ["MK0", "MK1", "MK2"], 600)
-    iota(T.IY[:], [[0, 16], [1, 4]], JO - 1, ["IY"], 270)
-    ms(T.PZ[:], 1.0, ["PZ"])
-    ms(T.PZ[:, 0::4], 0.0, ["PZ"])
-    d1k = lambda c, k: ["D1%d_%d_%d" % (c, k, s) for s in range(4)]
-    ms(D0[:, 0:128], 1.0, ["D0x"], 640)
-    lin("s", D1[:, 0:128], D0[:, 0:128], 0.0, 0.0, ["D0x"], ["D1x"], 640)
-    ms(D0[:, 128:256], 1.0, ["D0y"], 640)
-    iota(D1[:, 128:256], [[0, 640]], 0, ["D1y"], 1460)
-    op("v", lambda: V.memset(D0[:, 0::16, :], 0.0), ["D0y"], ["D0x", "D0a", "D0b", "D0c", "D0m"], (), vc(80))
-    op("v", lambda: V.memset(D1[:, 1::16, :], CEN - 2047.5), ["D1x", "D1y"], ["D1c", "D1a", "D1b"] + [a for c in range(NCH) for k in range(K + 1) for a in d1k(c, k)], (), vc(80))
-    for s, val in ((4, -1.0), (8, 1.0 / 8192), (11, 8192.0)):
-        ms(D0[:, s::16, :], val, ["D0c"], 80)
-    ms(D0[:, 12::16, 0], 0.0, ["D0c"])
-    for s, val in ((2, 2 * MAGIC), (3, -2 * MAGIC), (5, CEN), (11, -1024.0), (14, MAGIC), (15, -MAGIC)):
-        ms(D1[:, s::16, :], val, ["D1c"], 80)
-    lin("v", D1[:, 12::16, 0], T.exf[:], 1.0, 0.0, ["exf"], d1k(0, 0) + d1k(1, 0))
+        ts(P("thf", k), P("IO", sl(0, CW)), 0.0, P("MS", sl(k, k + 1)), ALU.mult, ALU.add)
+    ts(P("TH", 0), P("thf"), 240.0, None, ALU.min)
+    ts(P("exf"), P("exi"), -1024.0, None, ALU.add)
+    lin("v", P("ex32"), P("exi"), 32.0, -65536.0)
+    iota(P("BE"), [[0, 68]], 0)
+    for t in range(TV - 1):
+        iota(P("snd%d" % t, 0, ALL, 3), [[0, 16]], 0)
+    iota(P("BR"), [[0, 16], [RAMP, 4]], 0)
+    for n in ("BE", "BR"):
+        gcp(P(n, sl(0, 64, 4)), P("exf"))
+    iota(P("KC"), [[0, 16], [32, 4]], 65536 - 4194304)
+    iota(P("IX"), [[0, 16], [1, 4]], JO - 1)
+    iota(P("IY"), [[0, 16], [1, 2]], JO + 1)
+    ts(P("NB"), P("IO", sl(16, 16 + CW)), -16.0, -7.5 / 16, ALU.mult, ALU.add)
+    def step(s, c=None):
+        return sl(s, 2 * CL, 16) if c is None else sl(CL * c + s, CL * c + CL, 16)
+
+    ms(P("D0", sl(0, CL)), 1.0)
+    lin("s", P("D1", sl(0, CL)), P("D0", sl(0, CL)), 0.0, 0.0)
+    ms(P("D0", sl(CL, 2 * CL)), 1.0)
+    iota(P("D1", sl(CL, 2 * CL)), [[0, 640]], 0)
+    for s, val in ((0, 0.0), (1, 2.0 ** -25), (4, -8192.0), (8, -1.0)):
+        ms(P("D0", step(s)), val)
+    ms(P("D0", step(12), 0), 0.0)
+    for s, val in ((1, 0.5 - 2.0 ** -14), (2, ODD), (3, -ODD), (5, CEN - 4095.5), (6, 2 * MAGIC), (7, -2 * MAGIC), (14, MAGIC), (15, -MAGIC)):
+        ms(P("D1", step(s)), val)
+    iota(P("D1", step(9)), [[0, 16], [RAMP, 5]], int(CEN) - 3072)
+    iota(P("D1", step(10)), [[0, 16], [-RAMP, 5]], 0)
+    for k in range(2):
+        gcp(P("D1", step(12), k), P("exf"))
+    ts(P("D1", step(11), 1), P("exi"), -1.0, 1024.0, ALU.mult, ALU.add)
     for c in range(NCH):
-        iota(B("Ma", c)[:, :, 1], [[0, CL]], 0, ["Mz%d" % c], 400)
-        ts(B("ct", c)[:, :, :, 0], T.IO[:, 0:CW], 0.0, 2048.0, ALU.mult, ALU.add, ["IO"], ["cz%d" % c])
+        iota(B("Ma", c, ALL, 0), [[0, CL]], 0)
+        ts(B("ct", c, ALL, ALL, 0), P("IO", sl(0, CW)), 0.0, None, ALU.mult)
 
-    nbank = [0]
+    if Y_SCAN:
+        iota(P("yz"), [[0, 768]], 1)
+        iota(P("yz", sl(0, 768, 3)), [[0, 256]], 0)
+    nbank, keyed, held = [0], {}, []
 
-    def state(t):
-        return T["st%d" % t], ["st0_%d" % k for k in range(K)] if t == 0 else ["st%d" % t]
+    def cols(c):
+        return sl(CW * c, CW * c + CW)
+
+    def product(t, rows, L):
+        lin("v", P("D0", step(13), rows), L, 1.0 / 32, 37.0)
+        lin("v", P("D1", step(13), rows), L, 33.0, float(77 * t + 37 * 1024 - 80 * F - 1024))
+
+    def code0(t):
+        return P("le%d" % t) if t and AHEAD else P("st%d" % t, 0, ALL, 0)
+
+    def ahead(t):
+        L0 = code0(t)
+        tt(P("a1"), P("ex32"), P("D0", step(13), 0), ALU.mult)
+        tt(P("a2"), P("a1"), P("K3", ALL, 0), ALU.add)
+        ts(P("a3"), P("a2"), 5, W - 1, ALU.arith_shift_right, ALU.bitwise_and)
+        tt(P("a0"), P("a3"), L0, ALU.subtract)
+        tt(P("a1"), P("DD", ALL, 0), P("a0"), ALU.mult)
+        tt(P("se%d" % t), P("a1"), L0, ALU.add)
+        send(T.cores[(rank + 1) % NR], P("le%d" % (t + 1)), P("se%d" % t))
 
     def prep(t):
-        st, ks = state(t)
-        L0, k0 = (T["le%d" % t][:], ["le%d" % t]) if t else (st[:, 0, :, 0], ks[:1])
-        for rows, src, kk, a in ((slice(0, 1), L0, k0, "a"), (slice(1, K), st[:, 0, :, 1:K], ks, "b")):
-            lin(PREP_ENG, D0[:, 13::16, rows], src,  1.0 / 32, 37.0, kk, ["D0" + a])
-            lin(PREP_ENG, D1[:, 13::16, rows], src, 33.0, float(77 * t + 37 * 1024 - 80 * F - 1024), kk, ["D1" + a])
-        lin("g", BE[:, 0:64:4], T.exf[:], 1.0, 0.0, ["exf"], ["BE0_0", "BE1_0"], 16)
-        tt(D0[:, 12::16, 1:K], st[:, 1, :, 1:K], T.IY[:, :, 1:K], ALU.is_equal, ks + ["IY"], ["D0m"], 96)
-        for s in range(3):
-            ts(MK[:, s::4, s + 1:K], st[:, 1, :, s + 1:K], float(JO - 1 + s), None, ALU.is_equal, None, ks, ["MK%d" % s])
-        for k in range(K):
-            cp(T.L16[:, 16 * k:16 * k + 16], st[:, 0, :, k] if k else L0, ks if k else k0, ["L16_%d" % k])
-        lin(PREP_ENG, T.w7[:], st[:, 0], 2048.0, 0.0, ks, ["w7"])
-        tt(T.K3[:], T.w7[:], T.KC[:], ALU.add, ["w7", "KC"], ["K3"], 128)
+        st = "st%d" % t
+        if not AHEAD:
+            product(t, sl(0, 2), P(st, 0, ALL, sl(0, 2)))
+        for k, L in enumerate((code0(t), P(st, 0, ALL, 1))):
+            if AHEAD:
+                product(t, k, L)
+            (gcp if L16_G else cp)(P("L16", sl(16 * k, 16 * k + 16)), L)
+        ts(P("D0", step(12), 1), P(st, 1, ALL, 1), float(JO), None, ALU.is_equal)
+        product(t, sl(2, 4), P(st, 0, ALL, sl(2, 4)))
+        tt(P("D0", step(11), sl(2, 4)), P(st, 1, ALL, sl(2, 4)), P("IY"), ALU.is_equal)
+        lin("v", P("D1", step(11), sl(2, 4)), P(st, 1, ALL, sl(2, 4)), -float(RAMP), float(RAMP * (JO - 1)))
+        for s in range(4):
+            ts(P("MK", sl(s, 64, 4)), P(st, 1, ALL, sl(2, 4)), float(JO - 1 + s), BIG, ALU.is_equal, ALU.mult)
+        for k in (2, 3):
+            (gcp if L16_G else cp)(P("L16", sl(16 * k, 16 * k + 16)), P(st, 0, ALL, k))
         lo = 0
         for eng, n in XL_CALLS:
-            gather(eng, T.XL[:, CL * lo:CL * (lo + n)], XW.indirect(T.L16[:, CW * lo:CW * (lo + n)]),
-                   XK + ["L16_%d" % (j // 2) for j in range(lo, lo + n)], ["XL%d" % j for j in range(lo, lo + n)], CL * n)
+            gather(eng, P("XL", sl(CL * lo, CL * (lo + n))), ind(XW, P("L16", sl(CW * lo, CW * (lo + n)))))
             lo += n
+        lin("v", P("w7"), P(st, 0), 2048.0, 0.0)
+        tt(P("K3"), P("w7"), P("KC"), ALU.add)
 
     def chain(t, c, k):
-        SN, sn = (B("SN", c), "SN%d" % c) if k < K else (B("SE", c), "SE%d" % c)
-        scan(SN[:, 0:128], D0[:, CL * c:CL * c + CL, k], D1[:, CL * c:CL * c + CL, k], ALU.mult, ALU.add,
-             ["D0c", "D1c"] + d1k(c, k) + ([] if k == K else ["D0b", "D1b", "D0m"] if k else ["D0a", "D1a"]), [sn], 128)
+        cl = sl(CL * c, CL * c + CL)
+        scan(B("SN", c, sl(0, CL)), P("D0", cl, k), P("D1", cl, k), ALU.mult, ALU.add)
+        for n, s in (("BR", 9), ("BE", 10))[k == 3:] if k else ():
+            gcp(P(n, sl(32 * c + k, 32 * c + 32, 4)), B("SN", c, step(s, 0)))
         if k:
-            lin(BE_ENG if k < K else "v", BE[:, 32 * c + k:32 * c + k + 32:4], SN[:, 11:128:16], 1.0, 0.0, [sn],
-                ["BE%d_%d" % (c, k % 4)] + (["BE1_0"] if (c, k) == (0, K) else []), CW)
-            yk, yl_ = "y16%d_%d" % (c, k - 1), A("y%d" % (k - 1), c)
-            ts(yl_, SN[:, 8:128:16], 8192.0, float(W), ALU.mult, ALU.min, [sn], [yk])
-            ysrc = XW.indirect(yl_)
-            yo, yi_ = ("yb", "ya") if k % 2 else ("ya", "yb")
-            if k == 1:
-                gather(Y0_ENG[c], B(yo, c)[:], ysrc, XK + [yk], [yo + str(c)], CL)
-            else:
-                op("v", lambda: V.tensor_tensor(B(yo, c)[:], ysrc, B(yi_, c)[:], ALU.max), XK + [yk, yi_ + str(c)], [yo + str(c)], (), gc_(CL))
-        if k == K:
-            return
-        tt(SN[:, 140::16], SN[:, 13:128:16], SN[:, 15:128:16], ALU.subtract, ["SN%d" % c], ["w%d" % c])
-        ts(B("so", c)[:, 0:2 * CW], SN[:, 12::16], 1024.0 - 31.0 / 64, float(W + 1), ALU.add, ALU.min, ["SN%d" % c, "w%d" % c], ["n16%d" % c, "b16%d" % c])
+            gcp(P("DD", cols(c), k - 1), B("SN", c, step(3, 0)))
+        tt(B("SN", c, step(12, 1)), B("SN", c, step(13, 0)), B("SN", c, step(15, 0)), ALU.subtract)
+        ts(B("so", c), B("SN", c, step(12)), 1024.0 - 31.0 / 64, float(W + 1), ALU.add, ALU.min)
         lo = 0
         for n in C_CALLS:
-            gather("v", B("c16", c)[:, 32 * lo:32 * (lo + n)], T.FA[:].indirect(A("n16", c, 2 * lo, 2 * (lo + n))), ["FA", "FB", "n16%d" % c],
-                   ["c16%d_%d" % (c, j) for j in range(lo, lo + n)], 32 * n)
+            gather("v", B("c16", c, sl(16 * lo, 16 * (lo + n))), ind(P("FA"), B("so", c, sl(CW + lo, CW + lo + n))))
             lo += n
-        for h in range(2):
-            ts(B("cf", c)[:, :, h, :], B("c16", c)[:, HC * h:HC * h + HC], -2048.0, None, ALU.add, None, ["c16%d_%d" % (c, 2 * h), "c16%d_%d" % (c, 2 * h + 1)], ["cf%d_%d" % (c, h)])
-        op("v", lambda: V.transpose(B("ct", c)[:, :, :, 1:17], B("cf", c)[:]), ["cf%d_0" % c, "cf%d_1" % c], ["ct%d" % c], (), vc(64))
+        if ONE_CAST:
+            ts(B("cf", c), B("c16", c), -2048.0, None, ALU.add)
+        for h in range(0 if ONE_CAST else 2):
+            ts(B("cf", c, ALL, h), B("c16", c, sl(64 * h, 64 * h + 64)), -2048.0, None, ALU.add)
+        ct, cf = B("ct", c, ALL, ALL, sl(1, KW)), B("cf", c)
+        op("v", lambda: V.transpose(ct[0], cf[0]), [ct], [cf], vc(ct, cf))
+
+    def ymax(t, k):
+        lst = P("y16", sl(16 * k, 16 * k + 16))
+        ts(lst, P("BE", sl(k + 1, 64, 4)), 1024.0, float(W), ALU.add, ALU.min)
+        ops[-1]["after"] = [keyed[Y_AFTER[k]]] if Y_AFTER[k] else []
+        if Y_SCAN:
+            gather(Y_SCAN[k], P("yg", sl(k, 768, 3)), ind(XW, lst))
+            if k == 2:
+                scan(P("ys"), P("yz"), P("yg"), ALU.mult, ALU.max)
+        elif k == 0:
+            gather(Y0_ENG, P("ya"), ind(XW, lst))
+        else:
+            tt(P("ya" if k == 2 else "yb"), ind(XW, lst), P("yb" if k == 2 else "ya"), ALU.max)
 
     def row(t, c, k):
-        KT, kt, grp = B("KT", c), "KT%d" % c, "k%d_%d_%d" % (t, c, k)
-        Vt, Mt, Ma = B("V", c), B("M", c), B("Ma", c)
-        ok = "b16%d" % c
-        qsrc = XW.indirect(A("b16", c))
-        op("v", lambda: V.tensor_tensor(Mt[:, :, 0], qsrc, T.XL[:, CL * (2 * k + c):CL * (2 * k + c + 1)], ALU.max),
-           XK + [ok, "XL%d" % (2 * k + c)], ["q%d" % c], (), gc_(CL))
-        if Q_ENG == "v":
-            cp(Mt[:, :, 1], Mt[:, :, 0], ["q%d" % c], ["qq%d" % c], 64)
-        elif Q_ENG == "s":
-            op("s", lambda: S.activation(Mt[:, :, 1], Mt[:, :, 0], ACT.Copy), ["q%d" % c], ["qq%d" % c], (), vc(CL))
-        else:
-            op("g", lambda: g.affine_select(Mt[:, :, 1], Mt[:, :, 0], [[0, CL]], ALU.is_ge, 0.0, 0, 0), ["q%d" % c], ["qq%d" % c], (), 170 + 2 * CL * CYC)
-        qk = ["q%d" % c, "qq%d" % c]
-        vks = ["V%d_%d" % (c, j) for j in range(4)]
-        lo = 0
-        for eng, n in PIECES.get((c, k), PIECES[None]):
-            gather(eng, Vt[:, 512 * lo:512 * (lo + n)], XW.indirect(B("c16", c)[:, 32 * lo:32 * (lo + n)]), XK + ["c16%d_%d" % (c, j) for j in range(lo, lo + n)], vks[lo:lo + n], 512 * n, big=eng == "s")
+        grp = "k%d_%d_%d" % (t, c, k)
+        tt(B("M", c, ALL, 0), ind(XW, B("so", c, sl(0, CW))), P("XL", sl(CL * (2 * k + c), CL * (2 * k + c + 1))), ALU.max)
+        for i in held[:]:
+            ops[i]["after"] = [len(ops) - 1]
+            held.remove(i)
+        (gcp if Q_ENG == "g" else cp)(B("M", c, ALL, 1), B("M", c, ALL, 0))
+        lo, ends = 0, []
+        for eng, n in PIECES.get((t, c, k), PIECES.get((c, k), PIECES[None])):
+            gather(eng, B("V", c, sl(256 * lo, 256 * (lo + n))), ind(XW, B("c16", c, sl(16 * lo, 16 * (lo + n)))), big=eng == "s")
             lo += n
-        mm([(KT[:, 68 * h:68 * h + 68], T["G%d" % h][:, 16 - 16 * (gp - h):144 - 16 * (gp - h)], B("ct", c)[:, :, gp, :], 68) for h in range(2) for gp in range(2)],
-           ["G0", "G1", "ct%d" % c, "cz%d" % c], [kt + "c"], [kt], grp)
-        mm([(KT[:, 0:KW:17], T.NI[:], T.TH[:, t, k, :], CW)], ["NI", "TH%d" % t, kt + "c"], [kt + "t"], [kt], grp)
-        for p in range(2):
-            ab = (c, k, p) in ABS
-            mks = ["M%d_%d%d" % (c, 2 * p + j, ab) for j in range(2)]
-            for j in range(2):
+            ends.append(lo)
+        if ONE_CAST:
+            for a in range(4):
+                mm([(B("KT", c, sl(KW * (2 * a + h), KW * (2 * a + h + 1))), P("G%d" % h, sl(16 - 16 * (gp - h), 144 - 16 * (gp - h))), B("ct", c, a, gp))
+                    for h in range(2) for gp in range(2)], grp)
+        else:
+            mm([(B("KT", c, sl(68 * h, 68 * h + 68)), P("G%d" % h, sl(16 - 16 * (gp - h), 144 - 16 * (gp - h))), B("ct", c, ALL, gp)) for h in range(2) for gp in range(2)], grp)
+        mm([(B("KT", c, sl(0, CW * KW, KW)), P("NI"), P("TH", t, k))], grp)
+        for h in range(2):
+            ab = (c, k, h) in ABS
+            for j in (2 * h, 2 * h + 1):
                 bn = "PB_%d" % (nbank[0] % NB)
                 nbank[0] += 1
-                bank, a0, vo, vk = T[bn], HC * p + 32 * j, 1024 * p + 512 * j, vks[2 * p + j]
-                mm([(bank[:, :, a, :], (T.NQ if ab else T.I2)[:], Mt[:, a0:a0 + 32, 0:2], 64) for a in range(8)], ["NQ", "I2"] + qk, [bn], [bn], grp + bn)
-                mm([(bank[:], (T.ID if ab else T.NQ)[:], Vt[:, vo:vo + 512], 512)], ["ID", "NQ", vk], [bn], [bn], grp + bn)
-                if ab:
-                    op("s", lambda a0=a0, bank=bank: S.activation(Ma[:, a0:a0 + 32, 2:18], bank[:], ACT.Abs), [bn], [mks[j]], [bn], vc(512) + SFX)
-                else:
-                    e = 32 // TSPLIT
-                    for a in range(TSPLIT):
-                        tt(Mt[:, a0 + e * a:a0 + e * a + e, 2:18], Vt[:, vo + 16 * e * a:vo + 16 * e * (a + 1)], bank[:, e * a:e * a + e], ALU.min,
-                           [vk, bn], [mks[j] + "_%d" % a], 16 * e, x=[bn])
-            Z, Ms = (T.ZV, Ma) if ab else (T.ZM, Mt)
-            mm([(KT[:, 68 * p:68 * p + 68], Z[:, 15 - i:143 - i], Ms[:, HC * p + i:HC * p + HC:16, 1:18], 68) for i in range(16)],
-               ["ZV", "ZM", "Mz%d" % c, kt + "c"] + (mks if ab else [m + "_%d" % a for m in mks for a in range(TSPLIT)]) + qk, [kt + "m%d" % p], [kt], grp)
-        if k < K - 1:
-            tt(A("pre", c, 0, 32), BE[:, 32 * c:32 * c + 32], MK[:, 32 * c:32 * c + 32, k + 1], ALU.mult, bek[4 * c:4 * c + 4] + ["MK0", "MK1", "MK2"], ["pre%d" % c], 64)
-            scan(D1[:, CL * c:CL * c + CL:4, k + 1], T.PZ[:], A("pre", c, 0, 32), ALU.mult, ALU.add, ["PZ", "pre%d" % c], d1k(c, k + 1), 32)
-        SK = B("SK", c)
-        scan(SK[:], T.RS[:], KT[:, 0:KW], ALU.add, ALU.min, ["RS"] + [kt + a for a in ("c", "t", "m0", "m1")], ["SK%d" % c], KW, x=[kt])
-        for s, o in enumerate((ALU.subtract, ALU.subtract, ALU.is_ge)):
-            tt(D1[:, CL * c + 4 * s:CL * c + CL:16, k + 1], SK[:, 16::17], SK[:, 0::17], o, ["SK%d" % c], d1k(c, k + 1)[s:s + 1])
+                qs = [(P(bn, ALL, a), P("NQ" if ab else "I2"), B("M", c, sl(32 * j, 32 * j + 32), sl(0, 2))) for a in range(8)]
+                if j < SINGLE_Q:
+                    qs = [(P(bn, ALL, a // 2, a % 2), P("NQ" if ab else "I2"), B("M", c, sl(32 * j, 32 * j + 32), 0)) for a in range(16)]
+                late = j < V_FIRST.get((c, k), V_FIRST[None])
+                if not late:
+                    mm(qs, grp + bn)
+                for lo, hi in ((0, 16), (16, 32)) if 2 * j + 1 in ends and not ab and not late else ((0, 32),):
+                    mm([(P(bn, sl(lo, hi)), P("ID" if ab else "NQ"), B("V", c, sl(512 * j + 16 * lo, 512 * j + 16 * hi)))], grp + bn)
+                    if late:
+                        mm(qs, grp + bn)
+                    if ab:
+                        bank, out = P(bn), B("Ma", c, sl(32 * j, 32 * j + 32), sl(1, KW))
+                        op("s", lambda out=out, bank=bank: S.activation(out[0], bank[0], ACT.Abs), [out], [bank], 512 * CYC + SFX)
+                        continue
+                    a = 32 * j + lo
+                    while a < 32 * j + hi:
+                        e = min(a + TSPLIT[a // 8], 32 * j + hi)
+                        tt(B("M", c, sl(a, e), sl(2, 18)), B("V", c, sl(16 * a, 16 * e)), P(bn, sl(a - 32 * j, e - 32 * j)), ALU.min)
+                        if a >= Q_FIRST and (c, k) != (1, K - 1):
+                            held.append(len(ops) - 1)
+                        a = e
+            for i0, i1 in zip(SUMS[h], SUMS[h][1:]):
+                mm([(B("KT", c, sl(68 * h, 68 * h + 68)), P("ZV" if ab else "ZM", sl(15 - i, 143 - i)),
+                     B("Ma", c, sl(64 * h + i, 64 * h + 64, 16)) if ab else B("M", c, sl(64 * h + i, 64 * h + 64, 16), sl(1, 18))) for i in range(i0, i1)], grp)
+        scan(B("SK", c), P("RS"), B("KT", c, sl(0, CW * KW)), ALU.add, ALU.min)
+        keyed[c, k] = len(ops) - 1
 
-    def place(t, c):
-        so, kt = B("KT", c)[:, 256:256 + CW], "KT%d" % c
-        y = B("ya", c)
-        mm([(so, T.ZW[:, 15 - i:143 - i], y[:, i:CL:16], CW) for i in range(16)], ["ZW", "ya%d" % c],
-           [kt + a for a in ("s", "c", "t", "m0", "m1")], [kt], "s%d_%d" % (t, c))
-        cp(A("s1", c), so, [kt + "s"], ["s1%d" % c, kt + "c"], x=[kt])
-        ts(A("s2", c), A("s1", c), 15, None, ALU.bitwise_and, None, ["s1%d" % c], ["s2%d" % c])
-        tt(A("s3", c), A("s2", c), T.BASE[:], ALU.add, ["s2%d" % c, "BASE"], ["s3%d" % c])
-        ts(A("p16", c), A("s3", c), c16_, None, ALU.add, None, ["s3%d" % c, "c16_"], ["p16%d" % c])
+    def file_keys(t, c, k):
+        for j, s in enumerate((0, 4, 8)):
+            if k < K and j >= KEY_V:
+                gcp(P("D1", step(s, c), k), P("D1", step(0, c), k))
+            else:
+                tt(P("D1", step(s, c), k), B("SK", c, sl(KW - 1, None, KW)), B("SK", c, sl(0, None, KW)), ALU.subtract)
 
-    def scatter(t, c):
-        buf, o, key = XS[(t + 1) % 2], 2048 * c, "X%d_%d" % ((t + 1) % 2, c)
-        op("v", lambda: V.tensor_copy(buf[:, o:o + 2048].indirect(A("p16", c)), B("ya", c)[:]), ["p16%d" % c, "ya%d" % c, key], [key], (), gc_(CL, CS))
+    def pick(t, k):
+        scan(P("D1", sl(0, 2 * CL, 4), k), P("MK", ALL, k - 2), P("BR"), ALU.add, ALU.min)
+
+    def finish(t, c):
+        cl = sl(CL * c, CL * c + CL)
+        file_keys(t, c, K)
+        scan(P("SE", cl), P("D0", cl, K), P("D1", cl, K), ALU.mult, ALU.add)
+        lst = P("y16", sl(48 + CW * c, 48 + CW * c + CW))
+        ts(lst, P("SE", step(10, c)), 1024.0, float(W), ALU.add, ALU.min)
+        tt(P("yb", cl), ind(XW, lst), P("ys", sl(3 * CL * c + 2, 3 * CL * c + 3 * CL, 3)) if Y_SCAN else P("ya", cl), ALU.max)
+        so = P("MS", sl(128 + CW * c, 128 + CW * c + CW))
+        mm([(so, P("ZW", sl(15 - i, 143 - i)), P("yb", sl(CL * c + i, CL * c + CL, 16))) for i in range(16)], "s%d_%d" % (t, c))
+        tt(P("pk", cols(c)), so, P("NB"), ALU.add)
+        tt(P("pf", cols(c)), so, P("pk", cols(c)), ALU.subtract)
+        ts(P("p16", cols(c)), P("pf", cols(c)), 16.0, c16_, ALU.mult, ALU.add)
+        win = P(XS[(t + 1) % 2], sl(2048 * c, 2048 * c + 2048))
+        cp(ind(win, P("p16", cols(c))), P("yb", cl))
         if t == TV - 1:
-            dma("y", T.yx[:, 2048 * c:2048 * c + 2048], buf[:, o:o + 2048], [key], (), 1 << 19, 0.0 if c else 3500.0)
+            dma("y", T.yx[:, 2048 * c:2048 * c + 2048], win, 1 << 19, 0.0 if c else 3500.0)
 
-    def rewire_pre(t):
-        st, ks = state(t)
-        ts(T.LB[:], BE[:, 0:64], float(JO), 8192.0, ALU.is_lt, ALU.mult, bek, ["LB"])
-        scan(T.PP[:], T.LB[:], BE[:, 0:64], ALU.add, ALU.min, bek + ["LB"], ["PP"], 64)
-        scan(T.JJ[:], T.LB[:], T.IX[:], ALU.add, ALU.min, ["IX", "LB"], ["JJ"], 64)
-        lin(PREP_ENG, T.w0[:], T.PP[:], 32.0, -32768.0, ["PP"], ["w0"])
-        tt(T.w2[:], T.w0[:], D0[:, 13::16, 0:K], ALU.mult, ["w0", "D0a", "D0b"], ["w20", "w21"], 128)
-        tt(T.w3[:], T.w2[:], T.K3[:], ALU.add, ["w20", "w21", "K3"], ["w3"], 128)
-        ts(T.w4[:], T.w3[:], 5, W - 1, ALU.arith_shift_right, ALU.bitwise_and, ["w3"], ["w4"])
-        tt(T.w1[:], T.w4[:], st[:, 0], ALU.subtract, ["w4"] + ks, ["w1"], 128)
+    def rewire_early(t):
+        st, sb, r3 = "st%d" % t, "snd%d" % t, sl(0, 3)
+        BE = P("BE", sl(0, 64))
+        ts(P("LB"), BE, float(JO), 8192.0, ALU.is_lt, ALU.mult)
+        scan(P("PP"), P("LB"), BE, ALU.add, ALU.min)
+        scan(P("JJ"), P("LB"), P("IX"), ALU.add, ALU.min)
+        lin("v", P("w0"), P("PP"), 32.0, -32768.0)
+        tt(P("w2"), P("w0"), P("D0", step(13), sl(0, K)), ALU.mult)
+        tt(P("w3"), P("w2"), P("K3"), ALU.add)
+        ts(P("w4"), P("w3"), 5, W - 1, ALU.arith_shift_right, ALU.bitwise_and)
+        tt(P("w1"), P("w4"), P(st, 0), ALU.subtract)
+        Bs = P("BE", sl(1, 65))
+        tt(P("w2", ALL, r3), P("w1", ALL, r3), P("DD", ALL, r3), ALU.mult)
+        tt(P(sb, 0, ALL, r3), P("w2", ALL, r3), P(st, 0, ALL, r3), ALU.add)
+        tt(P("w5"), Bs, P(st, 1), ALU.max)
+        tt(P(sb, 1), P("w5"), P("JJ"), ALU.min)
         if t < TV - 1:
-            se, sk = T["se%d" % t][:], "se%d" % t
-            ts(T.ed[:], BE[:, 1:65:4], float(JO), None, ALU.is_ge, None, ["BE0_1", "BE1_1"], ["ed"])
-            tt(se, T.ed[:], T.w1[:, :, 0], ALU.mult, ["ed", "w1"], [sk])
-            tt(se, se, st[:, 0, :, 0], ALU.add, [sk] + ks, [sk])
-            send(T.cores[(rank + 1) % NR], T["le%d" % (t + 1)][:], se, [sk], ["le%d" % (t + 1)])
-
-    def rewire(t, cs):
-        st, ks = state(t)
-        lo, hi = CW * cs[0], CW * cs[-1] + CW
-        n = lambda a: [a + str(c) for c in cs]
-        Bs, be, sb = BE[:, 4 * lo + 1:4 * hi + 1], bek[lo // 2:hi // 2] + ["BE1_0"], T["snd%d" % t]
-        ts(T.DD[:, 4 * lo:4 * hi], Bs, float(JO), None, ALU.is_ge, None, be, n("DD"))
-        tt(T.w2[:, lo:hi], T.w1[:, lo:hi], T.DD[:, 4 * lo:4 * hi], ALU.mult, ["w1"] + n("DD"), n("w2"), 8 * (hi - lo))
-        tt(sb[:, 0, lo:hi], T.w2[:, lo:hi], st[:, 0, lo:hi], ALU.add, n("w2") + ks, n("sa%d" % t), 8 * (hi - lo))
-        tt(T.w5[:, 4 * lo:4 * hi], Bs, st[:, 1, lo:hi], ALU.max, be + ks, n("w5"), 8 * (hi - lo))
-        tt(sb[:, 1, lo:hi], T.w5[:, 4 * lo:4 * hi], T.JJ[:, 4 * lo:4 * hi], ALU.min, n("w5") + ["JJ"], n("sb%d" % t), 8 * (hi - lo))
-        if t < TV - 1:
-            send(T.cores[(rank + 1) % NR], T["st%d" % (t + 1)][:], sb[:], n("sa%d" % t) + n("sb%d" % t), ["st%d" % (t + 1)])
+            send(T.cores[(rank + 1) % NR], P("st%d" % (t + 1)), P(sb))
         else:
-            lin(OUT_ENG[cs[0]][K], sb[:, 1, lo:hi], sb[:, 1, lo:hi], 1.0, -float(JO), n("sb%d" % t), n("sb%d" % t))
-            for k in range(K):
-                lin(OUT_ENG[cs[0]][k], T.OUT[:, :, k, lo:hi], sb[:, :, lo:hi, k], 1.0, 0.0, n("sa%d" % t) + n("sb%d" % t), ["OUT%d_%d" % (cs[0], k)], 16)
+            ts(P(sb, 1, ALL, r3), P(sb, 1, ALL, r3), -float(JO), None, ALU.add)
+            for k in range(3):
+                gcp(P("OUT", ALL, k), P(sb, ALL, ALL, k))
+            send(T.cores[(rank - t) % NR], P("FIN"), P("OUT"))
+            dma("y", T.yl[:, 0:48], P("FIN", 0), 24576)
+            dma("s", T.yi[:, 0:48], P("FIN", 1), 24576)
+            tt(P("w6", 0), P("JJ", sl(3, 64, 4)), P(st, 1, ALL, 3), ALU.subtract)
+            ts(P("w6", 1), P(st, 1, ALL, 3), -float(JO), None, ALU.add)
+
+    def rewire_late(t, c):
+        st, sb, dead, cs = "st%d" % t, "sl%d" % t, P("SE", step(3, c)), ALL if c is None else cols(c)
+        tt(P("w8", 0, cs), dead, P("w1", cs, 3), ALU.mult)
+        tt(P(sb, 0, cs), P("w8", 0, cs), P(st, 0, cs, 3), ALU.add)
+        if t < TV - 1:
+            tt(P("w8", 1), P("SE", step(10)), P(st, 1, ALL, 3), ALU.max)
+            tt(P(sb, 1), P("w8", 1), P("JJ", sl(3, 64, 4)), ALU.min)
+        else:
+            tt(P("w8", 1, cs), dead, P("w6", 0, cs), ALU.mult)
+            tt(P(sb, 1, cs), P("w8", 1, cs), P("w6", 1, cs), ALU.add)
+
+    def count(t):
+        send(T.cores[(rank + 1) % NR], P("lt%d" % (t + 1)), P("sl%d" % t))
+        gcp(P("DD", ALL, 3), P("SE", step(3)))
+        mm([(P("MS", sl(0, 64)), P("ON"), P("DD"))])
+        c0, c1, ci, msum = P("cnt", sl(0, 1)), P("cnt", sl(1, 2)), P("cni", sl(0, 1)), P("MS", sl(0, 64))
+        op("v", lambda: V.tensor_reduce(c0[0], msum[0], AxisListType.X, ALU.add), [c0], [msum], 64 * CYC)
+        ts(ci, c0, 1.0 / 32, -31.0 / 64, ALU.mult, ALU.add)
+        ts(c1, ci, -32.0, c0, ALU.mult, ALU.add)
+        ts(P("TH", t + 1), P("thf"), c1, 240.0, ALU.add, ALU.min)
+
+    def patch(t):
+        gcp(P("st%d" % t, ALL, ALL, 3), P("lt%d" % t))
+        iota(P("BR", sl(2, 64, 4)), [[0, 16]], 2 * RAMP)
 
     for t in range(TV):
-        XW, XK = XS[t % 2][:], ["X%d_0" % (t % 2), "X%d_1" % (t % 2), "XZ"]
-        prep(t)
-        dma("y", XS[(t + 1) % 2][:, 0:W], XS[t % 2][:, 0:W], XK + ["FA"] + state(t)[1], ["X%d_0" % ((t + 1) % 2), "X%d_1" % ((t + 1) % 2)], 1 << 20)
+        XW = P(XS[t % 2])
+        if t:
+            do(patch, "patch", t)
+        do(prep, "prep", t)
+        dma("y", P(XS[(t + 1) % 2], sl(0, W)), P(XS[t % 2], sl(0, W)), 1 << 20, also=[P("lt%d" % t) if t else P("FA")])
         for k in range(K):
+            if k >= 2:
+                do(pick, "pick", t, k)
             for c in range(NCH):
-                chain(t, c, k)
+                if k:
+                    do(file_keys, "keys", t, c, k)
+                do(chain, "chain", t, c, k)
+            for j in range(3 if k == K - 1 else 0):
+                do(ymax, "y", t, j)
+            if k == AHEAD and t < TV - 1:
+                do(ahead, "ahead", t)
             if k == K - 1:
-                rewire_pre(t)
+                do(rewire_early, "early", t)
             for c in range(NCH):
-                row(t, c, k)
+                do(row, "row", t, c, k)
                 if k == K - 1:
-                    chain(t, c, K)
-                if k == K - 1 and t == TV - 1:
-                    rewire(t, [c])
+                    do(finish, "finish", t, c)
+                    if t == TV - 1:
+                        do(rewire_late, "late", t, c)
         if t < TV - 1:
-            rewire(t, range(NCH))
-        for c in range(NCH):
-            place(t, c)
-            scatter(t, c)
-        if t < TV - 1:
-            mm([(MS[:, 0:64], T.ON[:], T.DD[:], 64)], ["ON", "DD0", "DD1"], ["MS"], ["MS"], None)
-            op("v", lambda: V.tensor_reduce(T.cnt[:, 0:1], MS[:, 0:64], AxisListType.X, ALU.add), ["MS"], ["cn0"], ["MS"], vc(64))
-            ts(T.cni[:, 0:1], T.cnt[:, 0:1], 1.0 / 32, -31.0 / 64, ALU.mult, ALU.add, ["cn0"], ["cn1"])
-            ts(T.cnt[:, 1:2], T.cni[:, 0:1], -32.0, T.cnt[:, 0:1], ALU.mult, ALU.add, ["cn0", "cn1"], ["cn2"])
-            ts(T.TH[:, t + 1], T.thf[:], T.cnt[:, 1:2], 240.0, ALU.add, ALU.min, thk + ["cn2"], ["TH%d" % (t + 1)])
-    send(T.cores[(rank - (TV - 1)) % NR], T.FIN[:], T.OUT[:], ["OUT%d_%d" % (c, k) for c in range(NCH) for k in range(K)], ["FIN"])
-    dma("y", T.yl[:], T.FIN[:, 0], ["FIN"], (), 32768)
-    dma("s", T.yi[:], T.FIN[:, 1], ["FIN"], (), 32768)
+            do(rewire_late, "late", t, None)
+            do(count, "count", t)
+    send(T.cores[(rank - (TV - 1)) % NR], P("lt3"), P("sl2"), 0.6)
+    dma("y", T.yl[:, 48:64], P("lt3", 0), 8192)
+    dma("s", T.yi[:, 48:64], P("lt3", 1), 8192)
     return ops, nload
 
 
 def depend(ops):
-    lastw, readers, epoch = {}, {}, {}
+    hist, epoch = {}, {}
     for i, o in enumerate(ops):
-        d = set()
-        for k in o["r"]:
-            if k in lastw:
-                d.add(lastw[k])
-        for k in o["w"]:
-            if k in lastw:
-                d.add(lastw[k])
-            d.update(readers.get(k, ()))
+        d = set(o.get("after", ()))
+        for n, m in o["r"]:
+            d.update(e[0] for e in hist.get(n, ()) if e[2] and e[1] & m)
+        for n, m in o["w"]:
+            d.update(e[0] for e in hist.get(n, ()) if e[1] & m)
         for k in o["x"]:
-            e = epoch.setdefault("#" + k, [o["e"], [], []])
+            e = epoch.setdefault(k, [o["e"], [], []])
             if e[0] != o["e"]:
                 e[0], e[2], e[1] = o["e"], e[1], []
             d.update(e[2])
             e[1].append(i)
-        for k in o["r"]:
-            readers.setdefault(k, []).append(i)
-        for k in o["w"]:
-            lastw[k] = i
-            readers[k] = []
+        for n, m in o["w"]:
+            hist[n] = [[e[0], e[1] & ~m, e[2]] for e in hist.get(n, ()) if e[1] & ~m]
+        for n, m in o["r"]:
+            hist.setdefault(n, []).append([i, m, False])
+        for n, m in o["w"]:
+            hist.setdefault(n, []).append([i, m, True])
         d.discard(i)
         o["d"] = sorted(d)
 
@@ -560,16 +666,16 @@ def schedule(ops, nload):
     ap = [[j for j, kind in pred[i]] for i in range(n)]
     sp = [[j for j, kind in succ[i]] for i in range(n)]
 
-    marks = [i for i in range(n) if ops[i]["big"]]
+    ws = [[j for j, kind in succ[i] if kind == 1] for i in range(n)]
+    nm, nq = len(ms_), len(qn)
+    wgt = [float(WGT[m] / base[m]) for m in ms_]
+    st_, fin_, tail = ([[0.0] * n for _ in ms_] for _ in range(3))
 
-    def run(seq, lo=0, old=None):
-        out, tot = [], 0.0
-        for a in range(len(ms_)):
-            d, l, free = dur[a], lag[a], [0.0] * len(qn)
-            st, fin = (old[a][0][:], old[a][1][:]) if old else ([0.0] * n, [0.0] * n)
-            for i in seq[max(lo - 60, 0):lo] if lo > 60 and len({q[i] for i in seq[lo - 60:lo]}) == len(qn) else seq[:lo]:
-                free[q[i]] = st[i] + d[i]
-            for i in seq[lo:]:
+    def heads(part, free0):
+        out = []
+        for a in range(nm):
+            d, l, st, fin, free = dur[a], lag[a], st_[a], fin_[a], free0[a][:]
+            for i in part:
                 t = free[q[i]]
                 for j in wp[i]:
                     if fin[j] > t:
@@ -578,16 +684,22 @@ def schedule(ops, nload):
                 t += d[i]
                 free[q[i]] = t
                 fin[i] = t + l[i]
-            out.append((st, fin))
-            tot += float(WGT[ms_[a]] / base[ms_[a]]) * (max(fin) + CFG["eps"] * sum([fin[i] for i in marks]) / len(marks))
-        return tot, out
+            out.append(free)
+        return out
+
+    def tails(seq):
+        for a in range(nm):
+            d, l, tl, nx = dur[a], lag[a], tail[a], [0.0] * nq
+            for i in seq[::-1]:
+                t = max(nx[q[i]], l[i] + max([tl[j] for j in ws[i]] + [0.0]))
+                tl[i] = nx[q[i]] = t + d[i]
 
     def move(seq, pos, a, b, early):
         lo, hi = pos[a], pos[b]
         take, stack = {b if early else a}, [b if early else a]
         while stack:
             for j in (ap if early else sp)[stack.pop()]:
-                if lo <= pos[j] <= hi and j not in take:
+                if lo <= pos.get(j, -1) <= hi and j not in take:
                     if j == a or j == b:
                         return None
                     take.add(j)
@@ -596,48 +708,214 @@ def schedule(ops, nload):
         y = [i for i in seq[lo:hi + 1] if i not in take]
         return seq[:lo] + (x + y if early else y + x) + seq[hi + 1:]
 
-    seq = best[1]
-    val, out = run(seq)
-    top, fresh = (val, seq), True
-    for r in range(CFG["swaps"]):
-        if fresh:
-            pos, prev, nxt_, lastq = [0] * n, [-1] * n, [-1] * n, {}
-            for a, i in enumerate(seq):
-                pos[i] = a
-                if q[i] in lastq:
-                    prev[i] = lastq[q[i]]
-                    nxt_[prev[i]] = i
-                lastq[q[i]] = i
-            arcs = []
-            for a in range(len(ms_)):
-                st, fin = out[a]
-                i = max(range(n), key=lambda i: fin[i])
-                while st[i] > 0:
-                    j = prev[i]
-                    if j >= 0 and st[j] + dur[a][j] >= st[i] - 1e-6:
-                        arcs.append((j, i))
-                    else:
-                        j = max(wp[i], key=lambda j: fin[j])
-                    i = j
-            fresh = False
-        a, b = arcs[int(rnd() * len(arcs))]
-        early = rnd() < 0.5
-        while rnd() < CFG["jump"]:
-            if early and prev[a] >= 0:
-                a = prev[a]
-            if not early and nxt_[b] >= 0:
-                b = nxt_[b]
-        new = move(seq, pos, a, b, early)
-        if new is None:
-            continue
-        v2, o2 = run(new, pos[a], out)
-        if v2 <= val + CFG["temp"] * (1.0 - r / CFG["swaps"]) * -np.log(rnd() + 1e-12):
-            st, at = o2[0][0], {i: a for a, i in enumerate(new)}
-            seq, val, out, fresh = sorted(new, key=lambda i: (st[i], at[i])), v2, o2, True
-            if val < top[0]:
-                top = (val, seq)
-    ORDER["len"] = length(top[1])
-    return top[1]
+    def improve(part, rest, free0, tries, temp):
+        inside = set(part)
+        edge = [i for i in part if not ws[i] or [j for j in ws[i] if j not in inside]]
+        out = [[max([tail[a][j] for j in ws[i] if j not in inside] + [0.0]) for i in edge] for a in range(nm)]
+        nextq = {}
+        for i in rest[::-1]:
+            nextq[q[i]] = i
+        outq = [[tail[a][nextq[e]] if e in nextq else 0.0 for e in range(nq)] for a in range(nm)]
+
+        def value(p, lo=0):
+            if lo:
+                for a in range(nm):
+                    fin, keep = fin_[a], kept[a]
+                    for i in p[dirty[0]:lo]:
+                        fin[i] = keep[i]
+                dirty[0] = lo
+            free, tot, ends = heads(p[lo:], frees[lo] if lo else free0), 0.0, []
+            for a in range(nm):
+                fin = fin_[a]
+                v = [fin[i] + o for i, o in zip(edge, out[a])]
+                u = [f + o for f, o in zip(free[a], outq[a])]
+                top = max(max(v), max(u))
+                tot += wgt[a] * (top + CFG["eps"] * sum([max(x - top + CFG["near"], 0.0) for x in v + u]))
+                ends.append(edge[v.index(top)] if top in v else -1 - u.index(top))
+            return tot, ends
+
+        val, ends = value(part)
+        top, fresh = (val, part), True
+        for r in range(tries):
+            if fresh:
+                pos, prev, nxt_, lastq = {}, {}, {}, {}
+                kept, dirty, frees, now = [{i: fin_[a][i] for i in part} for a in range(nm)], [len(part)], [], free0
+                for a, i in enumerate(part):
+                    frees.append(now)
+                    now = [f[:] for f in now]
+                    for b in range(nm):
+                        now[b][q[i]] = st_[b][i] + dur[b][i]
+                    pos[i] = a
+                    if q[i] in lastq:
+                        prev[i] = lastq[q[i]]
+                        nxt_[prev[i]] = i
+                    lastq[q[i]] = i
+                arcs = []
+                for a in range(nm):
+                    st, fin, i = st_[a], fin_[a], ends[a] if ends[a] >= 0 else lastq.get(-1 - ends[a])
+                    while i in inside:
+                        j = prev.get(i)
+                        if j is not None and st[j] + dur[a][j] >= st[i] - 1e-6:
+                            arcs.append((j, i))
+                        else:
+                            j = max(wp[i], key=lambda j: fin[j]) if wp[i] else None
+                            if j is not None and fin[j] < st[i] - 1e-6:
+                                j = None
+                        i = j
+                fresh = False
+                if not arcs:
+                    break
+            a, b = arcs[int(rnd() * len(arcs))]
+            early = rnd() < 0.5
+            jump = CFG["jump"][int(rnd() * len(CFG["jump"]))]
+            while rnd() < jump:
+                if early:
+                    a = prev.get(a, a)
+                else:
+                    b = nxt_.get(b, b)
+            new = move(part, pos, a, b, early)
+            if new is None:
+                continue
+            v2, e2 = value(new, pos[a])
+            dirty[0] = pos[a]
+            if v2 <= val + temp * -np.log(rnd() + 1e-12):
+                heads(new, free0)
+                st, at = st_[0], {i: a for a, i in enumerate(new)}
+                part, val, ends, fresh = sorted(new, key=lambda i: (st[i], at[i])), v2, e2, True
+                if val < top[0]:
+                    top = (val, part)
+        return top[1]
+
+    def sweeps(seq, count, temp, only=None):
+        span = CFG["span"]
+        for r in range(count):
+            tails(seq)
+            at = only if isinstance(only, range) else [a for a, i in enumerate(seq) if only is None or ops[i]["tag"][0] == only]
+            lo = max(at[0] - int(span * rnd() / 2), 0)
+            free0 = heads(seq[:lo], [[0.0] * nq for _ in ms_])
+            step = int(span * (0.3 + 0.4 * rnd()))
+            while lo <= at[-1]:
+                seq[lo:lo + span] = improve(seq[lo:lo + span], seq[lo + span:], free0, CFG["swaps"], temp * (1.0 - r / count))
+                free0 = heads(seq[lo:lo + step], free0)
+                lo, step = lo + step, span // 2
+        return seq
+
+    def pattern():
+        role, turn, seen = {}, {}, {}
+        for i, o in enumerate(ops):
+            if o["tag"][1] in ("row", "chain", "keys"):
+                r = (o["tag"][1], o["e"], o["w"][0][0][:2])
+                seen[o["tag"][:4], r] = seen.get((o["tag"][:4], r), 0) + 1
+                role[i], turn[i] = r + (seen[o["tag"][:4], r],), 2 * o["tag"][3] + o["tag"][2]
+        core_ = [i for i in role if ops[i]["tag"][0] == 1]
+        inside = set(core_)
+        cp_ = {i: [j for j in ap[i] if j in inside] for i in core_}
+        cw = {i: [j for j in wp[i] if j in inside] for i in core_}
+        heads(best[1], [[0.0] * nq for _ in ms_])
+        ref = [i for i in core_ if role[i][2] == "SK"]
+        period = (st_[0][ref[5]] - st_[0][ref[1]]) / 4
+        shift = {role[i]: st_[0][i] / period - turn[i] for i in sorted(core_, key=lambda i: -abs(turn[i] - 4))}
+        for r, at in PLAN.items():
+            shift.update({r + (j + 1,): a for j, a in enumerate(at)})
+        names = list({role[i]: 0 for i in core_ if turn[i] == 4})
+        names += [r for r in shift if r not in names]
+        mates = {r: [s for s in names if s[1] == r[1] and s != r] for r in names}
+
+        def value(sh):
+            key = {}
+            for i in core_:
+                key[i] = max([turn[i] + sh[role[i]]] + [key[j] + 1e-6 for j in cp_[i] if j in key])
+            order_, tot = sorted(core_, key=key.get), 0.0
+            for a in range(nm):
+                d, l, st, fin, free = dur[a], lag[a], st_[a], fin_[a], [0.0] * nq
+                for i in order_:
+                    t = free[q[i]]
+                    for j in cw[i]:
+                        if fin[j] > t:
+                            t = fin[j]
+                    st[i] = t
+                    free[q[i]] = t + d[i]
+                    fin[i] = t + d[i] + l[i]
+                tot += wgt[a] * max(free)
+            return tot
+
+        def anneal(shift, names, tries, wide):
+            val = value(shift)
+            top = (val, shift)
+            for r in range(tries):
+                new, a = dict(shift), names[int(rnd() * len(names))]
+                if rnd() < 0.5 and a in mates:
+                    b = mates[a][int(rnd() * len(mates[a]))]
+                    new[a] = shift[b] + round(shift[a] - shift[b]) + (0.002 if rnd() < 0.5 else -0.002) * rnd()
+                else:
+                    lo, by = names.index(a), (rnd() - 0.5) * wide[int(rnd() * len(wide))]
+                    for b in names[lo:lo + (1 if rnd() < 0.5 else 1 + int(rnd() * 8))]:
+                        new[b] = shift[b] + by
+                v2 = value(new)
+                if v2 <= val + CFG["heat"] * (1.0 - r / tries) * -np.log(rnd() + 1e-12):
+                    shift, val = new, v2
+                    if val < top[0]:
+                        top = (val, shift)
+            value(top[1])
+            return dict(top[1])
+
+        shift = anneal(shift, names, CFG["pattern"], (0.3,))
+        ORDER["period"] = [(st_[a][ref[6]] - st_[a][ref[2]]) / 4 for a in range(nm)]
+        names, end = [], {}
+        for i, o in enumerate(ops):
+            step_ = o["tag"][1]
+            if step_ == "chain" and turn[i] < 2:
+                del role[i]
+            elif (step_ == "row" and turn[i] in CFG["apart"]) or step_ in CFG["ending"] or (step_ == "prep" and o["w"] and o["w"][0][0] == "XL"):
+                r = (o["tag"][1:], o["e"])
+                if o["tag"][0] == 1:
+                    names.append(r)
+                    shift[r] = turn[i] + shift[role[i]] if i in role else CFG["ending"].get(step_, 0.0) + 0.01 * o["tag"][-1]
+                role[i], turn[i] = r, 0
+        for i in [i for i in role if role[i] not in shift]:
+            del role[i]
+        core_[:] = [i for i in sorted(role) if ops[i]["tag"][0] == 1]
+        inside = set(core_)
+        cp_.update({i: [j for j in ap[i] if j in inside] for i in core_})
+        cw.update({i: [j for j in wp[i] if j in inside] for i in core_})
+        anneal(shift, names, CFG["whole"], (0.1, 0.3, 1.0))
+        ORDER["core"] = sorted([(st_[0][i], dur[0][i], role[i], turn[i]) for i in core_])
+        at = {ops[i]["tag"][1:]: st_[0][i] for i in core_}
+        key = [at[o["tag"][1:]] + 1e6 * o["tag"][0] if i in role else None for i, o in enumerate(ops)]
+        for i in range(n):
+            if ops[i]["tag"][1] in CFG["asap"]:
+                key[i] = max([key[j] + 100.0 for j in ap[i] if key[j] is not None] + [0.0])
+        for i in range(n - 1, -1, -1):
+            if key[i] is None:
+                key[i] = min([key[j] - 300.0 for j in sp[i] if key[j] is not None] + [1e9])
+        st, _ = pack(topo_order(key, False), False, 0)
+        return sorted(range(n), key=lambda i: (st[i], i))
+
+    seq = sweeps(pattern() if CFG["pattern"] else best[1], CFG["sweeps"][0], CFG["temp"])
+    seq = sweeps(seq, CFG["sweeps"][1], CFG["temp"], 1)
+    if CFG["sweeps"][1]:
+        heads(seq, [[0.0] * nq for _ in ms_])
+        st, twin = st_[0], {o["tag"]: i for i, o in enumerate(ops)}
+        mark = [st[twin[t, "row", 0, 0, 0]] for t in range(TV)]
+        period = st[twin[2, "chain", 0, 0, 0]] - st[twin[1, "chain", 0, 0, 0]]
+        key = []
+        for i, o in enumerate(ops):
+            t = o["tag"][0]
+            j = twin.get((1,) + o["tag"][1:])
+            if t < 0:
+                key.append(st[i] - 1e6)
+            elif j is not None:
+                key.append(st[j] + (t - 1) * period)
+            else:
+                near = [a for a in ap[i] if ops[a]["tag"][0] == t]
+                key.append(max([key[a] for a in near]) + 1.0 if near else st[i] + mark[1] + (t - 1) * period - mark[t])
+        st, _ = pack(topo_order(key, False), False, 0)
+        seq = sorted(range(n), key=lambda i: (st[i], i))
+    for part in (range(n - CFG["ends"], n), range(CFG["ends"])):
+        seq = sweeps(seq, CFG["sweeps"][3], CFG["temp"], part)
+    seq = sweeps(seq, CFG["sweeps"][2], CFG["temp"] / 4)
+    ORDER["len"] = length(seq)
+    return seq
 
 
 def rank_program(g, core, T, topo):

import numpy as np
from concourse.mybir import AluOpType, AxisListType, ActivationFunctionType

ALU, ACT = AluOpType, ActivationFunctionType
W, F, K, TV, NR = 4096, 2048, 4, 3, 4
NCH, CW = 2, 8
CL = 16 * CW
NENG = 8
KM = 65536.0
CEN = 1928.0 * 4096
JO = 3072
RAMP = 16384
BIG = 1073741824.0
MAGIC = 25769803776.0
ODD = 12582913.0
KW = 17
PIECES = {None: (("s", 2), ("s", 2), ("s", 2), ("s", 2)), (0, 0): (("s", 2), ("v", 2), ("s", 2), ("s", 2)), (1, 3): (("s", 4), ("s", 2), ("s", 2))}
ABS = [(1, 3, 1)]
C_CALLS = (8,)
NB = 5
TSPLIT = (16,) * 12 + (8, 8, 8, 8)
SUMS = ((0, 16), (0, 8, 16))
XL_CALLS = (("v", 1), ("v", 1), ("v", 1), ("v", 1), ("s", 4))
Y0_ENG = "s"
Y_SCAN = ""
AHEAD = 1
ONE_CAST = False
SINGLE_Q = 0
KEY_V = 3
Q_FIRST = 128
V_FIRST = {None: 1}
Q_ENG = "v"
Y_AFTER = (None, (1, 2), (1, 2))
L16_G = True
CYC = 0.83 * np.array([1.0, 1.25, 1.4, 1.25, 1.1])
CG = np.array([1.56, 1.56, 1.3, 1.9, 1.9])
CS = np.array([3.8, 3.8, 3.8, 3.8, 3.8])
PE = 0.5 * CYC
SFX = np.array([280.0, 280.0, 280.0, 280.0, 280.0])
FIX = np.array([4.0, 4.0, 4.0, 4.0, 4.0])
LAT = np.array([205.0, 155.0, 170.0, 220.0, 200.0])
REM = np.array([3900.0, 2000.0, 4500.0, 3900.0, 2600.0])
ISS = np.array([400.0, 100.0, 600.0, 300.0, 100.0])
DFX = np.array([800.0, 800.0, 1800.0, 1000.0, 1200.0])
DBW = np.array([400.0, 350.0, 180.0, 350.0, 250.0])
WGT = np.array([1.0, 1.0, 1.0, 1.0, 1.0])
CFG = {"rounds": 2, "jit": 30.0, "seed": 1, "swaps": 400, "sweeps": (32, 0, 0, 0), "ends": 200, "asap": ("late", "count", "ahead"), "whole": 20000, "apart": (0, 1, 6, 7), "ending": {"y": 7.5, "early": 7.6, "finish": 8.0}, "pattern": 4000, "heat": 0.0003, "span": 100, "temp": 0.00015, "models": (0, 2, 3), "eps": 0.02, "near": 600.0, "jump": (0.5, 0.9)}
ORDER = {}
PLAN = {
    ("keys", "v", "D1"): (0.08, 0.09, 0.10), ("chain", "v", "SN"): (0.19, 0.28), ("chain", "v", "so"): (0.37,), ("chain", "v", "c1"): (0.45,),
    ("chain", "g", "BR"): (0.25,), ("chain", "g", "BE"): (0.30,), ("chain", "g", "DD"): (0.35,),
    ("chain", "v", "cf"): (0.95, 0.965), ("chain", "v", "ct"): (1.04,),
    ("row", "v", "M_"): (0.80, 0.93, 1.15, 1.245, 1.33, 1.41, 1.54, 1.605, 1.67, 1.77, 1.70, 1.735),
    ("row", "s", "V_"): (0.60, 0.82, 1.04, 1.26), ("row", "v", "V_"): (0.54,), ("row", "s", "Ma"): (1.40, 1.60),
    ("row", "p", "PB"): (0.94, 1.008, 1.075, 1.14, 1.21, 1.30, 1.40, 1.50), ("row", "p", "KT"): (1.35, 1.36, 1.65, 1.797, 1.868), ("row", "v", "SK"): (2.0,),
}

SCRATCH = {}
for _n, _s, _d in (
    ("XA", [W + 16], "bfloat16"), ("XB", [W + 16], "bfloat16"), ("FA", [F + 8], "int32"),
    ("LI", [2, 4, 16], "int32"), ("exi", [16], "int32"), ("thi", [4], "int32"), ("wti", [4], "int32"),
    ("thb", [4], "bfloat16"), ("thf", [4, CW], "float32"), ("TH", [TV, 4, CW], "bfloat16"),
    ("IO", [160], "float32"), ("pci", [4], "int32"), ("col", [12], "float32"),
    ("E8", [128], "bfloat16"), ("E8i", [128], "float32"), ("NI", [128], "bfloat16"), ("NQ", [128], "bfloat16"), ("ON", [128], "bfloat16"), ("ID", [128], "bfloat16"),
    ("ZI", [144], "bfloat16"), ("ZV", [144], "bfloat16"), ("ZM", [144], "bfloat16"), ("ZW", [144], "bfloat16"),
    ("G0", [160], "float16"), ("G1", [160], "float16"),
    ("RS", [CW * KW], "float32"), ("IX", [64], "float32"), ("KC", [16, 4], "float32"), ("NB", [CW], "float32"), ("IY", [16, 2], "float32"),
    ("cnt", [4], "float32"), ("cni", [4], "int32"),
    ("XL", [1024], "bfloat16"), ("L16", [64], "uint16"), ("I2", [128], "bfloat16"),
    ("exf", [16], "float32"), ("BE", [68], "float32"), ("BR", [64], "float32"), ("MK", [64, 2], "float32"),
    ("D0", [256, 5], "float32"), ("D1", [256, 5], "float32"), ("SE", [256], "float32"),
    ("LB", [64], "float32"), ("DD", [16, 4], "bfloat16"), ("PP", [64], "float32"), ("JJ", [64], "float32"),
    ("K3", [16, 4], "float32"), ("w0", [64], "float32"), ("w1", [16, 4], "float32"), ("w2", [16, 4], "float32"),
    ("w3", [64], "int32"), ("w4", [64], "int32"), ("w5", [16, 4], "float32"), ("w6", [2, 16], "float32"), ("w7", [16, 4], "float32"),
    ("w8", [2, 16], "float32"), ("ex32", [16], "float32"), ("a0", [16], "float32"), ("a1", [16], "float32"), ("a2", [16], "int32"), ("a3", [16], "int32"),
    ("se0", [16], "float32"), ("se1", [16], "float32"), ("le1", [16], "float32"), ("le2", [16], "float32"),
    ("st0", [2, 16, 4], "float32"), ("st1", [2, 16, 4], "float32"), ("st2", [2, 16, 4], "float32"),
    ("snd0", [2, 16, 4], "float32"), ("snd1", [2, 16, 4], "float32"), ("snd2", [2, 16, 4], "float32"),
    ("lt1", [2, 16], "float32"), ("lt2", [2, 16], "float32"), ("lt3", [2, 16], "float32"),
    ("sl0", [2, 16], "float32"), ("sl1", [2, 16], "float32"), ("sl2", [2, 16], "float32"),
    ("OUT", [2, 3, 16], "float32"), ("FIN", [2, 3, 16], "float32"),
    ("ya", [256], "bfloat16"), ("yb", [256], "bfloat16"), ("y16", [64], "uint16"), ("p16", [16], "uint16"),
    ("yg", [768], "bfloat16"), ("ys", [768], "bfloat16"), ("yz", [768], "bfloat16"), ("pk", [16], "int32"), ("pf", [16], "float32"),
):
    SCRATCH[_n] = ("sbuf", [128] + _s, _d)
for _c in range(NCH):
    for _n, _s, _d in (
        ("V", [16 * CL], "bfloat16"), ("M", [CL, 18], "bfloat16"), ("Ma", [CL, 17], "bfloat16"), ("c16", [CL], "uint16"), ("cf", [4, 2, 16], "float16"),
        ("ct", [4, 2, 17], "float16"), ("SK", [CW * KW], "float32"), ("SN", [2 * CL], "float32"), ("so", [2 * CW], "uint16"),
    ):
        SCRATCH["%s_%d" % (_n, _c)] = ("sbuf", [128] + _s, _d)
    SCRATCH["KT_%d" % _c] = ("psum", [128, 512], "float32")
for _p in range(NB):
    SCRATCH["PB_%d" % _p] = ("psum", [128, 32, 8, 2], "float32")
SCRATCH["MS"] = ("psum", [128, 512], "float32")

SEMAPHORES = ["sv", "ss", "sp", "sg", "sent"] + ["d%d" % _i for _i in range(32)]
ESEM = {"v": "sv", "s": "ss", "p": "sp", "g": "sg"}
ALL = slice(None)


def sl(a, b, c=None):
    return slice(a, b, c)


def build_ops(g, core, T, topo):
    rank = T.rank_of(core)
    ops = []
    V, S = g.vector, g.scalar
    tag = [(-1, "setup"), 0]

    def do(fn, name, t, *a):
        tag[0], tag[1] = (t, name) + a, 0
        fn(t, *a)

    def P(name, *idx, p=ALL):
        shape = SCRATCH[name][1][1:]
        bits = np.zeros(int(np.prod(shape)), np.uint8)
        bits[np.arange(len(bits)).reshape(shape)[idx].reshape(-1)] = 1
        return (T[name][(p,) + idx], [(name, int.from_bytes(np.packbits(bits).tobytes(), "big"))], int(bits.sum()))

    def ind(win, off):
        return (win[0].indirect(off[0]), win[1], 16 * off[2], off[1])

    def ap(a):
        return a[0] if isinstance(a, tuple) else a

    def op(eng, fn, out, ins, cost, dma=None, grp=None, inc=16, big=False):
        r, w = [], []
        for a in ins:
            if isinstance(a, tuple):
                r += a[1] + (a[3] if len(a) > 3 else [])
        for a in out:
            if isinstance(a, tuple):
                w += a[1]
                r += a[3] if len(a) > 3 else []
        x = sorted({n for n, _ in r + w if SCRATCH[n][0] == "psum"})
        if eng == "v" and not [1 for a in list(out) + list(ins) if isinstance(a, tuple) and len(a) > 3]:
            cost = cost + FIX
        tag[1] += 1
        ops.append({"tag": tag[0] + (tag[1] - 1,), "big": big, "e": eng, "fn": fn, "r": r, "w": w, "x": x, "c": cost + 0 * CG, "dma": dma is not None,
                    "l": (0.0 if dma is None else dma) + 0 * CG, "grp": grp, "inc": inc})

    def narrow(*a):
        return all(SCRATCH[x[1][0][0]][2] in ("bfloat16", "float16", "uint16") for x in a)

    def vc(out, *ins):
        if len(out) > 3:
            return 55 + out[2] * CS * CYC
        if ins and len(ins[0]) > 3:
            return 55 + out[2] * CG * CYC
        return max(64, out[2] * (0.5 if narrow(out, *ins) else 1)) * CYC

    def ts(out, in0, s1, s2, o0, o1=None):
        if o1 is None:
            op("v", lambda: V.tensor_scalar(out[0], in0[0], ap(s1), None, o0), [out], [in0, s1], vc(out, in0))
        else:
            op("v", lambda: V.tensor_scalar(out[0], in0[0], ap(s1), ap(s2), o0, o1), [out], [in0, s1, s2], vc(out, in0))

    def lin(eng, out, in0, a, b):
        if eng == "v":
            ts(out, in0, a, b, ALU.mult, ALU.add)
        else:
            op("s", lambda: S.activation(out[0], in0[0], ACT.Identity, b, ap(a)), [out], [in0, a], max(64, out[2]) * CYC + SFX)

    def gcp(out, in0):
        op("g", lambda: g.affine_select(out[0], in0[0], [[0, out[2]]], ALU.is_ge, 0.0, 0, 0), [out], [in0], 170 + 2 * out[2] * CYC)

    def tt(out, a, b, o):
        two = len(a) == 3 and SCRATCH[a[1][0][0]][0] == SCRATCH[b[1][0][0]][0]
        op("v", lambda: V.tensor_tensor(out[0], a[0], b[0], o), [out], [a, b], max(64, out[2] * (2 if two else 1)) * CYC if len(a) == 3 else vc(out, a))

    def cp(out, in_):
        op("v", lambda: V.tensor_copy(out[0], in_[0]), [out], [in_], vc(out, in_))

    def ms(out, val):
        op("v", lambda: V.memset(out[0], val), [out], [], vc(out))

    def scan(out, d0, d1, o0, o1):
        op("v", lambda: V.tensor_tensor_scan(out[0], d0[0], d1[0], 0.0, o0, o1), [out], [d0, d1], vc(out, d0, d1))

    def gather(eng, out, src, big=False):
        if eng == "v":
            op("v", lambda: V.tensor_copy(out[0], src[0]), [out], [src], vc(out, src), big=big)
        else:
            op("s", lambda: S.activation(out[0], src[0], ACT.Copy), [out], [src], vc(out, src) + 10, big=big)

    def mm(lst, grp=None):
        op("p", [(o[0], l[0], r[0]) for o, l, r in lst], [a[0] for a in lst], [a[j] for a in lst for j in (1, 2)],
           10 + sum(max(64, a[2][2]) for a in lst) * PE, grp=grp)

    def dma(eng, out, in_, nbytes, after=0.0, also=()):
        q = {"y": g.sync, "s": g.scalar}[eng]
        op(eng, lambda: q.dma_start(ap(out), ap(in_)), [out], [in_] + list(also), 60.0, dma=DFX + nbytes / DBW + after)

    def iota(out, pat, base, mult=0):
        op("g", lambda: g.iota(out[0], pat, base, mult, allow_small_or_imprecise_dtypes=True), [out], [], 130 + 2 * out[2] * CYC)

    def send(dst, out, in_, share=1.0):
        rid, pid = topo.addr(dst)[0], topo.addr(dst)[1]
        m = 0
        for e in topo.engines(core, dst)[:NENG]:
            m += 1 << e
        first = not [1 for o in ops if o["dma"] and o["e"] == "g"]
        op("g", lambda sem: g.remote_dma(out[0], in_[0], sem, T.sem.sent, pid, rid, m), [out], [in_], ISS * share, dma=REM * share + (2000.0 if first else 0.0), inc=NENG)

    def B(n, c, *idx):
        return P("%s_%d" % (n, c), *idx)

    XS = ("XA", "XB")
    dma("y", P("LI", 0), T.lc[:], 32768)
    dma("s", P("exi"), T.ex[:], 8192)
    dma("y", P("LI", 1), T.up[:], 32768)
    dma("s", P("thi", p=sl(0, 8)), T.th[:], 128)
    dma("y", P("XA", sl(0, W)), T.xs[:], 1 << 20)
    dma("s", P("wti", sl(0, 1)), T.wt[:], 512)
    dma("s", P("FA", sl(F, F + 8)), T.fa[:, 0:8], 4096)
    dma("s", P("FA", sl(0, F)), T.fa[:], 2 << 20)
    nload = len(ops)
    op("g", lambda: g.iota(T.pci[:, 0:1], [[1, 1]], 0, 1), [P("pci", sl(0, 1))], [], 150)
    iota(P("IO"), [[1, 160]], -16)
    iota(P("E8i", p=sl(0, 8)), [[1, 8], [0, 16]], 0)
    cP, cG, cH1, cH0, c16_, cW = (P("col", sl(j, j + 1)) for j in range(6))
    pc = [P("pci", sl(j, j + 1)) for j in range(4)]
    cp(cP, pc[0])
    ts(pc[1], pc[0], 4, None, ALU.arith_shift_right)
    ts(pc[2], pc[0], 4, 1, ALU.arith_shift_right, ALU.bitwise_and)
    ts(pc[3], pc[0], 15, None, ALU.bitwise_and)
    cp(cG, pc[1])
    cp(cH1, pc[2])
    ts(cH0, pc[2], -1.0, 1.0, ALU.mult, ALU.add)
    ts(c16_, pc[3], 16.0, None, ALU.mult)
    ts(cW, P("wti", sl(0, 1)), 1.0 / 16, None, ALU.mult)
    ts(P("ID"), P("IO", sl(16, 144)), cP, None, ALU.is_equal)
    for n, a in (("NQ", -1.0), ("I2", 2.0), ("NI", KM)):
        lin("s", P(n), P("ID"), a, 0.0)
    iota(P("ON"), [[0, 128]], 1)
    ms(P("ZI"), 0.0)
    ts(P("ZI", sl(15, 128, 16)), P("IO", sl(16, 24)), cG, None, ALU.is_equal)
    lin("s", P("ZV"), P("ZI"), KM, 0.0)
    lin("s", P("ZM"), P("ZI"), -KM, 0.0)
    lin("s", P("ZW"), P("ZI"), cW, 0.0)
    ts(P("G0"), P("IO"), cP, cH0, ALU.is_equal, ALU.mult)
    ts(P("G1"), P("IO"), cP, cH1, ALU.is_equal, ALU.mult)
    iota(P("RS"), [[0, CW * KW]], -W)
    for j in range(2):
        ms(P("RS", sl(j, None, KW)), BIG)
    for X in XS:
        ms(P(X, sl(W, W + 16)), 0.0)
        ms(P(X, sl(W + 1, W + 2)), 31.0)
    for k in range(K):
        cp(P("st0", ALL, ALL, k), P("LI", ALL, k))
    ts(P("st0", 1), P("st0", 1), float(JO), None, ALU.add)
    ts(P("E8", p=sl(0, 8)), P("E8i", p=sl(0, 8)), P("col", sl(0, 1), p=sl(0, 8)), None, ALU.is_equal)
    ts(P("thb", p=sl(0, 8)), P("thi", p=sl(0, 8)), -1.0, None, ALU.add)
    mm([(P("MS", sl(0, 4)), P("E8", p=sl(0, 8)), P("thb", p=sl(0, 8)))])
    for k in range(K):
        ts(P("thf", k), P("IO", sl(0, CW)), 0.0, P("MS", sl(k, k + 1)), ALU.mult, ALU.add)
    ts(P("TH", 0), P("thf"), 240.0, None, ALU.min)
    ts(P("exf"), P("exi"), -1024.0, None, ALU.add)
    lin("v", P("ex32"), P("exi"), 32.0, -65536.0)
    iota(P("BE"), [[0, 68]], 0)
    for t in range(TV - 1):
        iota(P("snd%d" % t, 0, ALL, 3), [[0, 16]], 0)
    iota(P("BR"), [[0, 16], [RAMP, 4]], 0)
    for n in ("BE", "BR"):
        gcp(P(n, sl(0, 64, 4)), P("exf"))
    iota(P("KC"), [[0, 16], [32, 4]], 65536 - 4194304)
    iota(P("IX"), [[0, 16], [1, 4]], JO - 1)
    iota(P("IY"), [[0, 16], [1, 2]], JO + 1)
    ts(P("NB"), P("IO", sl(16, 16 + CW)), -16.0, -7.5 / 16, ALU.mult, ALU.add)
    def step(s, c=None):
        return sl(s, 2 * CL, 16) if c is None else sl(CL * c + s, CL * c + CL, 16)

    ms(P("D0", sl(0, CL)), 1.0)
    lin("s", P("D1", sl(0, CL)), P("D0", sl(0, CL)), 0.0, 0.0)
    ms(P("D0", sl(CL, 2 * CL)), 1.0)
    iota(P("D1", sl(CL, 2 * CL)), [[0, 640]], 0)
    for s, val in ((0, 0.0), (1, 2.0 ** -25), (4, -8192.0), (8, -1.0)):
        ms(P("D0", step(s)), val)
    ms(P("D0", step(12), 0), 0.0)
    for s, val in ((1, 0.5 - 2.0 ** -14), (2, ODD), (3, -ODD), (5, CEN - 4095.5), (6, 2 * MAGIC), (7, -2 * MAGIC), (14, MAGIC), (15, -MAGIC)):
        ms(P("D1", step(s)), val)
    iota(P("D1", step(9)), [[0, 16], [RAMP, 5]], int(CEN) - 3072)
    iota(P("D1", step(10)), [[0, 16], [-RAMP, 5]], 0)
    for k in range(2):
        gcp(P("D1", step(12), k), P("exf"))
    ts(P("D1", step(11), 1), P("exi"), -1.0, 1024.0, ALU.mult, ALU.add)
    for c in range(NCH):
        iota(B("Ma", c, ALL, 0), [[0, CL]], 0)
        ts(B("ct", c, ALL, ALL, 0), P("IO", sl(0, CW)), 0.0, None, ALU.mult)

    if Y_SCAN:
        iota(P("yz"), [[0, 768]], 1)
        iota(P("yz", sl(0, 768, 3)), [[0, 256]], 0)
    nbank, keyed, held = [0], {}, []

    def cols(c):
        return sl(CW * c, CW * c + CW)

    def product(t, rows, L):
        lin("v", P("D0", step(13), rows), L, 1.0 / 32, 37.0)
        lin("v", P("D1", step(13), rows), L, 33.0, float(77 * t + 37 * 1024 - 80 * F - 1024))

    def code0(t):
        return P("le%d" % t) if t and AHEAD else P("st%d" % t, 0, ALL, 0)

    def ahead(t):
        L0 = code0(t)
        tt(P("a1"), P("ex32"), P("D0", step(13), 0), ALU.mult)
        tt(P("a2"), P("a1"), P("K3", ALL, 0), ALU.add)
        ts(P("a3"), P("a2"), 5, W - 1, ALU.arith_shift_right, ALU.bitwise_and)
        tt(P("a0"), P("a3"), L0, ALU.subtract)
        tt(P("a1"), P("DD", ALL, 0), P("a0"), ALU.mult)
        tt(P("se%d" % t), P("a1"), L0, ALU.add)
        send(T.cores[(rank + 1) % NR], P("le%d" % (t + 1)), P("se%d" % t))

    def prep(t):
        st = "st%d" % t
        if not AHEAD:
            product(t, sl(0, 2), P(st, 0, ALL, sl(0, 2)))
        for k, L in enumerate((code0(t), P(st, 0, ALL, 1))):
            if AHEAD:
                product(t, k, L)
            (gcp if L16_G else cp)(P("L16", sl(16 * k, 16 * k + 16)), L)
        ts(P("D0", step(12), 1), P(st, 1, ALL, 1), float(JO), None, ALU.is_equal)
        product(t, sl(2, 4), P(st, 0, ALL, sl(2, 4)))
        tt(P("D0", step(11), sl(2, 4)), P(st, 1, ALL, sl(2, 4)), P("IY"), ALU.is_equal)
        lin("v", P("D1", step(11), sl(2, 4)), P(st, 1, ALL, sl(2, 4)), -float(RAMP), float(RAMP * (JO - 1)))
        for s in range(4):
            ts(P("MK", sl(s, 64, 4)), P(st, 1, ALL, sl(2, 4)), float(JO - 1 + s), BIG, ALU.is_equal, ALU.mult)
        for k in (2, 3):
            (gcp if L16_G else cp)(P("L16", sl(16 * k, 16 * k + 16)), P(st, 0, ALL, k))
        lo = 0
        for eng, n in XL_CALLS:
            gather(eng, P("XL", sl(CL * lo, CL * (lo + n))), ind(XW, P("L16", sl(CW * lo, CW * (lo + n)))))
            lo += n
        lin("v", P("w7"), P(st, 0), 2048.0, 0.0)
        tt(P("K3"), P("w7"), P("KC"), ALU.add)

    def chain(t, c, k):
        cl = sl(CL * c, CL * c + CL)
        scan(B("SN", c, sl(0, CL)), P("D0", cl, k), P("D1", cl, k), ALU.mult, ALU.add)
        for n, s in (("BR", 9), ("BE", 10))[k == 3:] if k else ():
            gcp(P(n, sl(32 * c + k, 32 * c + 32, 4)), B("SN", c, step(s, 0)))
        if k:
            gcp(P("DD", cols(c), k - 1), B("SN", c, step(3, 0)))
        tt(B("SN", c, step(12, 1)), B("SN", c, step(13, 0)), B("SN", c, step(15, 0)), ALU.subtract)
        ts(B("so", c), B("SN", c, step(12)), 1024.0 - 31.0 / 64, float(W + 1), ALU.add, ALU.min)
        lo = 0
        for n in C_CALLS:
            gather("v", B("c16", c, sl(16 * lo, 16 * (lo + n))), ind(P("FA"), B("so", c, sl(CW + lo, CW + lo + n))))
            lo += n
        if ONE_CAST:
            ts(B("cf", c), B("c16", c), -2048.0, None, ALU.add)
        for h in range(0 if ONE_CAST else 2):
            ts(B("cf", c, ALL, h), B("c16", c, sl(64 * h, 64 * h + 64)), -2048.0, None, ALU.add)
        ct, cf = B("ct", c, ALL, ALL, sl(1, KW)), B("cf", c)
        op("v", lambda: V.transpose(ct[0], cf[0]), [ct], [cf], vc(ct, cf))

    def ymax(t, k):
        lst = P("y16", sl(16 * k, 16 * k + 16))
        ts(lst, P("BE", sl(k + 1, 64, 4)), 1024.0, float(W), ALU.add, ALU.min)
        ops[-1]["after"] = [keyed[Y_AFTER[k]]] if Y_AFTER[k] else []
        if Y_SCAN:
            gather(Y_SCAN[k], P("yg", sl(k, 768, 3)), ind(XW, lst))
            if k == 2:
                scan(P("ys"), P("yz"), P("yg"), ALU.mult, ALU.max)
        elif k == 0:
            gather(Y0_ENG, P("ya"), ind(XW, lst))
        else:
            tt(P("ya" if k == 2 else "yb"), ind(XW, lst), P("yb" if k == 2 else "ya"), ALU.max)

    def row(t, c, k):
        grp = "k%d_%d_%d" % (t, c, k)
        tt(B("M", c, ALL, 0), ind(XW, B("so", c, sl(0, CW))), P("XL", sl(CL * (2 * k + c), CL * (2 * k + c + 1))), ALU.max)
        for i in held[:]:
            ops[i]["after"] = [len(ops) - 1]
            held.remove(i)
        (gcp if Q_ENG == "g" else cp)(B("M", c, ALL, 1), B("M", c, ALL, 0))
        lo, ends = 0, []
        for eng, n in PIECES.get((t, c, k), PIECES.get((c, k), PIECES[None])):
            gather(eng, B("V", c, sl(256 * lo, 256 * (lo + n))), ind(XW, B("c16", c, sl(16 * lo, 16 * (lo + n)))), big=eng == "s")
            lo += n
            ends.append(lo)
        if ONE_CAST:
            for a in range(4):
                mm([(B("KT", c, sl(KW * (2 * a + h), KW * (2 * a + h + 1))), P("G%d" % h, sl(16 - 16 * (gp - h), 144 - 16 * (gp - h))), B("ct", c, a, gp))
                    for h in range(2) for gp in range(2)], grp)
        else:
            mm([(B("KT", c, sl(68 * h, 68 * h + 68)), P("G%d" % h, sl(16 - 16 * (gp - h), 144 - 16 * (gp - h))), B("ct", c, ALL, gp)) for h in range(2) for gp in range(2)], grp)
        mm([(B("KT", c, sl(0, CW * KW, KW)), P("NI"), P("TH", t, k))], grp)
        for h in range(2):
            ab = (c, k, h) in ABS
            for j in (2 * h, 2 * h + 1):
                bn = "PB_%d" % (nbank[0] % NB)
                nbank[0] += 1
                qs = [(P(bn, ALL, a), P("NQ" if ab else "I2"), B("M", c, sl(32 * j, 32 * j + 32), sl(0, 2))) for a in range(8)]
                if j < SINGLE_Q:
                    qs = [(P(bn, ALL, a // 2, a % 2), P("NQ" if ab else "I2"), B("M", c, sl(32 * j, 32 * j + 32), 0)) for a in range(16)]
                late = j < V_FIRST.get((c, k), V_FIRST[None])
                if not late:
                    mm(qs, grp + bn)
                for lo, hi in ((0, 16), (16, 32)) if 2 * j + 1 in ends and not ab and not late else ((0, 32),):
                    mm([(P(bn, sl(lo, hi)), P("ID" if ab else "NQ"), B("V", c, sl(512 * j + 16 * lo, 512 * j + 16 * hi)))], grp + bn)
                    if late:
                        mm(qs, grp + bn)
                    if ab:
                        bank, out = P(bn), B("Ma", c, sl(32 * j, 32 * j + 32), sl(1, KW))
                        op("s", lambda out=out, bank=bank: S.activation(out[0], bank[0], ACT.Abs), [out], [bank], 512 * CYC + SFX)
                        continue
                    a = 32 * j + lo
                    while a < 32 * j + hi:
                        e = min(a + TSPLIT[a // 8], 32 * j + hi)
                        tt(B("M", c, sl(a, e), sl(2, 18)), B("V", c, sl(16 * a, 16 * e)), P(bn, sl(a - 32 * j, e - 32 * j)), ALU.min)
                        if a >= Q_FIRST and (c, k) != (1, K - 1):
                            held.append(len(ops) - 1)
                        a = e
            for i0, i1 in zip(SUMS[h], SUMS[h][1:]):
                mm([(B("KT", c, sl(68 * h, 68 * h + 68)), P("ZV" if ab else "ZM", sl(15 - i, 143 - i)),
                     B("Ma", c, sl(64 * h + i, 64 * h + 64, 16)) if ab else B("M", c, sl(64 * h + i, 64 * h + 64, 16), sl(1, 18))) for i in range(i0, i1)], grp)
        scan(B("SK", c), P("RS"), B("KT", c, sl(0, CW * KW)), ALU.add, ALU.min)
        keyed[c, k] = len(ops) - 1

    def file_keys(t, c, k):
        for j, s in enumerate((0, 4, 8)):
            if k < K and j >= KEY_V:
                gcp(P("D1", step(s, c), k), P("D1", step(0, c), k))
            else:
                tt(P("D1", step(s, c), k), B("SK", c, sl(KW - 1, None, KW)), B("SK", c, sl(0, None, KW)), ALU.subtract)

    def pick(t, k):
        scan(P("D1", sl(0, 2 * CL, 4), k), P("MK", ALL, k - 2), P("BR"), ALU.add, ALU.min)

    def finish(t, c):
        cl = sl(CL * c, CL * c + CL)
        file_keys(t, c, K)
        scan(P("SE", cl), P("D0", cl, K), P("D1", cl, K), ALU.mult, ALU.add)
        lst = P("y16", sl(48 + CW * c, 48 + CW * c + CW))
        ts(lst, P("SE", step(10, c)), 1024.0, float(W), ALU.add, ALU.min)
        tt(P("yb", cl), ind(XW, lst), P("ys", sl(3 * CL * c + 2, 3 * CL * c + 3 * CL, 3)) if Y_SCAN else P("ya", cl), ALU.max)
        so = P("MS", sl(128 + CW * c, 128 + CW * c + CW))
        mm([(so, P("ZW", sl(15 - i, 143 - i)), P("yb", sl(CL * c + i, CL * c + CL, 16))) for i in range(16)], "s%d_%d" % (t, c))
        tt(P("pk", cols(c)), so, P("NB"), ALU.add)
        tt(P("pf", cols(c)), so, P("pk", cols(c)), ALU.subtract)
        ts(P("p16", cols(c)), P("pf", cols(c)), 16.0, c16_, ALU.mult, ALU.add)
        win = P(XS[(t + 1) % 2], sl(2048 * c, 2048 * c + 2048))
        cp(ind(win, P("p16", cols(c))), P("yb", cl))
        if t == TV - 1:
            dma("y", T.yx[:, 2048 * c:2048 * c + 2048], win, 1 << 19, 0.0 if c else 3500.0)

    def rewire_early(t):
        st, sb, r3 = "st%d" % t, "snd%d" % t, sl(0, 3)
        BE = P("BE", sl(0, 64))
        ts(P("LB"), BE, float(JO), 8192.0, ALU.is_lt, ALU.mult)
        scan(P("PP"), P("LB"), BE, ALU.add, ALU.min)
        scan(P("JJ"), P("LB"), P("IX"), ALU.add, ALU.min)
        lin("v", P("w0"), P("PP"), 32.0, -32768.0)
        tt(P("w2"), P("w0"), P("D0", step(13), sl(0, K)), ALU.mult)
        tt(P("w3"), P("w2"), P("K3"), ALU.add)
        ts(P("w4"), P("w3"), 5, W - 1, ALU.arith_shift_right, ALU.bitwise_and)
        tt(P("w1"), P("w4"), P(st, 0), ALU.subtract)
        Bs = P("BE", sl(1, 65))
        tt(P("w2", ALL, r3), P("w1", ALL, r3), P("DD", ALL, r3), ALU.mult)
        tt(P(sb, 0, ALL, r3), P("w2", ALL, r3), P(st, 0, ALL, r3), ALU.add)
        tt(P("w5"), Bs, P(st, 1), ALU.max)
        tt(P(sb, 1), P("w5"), P("JJ"), ALU.min)
        if t < TV - 1:
            send(T.cores[(rank + 1) % NR], P("st%d" % (t + 1)), P(sb))
        else:
            ts(P(sb, 1, ALL, r3), P(sb, 1, ALL, r3), -float(JO), None, ALU.add)
            for k in range(3):
                gcp(P("OUT", ALL, k), P(sb, ALL, ALL, k))
            send(T.cores[(rank - t) % NR], P("FIN"), P("OUT"))
            dma("y", T.yl[:, 0:48], P("FIN", 0), 24576)
            dma("s", T.yi[:, 0:48], P("FIN", 1), 24576)
            tt(P("w6", 0), P("JJ", sl(3, 64, 4)), P(st, 1, ALL, 3), ALU.subtract)
            ts(P("w6", 1), P(st, 1, ALL, 3), -float(JO), None, ALU.add)

    def rewire_late(t, c):
        st, sb, dead, cs = "st%d" % t, "sl%d" % t, P("SE", step(3, c)), ALL if c is None else cols(c)
        tt(P("w8", 0, cs), dead, P("w1", cs, 3), ALU.mult)
        tt(P(sb, 0, cs), P("w8", 0, cs), P(st, 0, cs, 3), ALU.add)
        if t < TV - 1:
            tt(P("w8", 1), P("SE", step(10)), P(st, 1, ALL, 3), ALU.max)
            tt(P(sb, 1), P("w8", 1), P("JJ", sl(3, 64, 4)), ALU.min)
        else:
            tt(P("w8", 1, cs), dead, P("w6", 0, cs), ALU.mult)
            tt(P(sb, 1, cs), P("w8", 1, cs), P("w6", 1, cs), ALU.add)

    def count(t):
        send(T.cores[(rank + 1) % NR], P("lt%d" % (t + 1)), P("sl%d" % t))
        gcp(P("DD", ALL, 3), P("SE", step(3)))
        mm([(P("MS", sl(0, 64)), P("ON"), P("DD"))])
        c0, c1, ci, msum = P("cnt", sl(0, 1)), P("cnt", sl(1, 2)), P("cni", sl(0, 1)), P("MS", sl(0, 64))
        op("v", lambda: V.tensor_reduce(c0[0], msum[0], AxisListType.X, ALU.add), [c0], [msum], 64 * CYC)
        ts(ci, c0, 1.0 / 32, -31.0 / 64, ALU.mult, ALU.add)
        ts(c1, ci, -32.0, c0, ALU.mult, ALU.add)
        ts(P("TH", t + 1), P("thf"), c1, 240.0, ALU.add, ALU.min)

    def patch(t):
        gcp(P("st%d" % t, ALL, ALL, 3), P("lt%d" % t))
        iota(P("BR", sl(2, 64, 4)), [[0, 16]], 2 * RAMP)

    for t in range(TV):
        XW = P(XS[t % 2])
        if t:
            do(patch, "patch", t)
        do(prep, "prep", t)
        dma("y", P(XS[(t + 1) % 2], sl(0, W)), P(XS[t % 2], sl(0, W)), 1 << 20, also=[P("lt%d" % t) if t else P("FA")])
        for k in range(K):
            if k >= 2:
                do(pick, "pick", t, k)
            for c in range(NCH):
                if k:
                    do(file_keys, "keys", t, c, k)
                do(chain, "chain", t, c, k)
            for j in range(3 if k == K - 1 else 0):
                do(ymax, "y", t, j)
            if k == AHEAD and t < TV - 1:
                do(ahead, "ahead", t)
            if k == K - 1:
                do(rewire_early, "early", t)
            for c in range(NCH):
                do(row, "row", t, c, k)
                if k == K - 1:
                    do(finish, "finish", t, c)
                    if t == TV - 1:
                        do(rewire_late, "late", t, c)
        if t < TV - 1:
            do(rewire_late, "late", t, None)
            do(count, "count", t)
    send(T.cores[(rank - (TV - 1)) % NR], P("lt3"), P("sl2"), 0.6)
    dma("y", T.yl[:, 48:64], P("lt3", 0), 8192)
    dma("s", T.yi[:, 48:64], P("lt3", 1), 8192)
    return ops, nload


def depend(ops):
    hist, epoch = {}, {}
    for i, o in enumerate(ops):
        d = set(o.get("after", ()))
        for n, m in o["r"]:
            d.update(e[0] for e in hist.get(n, ()) if e[2] and e[1] & m)
        for n, m in o["w"]:
            d.update(e[0] for e in hist.get(n, ()) if e[1] & m)
        for k in o["x"]:
            e = epoch.setdefault(k, [o["e"], [], []])
            if e[0] != o["e"]:
                e[0], e[2], e[1] = o["e"], e[1], []
            d.update(e[2])
            e[1].append(i)
        for n, m in o["w"]:
            hist[n] = [[e[0], e[1] & ~m, e[2]] for e in hist.get(n, ()) if e[1] & ~m]
        for n, m in o["r"]:
            hist.setdefault(n, []).append([i, m, False])
        for n, m in o["w"]:
            hist.setdefault(n, []).append([i, m, True])
        d.discard(i)
        o["d"] = sorted(d)


def schedule(ops, nload):
    n = len(ops)
    eng = [o["e"] for o in ops]
    pred = [[(j, 0 if eng[j] == o["e"] == "p" else 1) for j in o["d"]] for o in ops]
    lastq = {}
    for i in range(nload):
        if eng[i] in lastq:
            pred[i].append((lastq[eng[i]], 2))
        lastq[eng[i]] = i
    succ = [[] for _ in ops]
    for i in range(n):
        for j, kind in pred[i]:
            succ[j].append((i, kind))
    rs = [CFG["seed"]]

    def rnd():
        rs[0] = (rs[0] * 1103515245 + 12345) % 2147483648
        return rs[0] / 2147483648.0

    def pack(seq, back, m):
        dur = [float(o["c"][m]) for o in ops]
        lag = [float(o["l"][m]) for o in ops]
        lat = float(LAT[m])
        st = [0.0] * n
        busy = {}
        for i in seq:
            t = lag[i] if back else 0.0
            for j, kind in (succ[i] if back else pred[i]):
                gap = 0.0 if kind != 1 else lat + lag[i if back else j]
                if st[j] + dur[j] + gap > t:
                    t = st[j] + dur[j] + gap
            b = busy.setdefault(eng[i], [])
            lo, hi = 0, len(b)
            while lo < hi:
                mid = (lo + hi) // 2
                if b[mid][1] <= t:
                    lo = mid + 1
                else:
                    hi = mid
            while lo < len(b) and b[lo][0] < t + dur[i]:
                t = max(t, b[lo][1])
                lo += 1
            b.insert(lo, (t, t + dur[i]))
            st[i] = t
        return st, dur

    def topo_order(key, back):
        nb, left = (pred if back else succ), [len(succ[i] if back else pred[i]) for i in range(n)]
        rank_ = sorted(range(n), key=lambda i: key[i])
        seq, waiting = [], {}
        for i in rank_:
            stack = [i] if left[i] == 0 else []
            if left[i]:
                waiting[i] = True
            while stack:
                a = stack.pop()
                seq.append(a)
                new = []
                for j, _ in nb[a]:
                    left[j] -= 1
                    if left[j] == 0 and j in waiting:
                        new.append(j)
                stack.extend(sorted(new, key=lambda j: -key[j]))
        return seq

    def length(seq):
        fin, free = [None] * n, {}
        for i in seq:
            t = free.get(eng[i], 0 * CG)
            for j, kind in pred[i]:
                if kind == 1:
                    t = np.maximum(t, fin[j] + LAT)
            free[eng[i]] = t + ops[i]["c"]
            fin[i] = free[eng[i]] + ops[i]["l"]
        return np.max(np.array(fin), axis=0)

    pr, nxt = [0.0] * n, 0.0
    for i in range(n - 1, -1, -1):
        pr[i] = float(ops[i]["c"][0] + ops[i]["l"][0]) + max([60.0 + pr[j] for j, _ in succ[i]] + [0.0])
        if ops[i]["big"]:
            pr[i] = nxt = max(pr[i], float(ops[i]["c"][0]) * 1.3 + nxt)
    key = [-a for a in pr]
    best, base = None, None
    for r in range(CFG["rounds"]):
        m = 0 if r % 2 == 0 else int(rnd() * len(CG))
        st, dur = pack(topo_order(key, False), False, m)
        seq = sorted(range(n), key=lambda i: (st[i], i))
        ln = length(seq)
        if base is None:
            base = ln
        val = float(np.sum(WGT * ln / base))
        if best is None or val < best[0]:
            best = (val, seq, st, dur, ln)
        elif r % 2 == 1:
            st, dur = best[2], best[3]
        bs, dur = pack(topo_order([-(st[i] + dur[i]) + CFG["jit"] * rnd() for i in range(n)], True), True, m)
        key = [-(bs[i] + dur[i]) for i in range(n)]
    ms_ = CFG["models"]
    qn = {e: a for a, e in enumerate(sorted(set(eng)))}
    q = [qn[e] for e in eng]
    dur = [[float(o["c"][m]) for o in ops] for m in ms_]
    lag = [[float(o["l"][m] + LAT[m]) for o in ops] for m in ms_]
    wp = [[j for j, kind in pred[i] if kind == 1] for i in range(n)]
    ap = [[j for j, kind in pred[i]] for i in range(n)]
    sp = [[j for j, kind in succ[i]] for i in range(n)]

    ws = [[j for j, kind in succ[i] if kind == 1] for i in range(n)]
    nm, nq = len(ms_), len(qn)
    wgt = [float(WGT[m] / base[m]) for m in ms_]
    st_, fin_, tail = ([[0.0] * n for _ in ms_] for _ in range(3))

    def heads(part, free0):
        out = []
        for a in range(nm):
            d, l, st, fin, free = dur[a], lag[a], st_[a], fin_[a], free0[a][:]
            for i in part:
                t = free[q[i]]
                for j in wp[i]:
                    if fin[j] > t:
                        t = fin[j]
                st[i] = t
                t += d[i]
                free[q[i]] = t
                fin[i] = t + l[i]
            out.append(free)
        return out

    def tails(seq):
        for a in range(nm):
            d, l, tl, nx = dur[a], lag[a], tail[a], [0.0] * nq
            for i in seq[::-1]:
                t = max(nx[q[i]], l[i] + max([tl[j] for j in ws[i]] + [0.0]))
                tl[i] = nx[q[i]] = t + d[i]

    def move(seq, pos, a, b, early):
        lo, hi = pos[a], pos[b]
        take, stack = {b if early else a}, [b if early else a]
        while stack:
            for j in (ap if early else sp)[stack.pop()]:
                if lo <= pos.get(j, -1) <= hi and j not in take:
                    if j == a or j == b:
                        return None
                    take.add(j)
                    stack.append(j)
        x = [i for i in seq[lo:hi + 1] if i in take]
        y = [i for i in seq[lo:hi + 1] if i not in take]
        return seq[:lo] + (x + y if early else y + x) + seq[hi + 1:]

    def improve(part, rest, free0, tries, temp):
        inside = set(part)
        edge = [i for i in part if not ws[i] or [j for j in ws[i] if j not in inside]]
        out = [[max([tail[a][j] for j in ws[i] if j not in inside] + [0.0]) for i in edge] for a in range(nm)]
        nextq = {}
        for i in rest[::-1]:
            nextq[q[i]] = i
        outq = [[tail[a][nextq[e]] if e in nextq else 0.0 for e in range(nq)] for a in range(nm)]

        def value(p, lo=0):
            if lo:
                for a in range(nm):
                    fin, keep = fin_[a], kept[a]
                    for i in p[dirty[0]:lo]:
                        fin[i] = keep[i]
                dirty[0] = lo
            free, tot, ends = heads(p[lo:], frees[lo] if lo else free0), 0.0, []
            for a in range(nm):
                fin = fin_[a]
                v = [fin[i] + o for i, o in zip(edge, out[a])]
                u = [f + o for f, o in zip(free[a], outq[a])]
                top = max(max(v), max(u))
                tot += wgt[a] * (top + CFG["eps"] * sum([max(x - top + CFG["near"], 0.0) for x in v + u]))
                ends.append(edge[v.index(top)] if top in v else -1 - u.index(top))
            return tot, ends

        val, ends = value(part)
        top, fresh = (val, part), True
        for r in range(tries):
            if fresh:
                pos, prev, nxt_, lastq = {}, {}, {}, {}
                kept, dirty, frees, now = [{i: fin_[a][i] for i in part} for a in range(nm)], [len(part)], [], free0
                for a, i in enumerate(part):
                    frees.append(now)
                    now = [f[:] for f in now]
                    for b in range(nm):
                        now[b][q[i]] = st_[b][i] + dur[b][i]
                    pos[i] = a
                    if q[i] in lastq:
                        prev[i] = lastq[q[i]]
                        nxt_[prev[i]] = i
                    lastq[q[i]] = i
                arcs = []
                for a in range(nm):
                    st, fin, i = st_[a], fin_[a], ends[a] if ends[a] >= 0 else lastq.get(-1 - ends[a])
                    while i in inside:
                        j = prev.get(i)
                        if j is not None and st[j] + dur[a][j] >= st[i] - 1e-6:
                            arcs.append((j, i))
                        else:
                            j = max(wp[i], key=lambda j: fin[j]) if wp[i] else None
                            if j is not None and fin[j] < st[i] - 1e-6:
                                j = None
                        i = j
                fresh = False
                if not arcs:
                    break
            a, b = arcs[int(rnd() * len(arcs))]
            early = rnd() < 0.5
            jump = CFG["jump"][int(rnd() * len(CFG["jump"]))]
            while rnd() < jump:
                if early:
                    a = prev.get(a, a)
                else:
                    b = nxt_.get(b, b)
            new = move(part, pos, a, b, early)
            if new is None:
                continue
            v2, e2 = value(new, pos[a])
            dirty[0] = pos[a]
            if v2 <= val + temp * -np.log(rnd() + 1e-12):
                heads(new, free0)
                st, at = st_[0], {i: a for a, i in enumerate(new)}
                part, val, ends, fresh = sorted(new, key=lambda i: (st[i], at[i])), v2, e2, True
                if val < top[0]:
                    top = (val, part)
        return top[1]

    def sweeps(seq, count, temp, only=None):
        span = CFG["span"]
        for r in range(count):
            tails(seq)
            at = only if isinstance(only, range) else [a for a, i in enumerate(seq) if only is None or ops[i]["tag"][0] == only]
            lo = max(at[0] - int(span * rnd() / 2), 0)
            free0 = heads(seq[:lo], [[0.0] * nq for _ in ms_])
            step = int(span * (0.3 + 0.4 * rnd()))
            while lo <= at[-1]:
                seq[lo:lo + span] = improve(seq[lo:lo + span], seq[lo + span:], free0, CFG["swaps"], temp * (1.0 - r / count))
                free0 = heads(seq[lo:lo + step], free0)
                lo, step = lo + step, span // 2
        return seq

    def pattern():
        role, turn, seen = {}, {}, {}
        for i, o in enumerate(ops):
            if o["tag"][1] in ("row", "chain", "keys"):
                r = (o["tag"][1], o["e"], o["w"][0][0][:2])
                seen[o["tag"][:4], r] = seen.get((o["tag"][:4], r), 0) + 1
                role[i], turn[i] = r + (seen[o["tag"][:4], r],), 2 * o["tag"][3] + o["tag"][2]
        core_ = [i for i in role if ops[i]["tag"][0] == 1]
        inside = set(core_)
        cp_ = {i: [j for j in ap[i] if j in inside] for i in core_}
        cw = {i: [j for j in wp[i] if j in inside] for i in core_}
        heads(best[1], [[0.0] * nq for _ in ms_])
        ref = [i for i in core_ if role[i][2] == "SK"]
        period = (st_[0][ref[5]] - st_[0][ref[1]]) / 4
        shift = {role[i]: st_[0][i] / period - turn[i] for i in sorted(core_, key=lambda i: -abs(turn[i] - 4))}
        for r, at in PLAN.items():
            shift.update({r + (j + 1,): a for j, a in enumerate(at)})
        names = list({role[i]: 0 for i in core_ if turn[i] == 4})
        names += [r for r in shift if r not in names]
        mates = {r: [s for s in names if s[1] == r[1] and s != r] for r in names}

        def value(sh):
            key = {}
            for i in core_:
                key[i] = max([turn[i] + sh[role[i]]] + [key[j] + 1e-6 for j in cp_[i] if j in key])
            order_, tot = sorted(core_, key=key.get), 0.0
            for a in range(nm):
                d, l, st, fin, free = dur[a], lag[a], st_[a], fin_[a], [0.0] * nq
                for i in order_:
                    t = free[q[i]]
                    for j in cw[i]:
                        if fin[j] > t:
                            t = fin[j]
                    st[i] = t
                    free[q[i]] = t + d[i]
                    fin[i] = t + d[i] + l[i]
                tot += wgt[a] * max(free)
            return tot

        def anneal(shift, names, tries, wide):
            val = value(shift)
            top = (val, shift)
            for r in range(tries):
                new, a = dict(shift), names[int(rnd() * len(names))]
                if rnd() < 0.5 and a in mates:
                    b = mates[a][int(rnd() * len(mates[a]))]
                    new[a] = shift[b] + round(shift[a] - shift[b]) + (0.002 if rnd() < 0.5 else -0.002) * rnd()
                else:
                    lo, by = names.index(a), (rnd() - 0.5) * wide[int(rnd() * len(wide))]
                    for b in names[lo:lo + (1 if rnd() < 0.5 else 1 + int(rnd() * 8))]:
                        new[b] = shift[b] + by
                v2 = value(new)
                if v2 <= val + CFG["heat"] * (1.0 - r / tries) * -np.log(rnd() + 1e-12):
                    shift, val = new, v2
                    if val < top[0]:
                        top = (val, shift)
            value(top[1])
            return dict(top[1])

        shift = anneal(shift, names, CFG["pattern"], (0.3,))
        ORDER["period"] = [(st_[a][ref[6]] - st_[a][ref[2]]) / 4 for a in range(nm)]
        names, end = [], {}
        for i, o in enumerate(ops):
            step_ = o["tag"][1]
            if step_ == "chain" and turn[i] < 2:
                del role[i]
            elif (step_ == "row" and turn[i] in CFG["apart"]) or step_ in CFG["ending"] or (step_ == "prep" and o["w"] and o["w"][0][0] == "XL"):
                r = (o["tag"][1:], o["e"])
                if o["tag"][0] == 1:
                    names.append(r)
                    shift[r] = turn[i] + shift[role[i]] if i in role else CFG["ending"].get(step_, 0.0) + 0.01 * o["tag"][-1]
                role[i], turn[i] = r, 0
        for i in [i for i in role if role[i] not in shift]:
            del role[i]
        core_[:] = [i for i in sorted(role) if ops[i]["tag"][0] == 1]
        inside = set(core_)
        cp_.update({i: [j for j in ap[i] if j in inside] for i in core_})
        cw.update({i: [j for j in wp[i] if j in inside] for i in core_})
        anneal(shift, names, CFG["whole"], (0.1, 0.3, 1.0))
        ORDER["core"] = sorted([(st_[0][i], dur[0][i], role[i], turn[i]) for i in core_])
        at = {ops[i]["tag"][1:]: st_[0][i] for i in core_}
        key = [at[o["tag"][1:]] + 1e6 * o["tag"][0] if i in role else None for i, o in enumerate(ops)]
        for i in range(n):
            if ops[i]["tag"][1] in CFG["asap"]:
                key[i] = max([key[j] + 100.0 for j in ap[i] if key[j] is not None] + [0.0])
        for i in range(n - 1, -1, -1):
            if key[i] is None:
                key[i] = min([key[j] - 300.0 for j in sp[i] if key[j] is not None] + [1e9])
        st, _ = pack(topo_order(key, False), False, 0)
        return sorted(range(n), key=lambda i: (st[i], i))

    seq = sweeps(pattern() if CFG["pattern"] else best[1], CFG["sweeps"][0], CFG["temp"])
    seq = sweeps(seq, CFG["sweeps"][1], CFG["temp"], 1)
    if CFG["sweeps"][1]:
        heads(seq, [[0.0] * nq for _ in ms_])
        st, twin = st_[0], {o["tag"]: i for i, o in enumerate(ops)}
        mark = [st[twin[t, "row", 0, 0, 0]] for t in range(TV)]
        period = st[twin[2, "chain", 0, 0, 0]] - st[twin[1, "chain", 0, 0, 0]]
        key = []
        for i, o in enumerate(ops):
            t = o["tag"][0]
            j = twin.get((1,) + o["tag"][1:])
            if t < 0:
                key.append(st[i] - 1e6)
            elif j is not None:
                key.append(st[j] + (t - 1) * period)
            else:
                near = [a for a in ap[i] if ops[a]["tag"][0] == t]
                key.append(max([key[a] for a in near]) + 1.0 if near else st[i] + mark[1] + (t - 1) * period - mark[t])
        st, _ = pack(topo_order(key, False), False, 0)
        seq = sorted(range(n), key=lambda i: (st[i], i))
    for part in (range(n - CFG["ends"], n), range(CFG["ends"])):
        seq = sweeps(seq, CFG["sweeps"][3], CFG["temp"], part)
    seq = sweeps(seq, CFG["sweeps"][2], CFG["temp"] / 4)
    ORDER["len"] = length(seq)
    return seq


def rank_program(g, core, T, topo):
    if T.rank_of(core) is None:
        return
    ops, nload = build_ops(g, core, T, topo)
    depend(ops)
    if "seq" not in ORDER:
        ORDER["seq"] = schedule(ops, nload)
    order = ORDER["seq"]
    Q = {"v": g.vector, "s": g.scalar, "p": g.tensor, "g": g, "y": g.sync}
    pos, nd = {}, 0
    for i in order:
        o = ops[i]
        if o["dma"]:
            o["sem"], o["at"] = "d%d" % nd, 1
            nd += 1
        else:
            pos[o["e"]] = pos.get(o["e"], 0) + 1
            o["sem"], o["at"] = ESEM[o["e"]], pos[o["e"]]
    know = {e: {} for e in Q}
    need = set()
    for i in order:
        o = ops[i]
        kn = know[o["e"]]
        want = {}
        for j in sorted(o["d"], key=lambda j: -ops[j]["at"]):
            a = ops[j]
            if a["e"] == o["e"] == "p" or kn.get(a["sem"], 0) >= a["at"]:
                continue
            want[a["sem"]] = j
            kn[a["sem"]] = a["at"]
            if not (a["dma"] and a["e"] == "g"):
                for s, v in a["kn"].items():
                    kn[s] = max(kn.get(s, 0), v)
        o["waits"] = sorted(want.values())
        o["kn"] = dict(kn)
        need.update(want.values())
    first, last = {}, {}
    for i in order:
        gp = ops[i]["grp"]
        if gp is not None:
            first.setdefault(gp, i)
            last[gp] = i
    total, nsend = {}, 0
    for i in order:
        o = ops[i]
        q = Q[o["e"]]
        for j in o["waits"]:
            q.wait_ge(T.sem[ops[j]["sem"]], ops[j]["val"])
        if o["dma"]:
            if o["e"] == "g":
                o["fn"](T.sem[o["sem"]])
                nsend += o["inc"]
            else:
                o["fn"]().then_inc(T.sem[o["sem"]], 16)
            o["val"] = total[o["sem"]] = o["inc"]
            continue
        if o["e"] == "p":
            gp, lst = o["grp"], o["fn"]
            for a, m in enumerate(lst):
                ins = q.matmul(m[0], m[1], m[2], gp is None or (first[gp] == i and a == 0), gp is None or (last[gp] == i and a == len(lst) - 1))
        else:
            ins = o["fn"]()
        if i in need:
            total[o["sem"]] = total.get(o["sem"], 0) + 1
            ins.then_inc(T.sem[o["sem"]], 1)
        o["val"] = total.get(o["sem"], 0)
    g.wait_ge(T.sem.sent, nsend)
    for s in sorted(total):
        g.wait_ge(T.sem[s], total[s])
